import numpy as np
import ml_dtypes


def mxq(x, axis, fmt="e4m3"):
    dtype, down = {"e4m3": (ml_dtypes.float8_e4m3fn, 7), "e5m2": (ml_dtypes.float8_e5m2, 14)}[fmt]
    v = np.moveaxis(np.asarray(x, np.float32).astype(ml_dtypes.bfloat16).astype(np.float64), axis, -1)
    blocks = v.reshape(v.shape[:-1] + (-1, 32))
    amax = np.abs(blocks).max(-1, keepdims=True)
    byte = np.maximum(np.where(amax > 0, np.frexp(amax)[1] - 1 + 127, 0) - down, 1)
    scale = np.exp2(byte - 127.0)
    codes = (blocks / scale).astype(np.float32).astype(dtype).astype(np.float64)
    return np.moveaxis((codes * scale).reshape(v.shape), -1, axis)


WIDE = False


def mx_kscale(k):
    if not WIDE:
        return np.ones(k)
    levels = np.array([10, -10, 5, -5, 0])
    if k % 512:
        return np.exp2(np.random.permutation(np.resize(levels, k // 32))).repeat(32)
    a = np.empty((k // 512, 16))
    for p in range(k // 512):
        a[p, :8] = np.random.permutation(np.resize(levels, 8))
        for g in range(8):
            far = levels[np.abs(levels - a[p, g]) >= 10]
            a[p, g + 8] = far[np.random.randint(len(far))]
    return np.exp2(a.ravel()).repeat(32)


def f64(x):
    return np.asarray(x).astype(np.float64)


def striped(idx):
    return np.tile(idx.reshape(-1, 16).T, (8, 1)).astype(np.uint16)


def unstriped(offs):
    return offs[:16].T.reshape(-1).astype(np.int64)


def relu(v):
    return np.maximum(v, 0.0)


K, T, E, C, N = 1024, 512, 8, 256, 128
TOP = 4


def by_expert(wq, xq):
    return np.concatenate([wq[e].T @ xq[:, e * C:(e + 1) * C] for e in range(E)], axis=1)


def setup_inputs():
    n = np.random.standard_normal
    s = mx_kscale(K)[:, None]
    deal = np.repeat(np.arange(E), C).reshape(TOP, T)[:, np.random.permutation(T)]
    deal = np.take_along_axis(deal, np.argsort(np.random.rand(TOP, T), axis=0), axis=0)
    for _ in range(8):
        s_, t_ = np.random.permutation(T).reshape(2, -1); r = np.random.randint(TOP, size=T // 2); x, y = deal[r, s_].copy(), deal[r, t_].copy()
        ok = ~((deal[:, s_] == y).any(0) | (deal[:, t_] == x).any(0)); deal[r[ok], s_[ok]] = y[ok]; deal[r[ok], t_[ok]] = x[ok]
    order = np.lexsort((np.random.rand(TOP * T), deal.reshape(-1)))
    slot_token = order % T; pos = np.empty(TOP * T, np.int64); pos[order] = np.arange(TOP * T); pos = pos.reshape(TOP, T)
    g = np.random.uniform(0.5, 1.5, (TOP, T)); g = g / g.sum(0)
    w_slot = np.empty(E * C)
    for r in range(TOP): w_slot[pos[r]] = g[r]
    return {
        "xT": (n((K, T)) * s).astype(np.float32),
        "w": (n((E, K, N)) / np.sqrt(K) / s[None]).astype(np.float32),
        "b": (0.3 * n((N, E))).astype(np.float32),
        "gate": np.tile(w_slot, (K, 1)).astype(np.float32),
        "offs": striped(slot_token),
        "pos1": striped(pos[0]),
        "pos2": striped(pos[1]),
        "pos3": striped(pos[2]),
        "pos4": striped(pos[3]),
    }


def reference(xT, w, b, gate, offs, pos1, pos2, pos3, pos4):
    idx = unstriped(offs)
    xq = mxq(f64(gate) * f64(xT)[:, idx], 0, "e4m3")
    y = by_expert(mxq(f64(w), 1, "e4m3"), xq)
    y = relu(y + np.repeat(f64(b), C, axis=1))
    return y[:, unstriped(pos1)] + y[:, unstriped(pos2)] + y[:, unstriped(pos3)] + y[:, unstriped(pos4)]

@@ -1,0 +1,176 @@
+from contextlib import ExitStack
+
+import concourse.mybir as mybir
+
+K, T, E, C, N = 1024, 512, 8, 256, 128
+TOP = 4
+S = E * C
+FLOPS = 2 * K * N * S
+BYTES = 4 * (K * T + E * K * N + N * E + 128 * S + N * T) + 2 * 128 * (S // 16 + TOP * T // 16)
+
+F32 = mybir.dt.float32
+BF16 = mybir.dt.bfloat16
+U32 = mybir.dt.uint32
+U16 = mybir.dt.uint16
+U8 = mybir.dt.uint8
+FP8X4 = mybir.dt.float8_e4m3fn_x4
+MULT = mybir.AluOpType.mult
+ADD = mybir.AluOpType.add
+RELU = mybir.ActivationFunctionType.Relu
+
+P = 128
+PACK = 4
+PASSES = K // (P * PACK)
+WINDOW = 528
+CHUNKS = [(0, 512), (512, 512), (1024, 512), (1536, 256), (1792, 256)]
+HALF = T // 2
+
+
+def tile_moe_pre_lin_relu_kernel(tc, xT, w, b, gate, offs, pos1, pos2, pos3, pos4, out):
+    nc = tc.nc
+    with ExitStack() as ctx:
+        keep = ctx.enter_context(tc.tile_pool(name="keep", bufs=1))
+        ring = ctx.enter_context(tc.tile_pool(name="ring", bufs=3))
+        psum = ctx.enter_context(tc.psum_pool(name="psum", bufs=4))
+
+        slot_token = keep.tile([P, S // 16], U16, name="slot_token")
+        token_slot = [keep.tile([P, T // 16], U16, name="token_slot%d" % r) for r in range(TOP)]
+        x_rows = [[keep.tile([P, WINDOW], F32, name="x_rows%d_%d" % (g, j)) for j in range(PACK)] for g in range(PASSES)]
+        gates = [keep.tile([P, n], F32, name="gate%d" % s0) for s0, n in CHUNKS]
+        w_raw = [keep.tile([P, PASSES, PACK, N], F32, name="w_raw%d" % e) for e in range(E)]
+        w_bf = [keep.tile([P, PASSES, N, PACK], BF16, name="w_bf%d" % e, align_bytes=64) for e in range(E)]
+        w_codes = [keep.tile([P, PASSES * N], U32, name="w_codes%d" % e, align_bytes=64) for e in range(E)]
+        w_scales = [keep.tile([P, PASSES * N], U8, name="w_scales%d" % e, align_bytes=64) for e in range(E)]
+        bias = keep.tile([P, E], F32, name="bias")
+        y = keep.tile([P, S], F32, name="y")
+
+        x_view = xT.rearrange("(g p j) t -> g j p t", g=PASSES, j=PACK)
+
+        def load_x(g, j):
+            nc.sync.dma_start(out=x_rows[g][j][:, 0:T], in_=x_view[g, j])
+
+        def load_gate(c):
+            s0, n = CHUNKS[c]
+            nc.sync.dma_start(out=gates[c][:], in_=gate[0:P, s0 : s0 + n])
+
+        def load_w(e):
+            nc.sync.dma_start(
+                out=w_raw[e][:].rearrange("p g j n -> p g (j n)"),
+                in_=w[e].rearrange("(g p j) n -> p g (j n)", g=PASSES, j=PACK),
+            )
+
+        nc.sync.dma_start(slot_token[:], offs)
+        load_gate(0)
+        for j in range(PACK):
+            load_x(0, j)
+        load_w(0)
+        for j in range(PACK):
+            load_x(1, j)
+        load_w(1)
+        load_gate(1)
+        nc.sync.dma_start(out=bias[:], in_=b)
+        for e in range(2, E):
+            load_w(e)
+            if e < len(CHUNKS):
+                load_gate(e)
+        for r, pos in enumerate((pos1, pos2, pos3, pos4)):
+            nc.sync.dma_start(token_slot[r][:], pos)
+
+        def round_w(e):
+            nc.scalar.copy(out=w_bf[e][:], in_=w_raw[e][:].rearrange("p g j n -> p g n j"))
+
+        def quantize_w(e):
+            nc.vector.quantize_mx(
+                out=w_codes[e][:].bitcast(FP8X4), scales=w_scales[e][:], in_=w_bf[e][:].rearrange("p g n j -> p (g n j)")
+            )
+
+        x_bf, x_codes, x_scales = {}, {}, {}
+
+        def gather_x(c, g):
+            s0, n = CHUNKS[c]
+            gated = ring.tile([P, PACK, n], F32, name="gated")
+            for j in range(PACK):
+                nc.vector.tensor_tensor(
+                    gated[:, j, :], x_rows[g][j][:].indirect(slot_token[:, s0 // 16 : (s0 + n) // 16]), gates[c][:], MULT
+                )
+            x_bf[c, g] = ring.tile([P, n, PACK], BF16, name="x_bf", align_bytes=64)
+            nc.scalar.copy(out=x_bf[c, g][:], in_=gated[:].rearrange("p j n -> p n j"))
+
+        def quantize_x(c, g):
+            n = CHUNKS[c][1]
+            x_codes[c, g] = keep.tile([P, n], U32, name="x_codes%d_%d" % (c, g), align_bytes=64)
+            x_scales[c, g] = keep.tile([P, n], U8, name="x_scales%d_%d" % (c, g), align_bytes=64)
+            nc.vector.quantize_mx(
+                out=x_codes[c, g][:].bitcast(FP8X4), scales=x_scales[c, g][:], in_=x_bf[c, g][:].rearrange("p n j -> p (n j)")
+            )
+
+        def expert(e):
+            c = max(i for i, (s0, n) in enumerate(CHUNKS) if s0 <= e * C)
+            cols = slice(e * C - CHUNKS[c][0], (e + 1) * C - CHUNKS[c][0])
+            acc = psum.tile([P, C], F32, name="acc")
+            for g in range(PASSES):
+                nc.tensor.matmul_mx(
+                    out=acc[:],
+                    lhsT=w_codes[e][:, g * N : (g + 1) * N].bitcast(FP8X4),
+                    lhsT_scale=w_scales[e][:, g * N : (g + 1) * N],
+                    rhs=x_codes[c, g][:, cols].bitcast(FP8X4),
+                    rhs_scale=x_scales[c, g][:, cols],
+                    start=(g == 0),
+                    stop=(g == PASSES - 1),
+                )
+            nc.scalar.activation(out=y[:, e * C : (e + 1) * C], in_=acc[:], func=RELU, bias=bias[:, e : e + 1])
+
+        round_w(0)
+        gather_x(0, 0)
+        round_w(1)
+        gather_x(0, 1)
+        quantize_x(0, 0)
+        round_w(2)
+        gather_x(1, 0)
+        quantize_x(0, 1)
+        quantize_w(0)
+        quantize_w(1)
+        round_w(3)
+        gather_x(1, 1)
+        expert(0)
+        expert(1)
+        quantize_x(1, 0)
+        round_w(4)
+        gather_x(2, 0)
+        quantize_x(1, 1)
+        quantize_w(2)
+        quantize_w(3)
+        round_w(5)
+        gather_x(2, 1)
+        expert(2)
+        expert(3)
+        quantize_x(2, 0)
+        round_w(6)
+        round_w(7)
+        gather_x(3, 0)
+        quantize_w(4)
+        quantize_w(5)
+        gather_x(3, 1)
+        quantize_x(2, 1)
+        gather_x(4, 0)
+        expert(4)
+        expert(5)
+        quantize_x(3, 0)
+        gather_x(4, 1)
+        quantize_x(3, 1)
+        quantize_w(6)
+        expert(6)
+        quantize_x(4, 0)
+        quantize_w(7)
+        quantize_x(4, 1)
+        expert(7)
+
+        picked = keep.tile([P, 2, TOP, HALF], F32, name="picked")
+        pairs = keep.tile([P, 2, 2, HALF], F32, name="pairs")
+        total = keep.tile([P, 2, HALF], F32, name="total")
+        for h in range(2):
+            for r in range(TOP):
+                nc.vector.tensor_copy(picked[:, h, r, :], y[:].indirect(token_slot[r][:, h * HALF // 16 : (h + 1) * HALF // 16]))
+            nc.vector.tensor_tensor(pairs[:, h], picked[:, h, 0:2, :], picked[:, h, 2:4, :], ADD)
+            nc.vector.tensor_tensor(total[:, h, :], pairs[:, h, 0, :], pairs[:, h, 1, :], ADD)
+            nc.sync.dma_start(out=out[:, h * HALF : (h + 1) * HALF], in_=total[:, h, :])

@@ -21,8 +21,7 @@ RELU = mybir.ActivationFunctionType.Relu
 P = 128
 PACK = 4
 PASSES = K // (P * PACK)
-WINDOW = 528
-CHUNKS = [(0, 512), (512, 512), (1024, 512), (1536, 256), (1792, 256)]
+WINDOW = 1040
 HALF = T // 2
 
 
@@ -31,16 +30,19 @@ def tile_moe_pre_lin_relu_kernel(tc, xT, w, b, gate, offs, pos1, pos2, pos3, pos
     with ExitStack() as ctx:
         keep = ctx.enter_context(tc.tile_pool(name="keep", bufs=1))
         ring = ctx.enter_context(tc.tile_pool(name="ring", bufs=3))
-        psum = ctx.enter_context(tc.psum_pool(name="psum", bufs=4))
+        psum = ctx.enter_context(tc.psum_pool(name="psum", bufs=6))
 
         slot_token = keep.tile([P, S // 16], U16, name="slot_token")
         token_slot = [keep.tile([P, T // 16], U16, name="token_slot%d" % r) for r in range(TOP)]
         x_rows = [[keep.tile([P, WINDOW], F32, name="x_rows%d_%d" % (g, j)) for j in range(PACK)] for g in range(PASSES)]
-        gates = [keep.tile([P, n], F32, name="gate%d" % s0) for s0, n in CHUNKS]
-        w_raw = [keep.tile([P, PASSES, PACK, N], F32, name="w_raw%d" % e) for e in range(E)]
-        w_bf = [keep.tile([P, PASSES, N, PACK], BF16, name="w_bf%d" % e, align_bytes=64) for e in range(E)]
-        w_codes = [keep.tile([P, PASSES * N], U32, name="w_codes%d" % e, align_bytes=64) for e in range(E)]
-        w_scales = [keep.tile([P, PASSES * N], U8, name="w_scales%d" % e, align_bytes=64) for e in range(E)]
+        gates = keep.tile([P, S], F32, name="gates")
+        w_raw = keep.tile([P, E, PASSES, PACK, N], F32, name="w_raw")
+        w_bf = keep.tile([P, E * PASSES * N * PACK], BF16, name="w_bf", align_bytes=64)
+        w_codes = keep.tile([P, E * PASSES * N], U32, name="w_codes", align_bytes=64)
+        w_scales = keep.tile([P, E * PASSES * N], U8, name="w_scales", align_bytes=64)
+        x_bf = keep.tile([P, PASSES, S * PACK], BF16, name="x_bf", align_bytes=64)
+        x_codes = keep.tile([P, PASSES, S], U32, name="x_codes", align_bytes=64)
+        x_scales = keep.tile([P, PASSES, S], U8, name="x_scales", align_bytes=64)
         bias = keep.tile([P, E], F32, name="bias")
         y = keep.tile([P, S], F32, name="y")
 
@@ -49,121 +51,115 @@ def tile_moe_pre_lin_relu_kernel(tc, xT, w, b, gate, offs, pos1, pos2, pos3, pos
         def load_x(g, j):
             nc.sync.dma_start(out=x_rows[g][j][:, 0:T], in_=x_view[g, j])
 
-        def load_gate(c):
-            s0, n = CHUNKS[c]
-            nc.sync.dma_start(out=gates[c][:], in_=gate[0:P, s0 : s0 + n])
+        def load_gate(s0, s1):
+            nc.sync.dma_start(out=gates[:, s0:s1], in_=gate[0:P, s0:s1])
 
         def load_w(e):
             nc.sync.dma_start(
-                out=w_raw[e][:].rearrange("p g j n -> p g (j n)"),
+                out=w_raw[:, e].rearrange("p g j n -> p g (j n)"),
                 in_=w[e].rearrange("(g p j) n -> p g (j n)", g=PASSES, j=PACK),
             )
 
+        load_x(0, 0)
+        load_gate(0, 256)
         nc.sync.dma_start(slot_token[:], offs)
-        load_gate(0)
-        for j in range(PACK):
-            load_x(0, j)
+        load_gate(256, 512)
+        load_gate(512, 1024)
+        load_x(0, 1)
         load_w(0)
-        for j in range(PACK):
-            load_x(1, j)
+        load_x(0, 2)
         load_w(1)
-        load_gate(1)
+        load_x(0, 3)
+        load_w(2)
+        load_x(1, 0)
+        load_w(3)
+        for j in range(1, PACK):
+            load_x(1, j)
+        load_gate(1024, S)
         nc.sync.dma_start(out=bias[:], in_=b)
-        for e in range(2, E):
+        for e in range(4, E):
             load_w(e)
-            if e < len(CHUNKS):
-                load_gate(e)
         for r, pos in enumerate((pos1, pos2, pos3, pos4)):
             nc.sync.dma_start(token_slot[r][:], pos)
 
+        def interleave(dst, src):
+            nc.scalar.copy(out=dst.rearrange("p (n j) -> p n j", j=PACK), in_=src.rearrange("p j n -> p n j"))
+
         def round_w(e):
-            nc.scalar.copy(out=w_bf[e][:], in_=w_raw[e][:].rearrange("p g j n -> p g n j"))
-
-        def quantize_w(e):
-            nc.vector.quantize_mx(
-                out=w_codes[e][:].bitcast(FP8X4), scales=w_scales[e][:], in_=w_bf[e][:].rearrange("p g n j -> p (g n j)")
-            )
-
-        x_bf, x_codes, x_scales = {}, {}, {}
-
-        def gather_x(c, g):
-            s0, n = CHUNKS[c]
-            gated = ring.tile([P, PACK, n], F32, name="gated")
-            for j in range(PACK):
-                nc.vector.tensor_tensor(
-                    gated[:, j, :], x_rows[g][j][:].indirect(slot_token[:, s0 // 16 : (s0 + n) // 16]), gates[c][:], MULT
-                )
-            x_bf[c, g] = ring.tile([P, n, PACK], BF16, name="x_bf", align_bytes=64)
-            nc.scalar.copy(out=x_bf[c, g][:], in_=gated[:].rearrange("p j n -> p n j"))
-
-        def quantize_x(c, g):
-            n = CHUNKS[c][1]
-            x_codes[c, g] = keep.tile([P, n], U32, name="x_codes%d_%d" % (c, g), align_bytes=64)
-            x_scales[c, g] = keep.tile([P, n], U8, name="x_scales%d_%d" % (c, g), align_bytes=64)
-            nc.vector.quantize_mx(
-                out=x_codes[c, g][:].bitcast(FP8X4), scales=x_scales[c, g][:], in_=x_bf[c, g][:].rearrange("p n j -> p (n j)")
-            )
-
-        def expert(e):
-            c = max(i for i, (s0, n) in enumerate(CHUNKS) if s0 <= e * C)
-            cols = slice(e * C - CHUNKS[c][0], (e + 1) * C - CHUNKS[c][0])
-            acc = psum.tile([P, C], F32, name="acc")
             for g in range(PASSES):
+                first = (e * PASSES + g) * N * PACK
+                interleave(w_bf[:, first : first + N * PACK], w_raw[:, e, g])
+
+        def quantize_w(e0, e1):
+            cols = slice(e0 * PASSES * N, e1 * PASSES * N)
+            nc.vector.quantize_mx(
+                out=w_codes[:, cols].bitcast(FP8X4), scales=w_scales[:, cols], in_=w_bf[:, cols.start * PACK : cols.stop * PACK]
+            )
+
+        def gather_x(g, s0, s1, first_cuts=(), round_cuts=()):
+            gated = ring.tile([P, PACK, s1 - s0], F32, name="gated")
+            for j in range(PACK):
+                cuts = [s0] + (list(first_cuts) if j == 0 else []) + [s1]
+                for a, z in zip(cuts, cuts[1:]):
+                    nc.vector.tensor_tensor(
+                        gated[:, j, a - s0 : z - s0], x_rows[g][j][:].indirect(slot_token[:, a // 16 : z // 16]), gates[:, a:z], MULT
+                    )
+            cuts = [s0] + list(round_cuts) + [s1]
+            for a, z in zip(cuts, cuts[1:]):
+                interleave(x_bf[:, g, a * PACK : z * PACK], gated[:, :, a - s0 : z - s0])
+
+        def quantize_x(g, s0, s1):
+            nc.vector.quantize_mx(
+                out=x_codes[:, g, s0:s1].bitcast(FP8X4), scales=x_scales[:, g, s0:s1], in_=x_bf[:, g, s0 * PACK : s1 * PACK]
+            )
+
+        def expert(s0, s1):
+            e = s0 // C
+            acc = psum.tile([P, s1 - s0], F32, name="acc")
+            for g in range(PASSES):
+                cols = slice((e * PASSES + g) * N, (e * PASSES + g + 1) * N)
                 nc.tensor.matmul_mx(
                     out=acc[:],
-                    lhsT=w_codes[e][:, g * N : (g + 1) * N].bitcast(FP8X4),
-                    lhsT_scale=w_scales[e][:, g * N : (g + 1) * N],
-                    rhs=x_codes[c, g][:, cols].bitcast(FP8X4),
-                    rhs_scale=x_scales[c, g][:, cols],
+                    lhsT=w_codes[:, cols].bitcast(FP8X4),
+                    lhsT_scale=w_scales[:, cols],
+                    rhs=x_codes[:, g, s0:s1].bitcast(FP8X4),
+                    rhs_scale=x_scales[:, g, s0:s1],
                     start=(g == 0),
                     stop=(g == PASSES - 1),
                 )
-            nc.scalar.activation(out=y[:, e * C : (e + 1) * C], in_=acc[:], func=RELU, bias=bias[:, e : e + 1])
+            nc.scalar.activation(out=y[:, s0:s1], in_=acc[:], func=RELU, bias=bias[:, e : e + 1])
 
-        round_w(0)
-        gather_x(0, 0)
-        round_w(1)
-        gather_x(0, 1)
-        quantize_x(0, 0)
-        round_w(2)
-        gather_x(1, 0)
-        quantize_x(0, 1)
-        quantize_w(0)
-        quantize_w(1)
-        round_w(3)
-        gather_x(1, 1)
-        expert(0)
-        expert(1)
-        quantize_x(1, 0)
-        round_w(4)
-        gather_x(2, 0)
-        quantize_x(1, 1)
-        quantize_w(2)
-        quantize_w(3)
-        round_w(5)
-        gather_x(2, 1)
-        expert(2)
-        expert(3)
-        quantize_x(2, 0)
-        round_w(6)
-        round_w(7)
-        gather_x(3, 0)
-        quantize_w(4)
-        quantize_w(5)
-        gather_x(3, 1)
-        quantize_x(2, 1)
-        gather_x(4, 0)
-        expert(4)
-        expert(5)
-        quantize_x(3, 0)
-        gather_x(4, 1)
-        quantize_x(3, 1)
-        quantize_w(6)
-        expert(6)
-        quantize_x(4, 0)
-        quantize_w(7)
-        quantize_x(4, 1)
-        expert(7)
+        for e in range(4):
+            round_w(e)
+        gather_x(0, 0, 1024, first_cuts=(256, 512))
+        for e in range(4, 6):
+            round_w(e)
+        gather_x(1, 0, 1024)
+        quantize_w(0, 4)
+        quantize_x(0, 0, 1024)
+        gather_x(0, 1024, 1536)
+        for e in range(6, 8):
+            round_w(e)
+        gather_x(1, 1024, 1536)
+        quantize_x(1, 0, 1024)
+        for e in range(4):
+            expert(e * C, (e + 1) * C)
+        gather_x(0, 1536, 2048)
+        quantize_w(4, 6)
+        quantize_x(0, 1024, 1536)
+        quantize_x(1, 1024, 1536)
+        gather_x(1, 1536, 1792)
+        for e in range(4, 6):
+            expert(e * C, (e + 1) * C)
+        gather_x(1, 1792, 2048, round_cuts=(1920,))
+        quantize_w(6, 8)
+        quantize_x(0, 1536, 2048)
+        quantize_x(1, 1536, 1792)
+        quantize_x(1, 1792, 1920)
+        quantize_x(1, 1920, 2048)
+        expert(1536, 1792)
+        expert(1792, 1920)
+        expert(1920, 2048)
 
         picked = keep.tile([P, 2, TOP, HALF], F32, name="picked")
         pairs = keep.tile([P, 2, 2, HALF], F32, name="pairs")

@@ -161,12 +161,20 @@ def tile_moe_pre_lin_relu_kernel(tc, xT, w, b, gate, offs, pos1, pos2, pos3, pos
         expert(1792, 1920)
         expert(1920, 2048)
 
-        picked = keep.tile([P, 2, TOP, HALF], F32, name="picked")
-        pairs = keep.tile([P, 2, 2, HALF], F32, name="pairs")
-        total = keep.tile([P, 2, HALF], F32, name="total")
+        halves = [slice(h * HALF, (h + 1) * HALF) for h in range(2)]
+        picked = [[keep.tile([P, HALF], F32, name="picked%d_%d" % (h, r)) for r in range(TOP)] for h in range(2)]
+        sums = [[picked[h][0]] + [keep.tile([P, HALF], F32, name="sum%d_%d" % (h, r)) for r in range(1, TOP)] for h in range(2)]
+
+        def pick(h, r):
+            nc.vector.tensor_copy(picked[h][r][:], y[:].indirect(token_slot[r][:, halves[h].start // 16 : halves[h].stop // 16]))
+
         for h in range(2):
-            for r in range(TOP):
-                nc.vector.tensor_copy(picked[:, h, r, :], y[:].indirect(token_slot[r][:, h * HALF // 16 : (h + 1) * HALF // 16]))
-            nc.vector.tensor_tensor(pairs[:, h], picked[:, h, 0:2, :], picked[:, h, 2:4, :], ADD)
-            nc.vector.tensor_tensor(total[:, h, :], pairs[:, h, 0, :], pairs[:, h, 1, :], ADD)
-            nc.sync.dma_start(out=out[:, h * HALF : (h + 1) * HALF], in_=total[:, h, :])
+            for r in range(TOP - 1):
+                pick(h, r)
+                if r > 0:
+                    nc.gpsimd.tensor_tensor(sums[h][r][:], sums[h][r - 1][:], picked[h][r][:], ADD)
+        for h in range(2):
+            pick(h, TOP - 1)
+        for h, queue in enumerate((nc.sync, nc.scalar)):
+            nc.vector.tensor_tensor(sums[h][TOP - 1][:], sums[h][TOP - 2][:], picked[h][TOP - 1][:], ADD)
+            queue.dma_start(out=out[:, halves[h]], in_=sums[h][TOP - 1][:])

@@ -162,19 +162,13 @@ def tile_moe_pre_lin_relu_kernel(tc, xT, w, b, gate, offs, pos1, pos2, pos3, pos
         expert(1920, 2048)
 
         halves = [slice(h * HALF, (h + 1) * HALF) for h in range(2)]
-        picked = [[keep.tile([P, HALF], F32, name="picked%d_%d" % (h, r)) for r in range(TOP)] for h in range(2)]
-        sums = [[picked[h][0]] + [keep.tile([P, HALF], F32, name="sum%d_%d" % (h, r)) for r in range(1, TOP)] for h in range(2)]
-
-        def pick(h, r):
-            nc.vector.tensor_copy(picked[h][r][:], y[:].indirect(token_slot[r][:, halves[h].start // 16 : halves[h].stop // 16]))
-
-        for h in range(2):
-            for r in range(TOP - 1):
-                pick(h, r)
-                if r > 0:
-                    nc.gpsimd.tensor_tensor(sums[h][r][:], sums[h][r - 1][:], picked[h][r][:], ADD)
-        for h in range(2):
-            pick(h, TOP - 1)
+        sums = [[keep.tile([P, HALF], F32, name="sum%d_%d" % (h, r)) for r in range(TOP)] for h in range(2)]
+        for r in range(TOP):
+            for h in range(2):
+                looked_up = y[:].indirect(token_slot[r][:, halves[h].start // 16 : halves[h].stop // 16])
+                if r == 0:
+                    nc.vector.tensor_copy(sums[h][r][:], looked_up)
+                else:
+                    nc.vector.tensor_tensor(sums[h][r][:], looked_up, sums[h][r - 1][:], ADD)
         for h, queue in enumerate((nc.sync, nc.scalar)):
-            nc.vector.tensor_tensor(sums[h][TOP - 1][:], sums[h][TOP - 2][:], picked[h][TOP - 1][:], ADD)
             queue.dma_start(out=out[:, halves[h]], in_=sums[h][TOP - 1][:])

@@ -22,29 +22,32 @@ P = 128
 PACK = 4
 PASSES = K // (P * PACK)
 WINDOW = 1040
-HALF = T // 2
+SPLIT = 256
 
 
 def tile_moe_pre_lin_relu_kernel(tc, xT, w, b, gate, offs, pos1, pos2, pos3, pos4, out):
     nc = tc.nc
     with ExitStack() as ctx:
         keep = ctx.enter_context(tc.tile_pool(name="keep", bufs=1))
-        ring = ctx.enter_context(tc.tile_pool(name="ring", bufs=3))
+        ring = ctx.enter_context(tc.tile_pool(name="ring", bufs=2))
         psum = ctx.enter_context(tc.psum_pool(name="psum", bufs=6))
 
         slot_token = keep.tile([P, S // 16], U16, name="slot_token")
         token_slot = [keep.tile([P, T // 16], U16, name="token_slot%d" % r) for r in range(TOP)]
-        x_rows = [[keep.tile([P, WINDOW], F32, name="x_rows%d_%d" % (g, j)) for j in range(PACK)] for g in range(PASSES)]
+        x_rows = [
+            [keep.tile([P, WINDOW], F32, name="x_rows%d_%d" % (g, j), align_bytes=64) for j in range(PACK)] for g in range(PASSES)
+        ]
         gates = keep.tile([P, S], F32, name="gates")
         w_raw = keep.tile([P, E, PASSES, PACK, N], F32, name="w_raw")
         w_bf = keep.tile([P, E * PASSES * N * PACK], BF16, name="w_bf", align_bytes=64)
-        w_codes = keep.tile([P, E * PASSES * N], U32, name="w_codes", align_bytes=64)
         w_scales = keep.tile([P, E * PASSES * N], U8, name="w_scales", align_bytes=64)
         x_bf = keep.tile([P, PASSES, S * PACK], BF16, name="x_bf", align_bytes=64)
-        x_codes = keep.tile([P, PASSES, S], U32, name="x_codes", align_bytes=64)
         x_scales = keep.tile([P, PASSES, S], U8, name="x_scales", align_bytes=64)
         bias = keep.tile([P, E], F32, name="bias")
         y = keep.tile([P, S], F32, name="y")
+        w_codes = {}
+        w_blocks = [(e, g) for e in range(E - 2) for g in range(PASSES)] + [(e, g) for g in range(PASSES) for e in (E - 2, E - 1)]
+        x_codes = {}
 
         x_view = xT.rearrange("(g p j) t -> g j p t", g=PASSES, j=PACK)
 
@@ -83,20 +86,25 @@ def tile_moe_pre_lin_relu_kernel(tc, xT, w, b, gate, offs, pos1, pos2, pos3, pos
             nc.sync.dma_start(token_slot[r][:], pos)
 
         def interleave(dst, src):
-            nc.scalar.copy(out=dst.rearrange("p (n j) -> p n j", j=PACK), in_=src.rearrange("p j n -> p n j"))
+            nc.scalar.copy(
+                out=dst.rearrange("p (c i j) -> p c j i", i=PACK, j=PACK), in_=src.rearrange("p j (c i) -> p c j i", i=PACK)
+            )
 
         def round_w(e):
             for g in range(PASSES):
-                first = (e * PASSES + g) * N * PACK
+                first = w_blocks.index((e, g)) * N * PACK
                 interleave(w_bf[:, first : first + N * PACK], w_raw[:, e, g])
 
-        def quantize_w(e0, e1):
-            cols = slice(e0 * PASSES * N, e1 * PASSES * N)
+        def quantize_w(b0, b1, tag=""):
+            cols = slice(b0 * N, b1 * N)
+            codes = keep.tile([P, cols.stop - cols.start], U32, name="w_codes%d" % b0, tag=tag, align_bytes=64)
             nc.vector.quantize_mx(
-                out=w_codes[:, cols].bitcast(FP8X4), scales=w_scales[:, cols], in_=w_bf[:, cols.start * PACK : cols.stop * PACK]
+                out=codes[:].bitcast(FP8X4), scales=w_scales[:, cols], in_=w_bf[:, cols.start * PACK : cols.stop * PACK]
             )
+            for block in range(b0, b1):
+                w_codes[w_blocks[block]] = codes[:, (block - b0) * N : (block - b0 + 1) * N]
 
-        def gather_x(g, s0, s1, first_cuts=(), round_cuts=()):
+        def gather_x(g, s0, s1, first_cuts=()):
             gated = ring.tile([P, PACK, s1 - s0], F32, name="gated")
             for j in range(PACK):
                 cuts = [s0] + (list(first_cuts) if j == 0 else []) + [s1]
@@ -104,25 +112,36 @@ def tile_moe_pre_lin_relu_kernel(tc, xT, w, b, gate, offs, pos1, pos2, pos3, pos
                     nc.vector.tensor_tensor(
                         gated[:, j, a - s0 : z - s0], x_rows[g][j][:].indirect(slot_token[:, a // 16 : z // 16]), gates[:, a:z], MULT
                     )
-            cuts = [s0] + list(round_cuts) + [s1]
-            for a, z in zip(cuts, cuts[1:]):
+            interleave(x_bf[:, g, s0 * PACK : s1 * PACK], gated[:])
+
+        def gather_last(g, s0, cut, s1):
+            gated = ring.tile([P, PACK, s1 - s0], F32, name="gated")
+            whole = [(j, s0, s1) for j in range(PACK // 2)]
+            halves = [(j, a, z) for a, z in ((s0, cut), (cut, s1)) for j in range(PACK // 2, PACK)]
+            for j, a, z in whole + halves:
+                nc.vector.tensor_tensor(
+                    gated[:, j, a - s0 : z - s0], x_rows[g][j][:].indirect(slot_token[:, a // 16 : z // 16]), gates[:, a:z], MULT
+                )
+            for a, z in ((s0, cut), (cut, s1)):
                 interleave(x_bf[:, g, a * PACK : z * PACK], gated[:, :, a - s0 : z - s0])
 
-        def quantize_x(g, s0, s1):
-            nc.vector.quantize_mx(
-                out=x_codes[:, g, s0:s1].bitcast(FP8X4), scales=x_scales[:, g, s0:s1], in_=x_bf[:, g, s0 * PACK : s1 * PACK]
-            )
+        def quantize_x(g, s0, s1, tag=""):
+            codes = keep.tile([P, s1 - s0], U32, name="x_codes%d_%d" % (g, s0), tag=tag, align_bytes=64)
+            nc.vector.quantize_mx(out=codes[:].bitcast(FP8X4), scales=x_scales[:, g, s0:s1], in_=x_bf[:, g, s0 * PACK : s1 * PACK])
+            for s in range(s0, s1, P):
+                x_codes[g, s] = (codes, s - s0)
 
         def expert(s0, s1):
             e = s0 // C
             acc = psum.tile([P, s1 - s0], F32, name="acc")
             for g in range(PASSES):
-                cols = slice((e * PASSES + g) * N, (e * PASSES + g + 1) * N)
+                cols = slice(w_blocks.index((e, g)) * N, (w_blocks.index((e, g)) + 1) * N)
+                codes, first = x_codes[g, s0]
                 nc.tensor.matmul_mx(
                     out=acc[:],
-                    lhsT=w_codes[:, cols].bitcast(FP8X4),
+                    lhsT=w_codes[e, g].bitcast(FP8X4),
                     lhsT_scale=w_scales[:, cols],
-                    rhs=x_codes[:, g, s0:s1].bitcast(FP8X4),
+                    rhs=codes[:, first : first + s1 - s0].bitcast(FP8X4),
                     rhs_scale=x_scales[:, g, s0:s1],
                     start=(g == 0),
                     stop=(g == PASSES - 1),
@@ -135,25 +154,24 @@ def tile_moe_pre_lin_relu_kernel(tc, xT, w, b, gate, offs, pos1, pos2, pos3, pos
         for e in range(4, 6):
             round_w(e)
         gather_x(1, 0, 1024)
-        quantize_w(0, 4)
+        quantize_w(0, 8)
         quantize_x(0, 0, 1024)
-        gather_x(0, 1024, 1536)
         for e in range(6, 8):
             round_w(e)
-        gather_x(1, 1024, 1536)
+        gather_x(0, 1024, 2048)
         quantize_x(1, 0, 1024)
+        quantize_w(8, 12)
+        quantize_w(12, 14)
         for e in range(4):
             expert(e * C, (e + 1) * C)
-        gather_x(0, 1536, 2048)
-        quantize_w(4, 6)
-        quantize_x(0, 1024, 1536)
-        quantize_x(1, 1024, 1536)
+        gather_x(1, 1024, 1536)
+        quantize_x(0, 1024, 2048)
         gather_x(1, 1536, 1792)
+        quantize_x(1, 1024, 1536)
         for e in range(4, 6):
             expert(e * C, (e + 1) * C)
-        gather_x(1, 1792, 2048, round_cuts=(1920,))
-        quantize_w(6, 8)
-        quantize_x(0, 1536, 2048)
+        gather_last(1, 1792, 1920, 2048)
+        quantize_w(14, 16, tag="x_rows1_1")
         quantize_x(1, 1536, 1792)
         quantize_x(1, 1792, 1920)
         quantize_x(1, 1920, 2048)
@@ -161,14 +179,14 @@ def tile_moe_pre_lin_relu_kernel(tc, xT, w, b, gate, offs, pos1, pos2, pos3, pos
         expert(1792, 1920)
         expert(1920, 2048)
 
-        halves = [slice(h * HALF, (h + 1) * HALF) for h in range(2)]
-        sums = [[keep.tile([P, HALF], F32, name="sum%d_%d" % (h, r)) for r in range(TOP)] for h in range(2)]
+        parts = [slice(0, SPLIT), slice(SPLIT, T)]
+        sums = [[keep.tile([P, part.stop - part.start], F32, name="sum%d_%d" % (h, r)) for r in range(TOP)] for h, part in enumerate(parts)]
         for r in range(TOP):
-            for h in range(2):
-                looked_up = y[:].indirect(token_slot[r][:, halves[h].start // 16 : halves[h].stop // 16])
+            for h, part in enumerate(parts):
+                looked_up = y[:].indirect(token_slot[r][:, part.start // 16 : part.stop // 16])
                 if r == 0:
                     nc.vector.tensor_copy(sums[h][r][:], looked_up)
                 else:
                     nc.vector.tensor_tensor(sums[h][r][:], looked_up, sums[h][r - 1][:], ADD)
         for h, queue in enumerate((nc.sync, nc.scalar)):
-            queue.dma_start(out=out[:, halves[h]], in_=sums[h][TOP - 1][:])
+            queue.dma_start(out=out[:, parts[h]], in_=sums[h][TOP - 1][:])

@@ -21,7 +21,7 @@ RELU = mybir.ActivationFunctionType.Relu
 P = 128
 PACK = 4
 PASSES = K // (P * PACK)
-WINDOW = 1040
+WINDOW = (S + 16, 1536 + 16)
 SPLIT = 256
 
 
@@ -29,13 +29,12 @@ def tile_moe_pre_lin_relu_kernel(tc, xT, w, b, gate, offs, pos1, pos2, pos3, pos
     nc = tc.nc
     with ExitStack() as ctx:
         keep = ctx.enter_context(tc.tile_pool(name="keep", bufs=1))
-        ring = ctx.enter_context(tc.tile_pool(name="ring", bufs=2))
         psum = ctx.enter_context(tc.psum_pool(name="psum", bufs=6))
 
         slot_token = keep.tile([P, S // 16], U16, name="slot_token")
         token_slot = [keep.tile([P, T // 16], U16, name="token_slot%d" % r) for r in range(TOP)]
         x_rows = [
-            [keep.tile([P, WINDOW], F32, name="x_rows%d_%d" % (g, j), align_bytes=64) for j in range(PACK)] for g in range(PASSES)
+            [keep.tile([P, WINDOW[g]], F32, name="x_rows%d_%d" % (g, j), align_bytes=64) for j in range(PACK)] for g in range(PASSES)
         ]
         gates = keep.tile([P, S], F32, name="gates")
         w_raw = keep.tile([P, E, PASSES, PACK, N], F32, name="w_raw")
@@ -44,7 +43,6 @@ def tile_moe_pre_lin_relu_kernel(tc, xT, w, b, gate, offs, pos1, pos2, pos3, pos
         x_bf = keep.tile([P, PASSES, S * PACK], BF16, name="x_bf", align_bytes=64)
         x_scales = keep.tile([P, PASSES, S], U8, name="x_scales", align_bytes=64)
         bias = keep.tile([P, E], F32, name="bias")
-        y = keep.tile([P, S], F32, name="y")
         w_codes = {}
         w_blocks = [(e, g) for e in range(E - 2) for g in range(PASSES)] + [(e, g) for g in range(PASSES) for e in (E - 2, E - 1)]
         x_codes = {}
@@ -64,21 +62,17 @@ def tile_moe_pre_lin_relu_kernel(tc, xT, w, b, gate, offs, pos1, pos2, pos3, pos
             )
 
         load_x(0, 0)
-        load_gate(0, 256)
+        load_gate(0, 128)
         nc.sync.dma_start(slot_token[:], offs)
-        load_gate(256, 512)
-        load_gate(512, 1024)
-        load_x(0, 1)
-        load_w(0)
-        load_x(0, 2)
-        load_w(1)
-        load_x(0, 3)
-        load_w(2)
-        load_x(1, 0)
-        load_w(3)
+        load_gate(128, 384)
+        load_gate(384, 896)
+        load_gate(896, S)
         for j in range(1, PACK):
+            load_x(0, j)
+            load_w(j - 1)
+        load_w(3)
+        for j in range(PACK):
             load_x(1, j)
-        load_gate(1024, S)
         nc.sync.dma_start(out=bias[:], in_=b)
         for e in range(4, E):
             load_w(e)
@@ -104,18 +98,20 @@ def tile_moe_pre_lin_relu_kernel(tc, xT, w, b, gate, offs, pos1, pos2, pos3, pos
             for block in range(b0, b1):
                 w_codes[w_blocks[block]] = codes[:, (block - b0) * N : (block - b0 + 1) * N]
 
-        def gather_x(g, s0, s1, first_cuts=()):
-            gated = ring.tile([P, PACK, s1 - s0], F32, name="gated")
+        def gather_x(g, s0, s1, tag, first_cuts=(), round_cuts=()):
+            gated = keep.tile([P, PACK, s1 - s0], F32, name="gated%d_%d" % (g, s0), tag=tag)
             for j in range(PACK):
                 cuts = [s0] + (list(first_cuts) if j == 0 else []) + [s1]
                 for a, z in zip(cuts, cuts[1:]):
                     nc.vector.tensor_tensor(
                         gated[:, j, a - s0 : z - s0], x_rows[g][j][:].indirect(slot_token[:, a // 16 : z // 16]), gates[:, a:z], MULT
                     )
-            interleave(x_bf[:, g, s0 * PACK : s1 * PACK], gated[:])
+            cuts = [s0] + list(round_cuts) + [s1]
+            for a, z in zip(cuts, cuts[1:]):
+                interleave(x_bf[:, g, a * PACK : z * PACK], gated[:, :, a - s0 : z - s0])
 
-        def gather_last(g, s0, cut, s1):
-            gated = ring.tile([P, PACK, s1 - s0], F32, name="gated")
+        def gather_last(g, s0, cut, s1, tag):
+            gated = keep.tile([P, PACK, s1 - s0], F32, name="gated%d_%d" % (g, s0), tag=tag)
             whole = [(j, s0, s1) for j in range(PACK // 2)]
             halves = [(j, a, z) for a, z in ((s0, cut), (cut, s1)) for j in range(PACK // 2, PACK)]
             for j, a, z in whole + halves:
@@ -148,29 +144,22 @@ def tile_moe_pre_lin_relu_kernel(tc, xT, w, b, gate, offs, pos1, pos2, pos3, pos
                 )
             nc.scalar.activation(out=y[:, s0:s1], in_=acc[:], func=RELU, bias=bias[:, e : e + 1])
 
-        for e in range(4):
+        for e in range(E):
             round_w(e)
-        gather_x(0, 0, 1024, first_cuts=(256, 512))
-        for e in range(4, 6):
-            round_w(e)
-        gather_x(1, 0, 1024)
-        quantize_w(0, 8)
+        y = keep.tile([P, S], F32, name="y", tag="w_raw")
+        gather_x(0, 0, S, "gated_pass0", first_cuts=(128, 384, 896))
+        gather_x(1, 0, 1536, "gated_pass1", round_cuts=(1024,))
+        quantize_w(0, 8, tag="x_rows0_1")
+        quantize_w(8, 12, tag="x_rows0_2")
+        quantize_w(12, 14, tag="x_rows0_3")
         quantize_x(0, 0, 1024)
-        for e in range(6, 8):
-            round_w(e)
-        gather_x(0, 1024, 2048)
-        quantize_x(1, 0, 1024)
-        quantize_w(8, 12)
-        quantize_w(12, 14)
-        for e in range(4):
-            expert(e * C, (e + 1) * C)
-        gather_x(1, 1024, 1536)
         quantize_x(0, 1024, 2048)
-        gather_x(1, 1536, 1792)
+        gather_x(1, 1536, 1792, "gated_pass0")
+        quantize_x(1, 0, 1024)
         quantize_x(1, 1024, 1536)
-        for e in range(4, 6):
+        for e in range(6):
             expert(e * C, (e + 1) * C)
-        gather_last(1, 1792, 1920, 2048)
+        gather_last(1, 1792, 1920, 2048, "gated_pass1")
         quantize_w(14, 16, tag="x_rows1_1")
         quantize_x(1, 1536, 1792)
         quantize_x(1, 1792, 1920)
@@ -180,7 +169,7 @@ def tile_moe_pre_lin_relu_kernel(tc, xT, w, b, gate, offs, pos1, pos2, pos3, pos
         expert(1920, 2048)
 
         parts = [slice(0, SPLIT), slice(SPLIT, T)]
-        sums = [[keep.tile([P, part.stop - part.start], F32, name="sum%d_%d" % (h, r)) for r in range(TOP)] for h, part in enumerate(parts)]
+        sums = [[keep.tile([P, part.stop - part.start], F32, name="sum%d_%d" % (h, r), tag="x_rows%d_%d" % (h, r), align_bytes=64) for r in range(TOP)] for h, part in enumerate(parts)]
         for r in range(TOP):
             for h, part in enumerate(parts):
                 looked_up = y[:].indirect(token_slot[r][:, part.start // 16 : part.stop // 16])

@@ -43,6 +43,8 @@ def tile_moe_pre_lin_relu_kernel(tc, xT, w, b, gate, offs, pos1, pos2, pos3, pos
         x_bf = keep.tile([P, PASSES, S * PACK], BF16, name="x_bf", align_bytes=64)
         x_scales = keep.tile([P, PASSES, S], U8, name="x_scales", align_bytes=64)
         bias = keep.tile([P, E], F32, name="bias")
+        gated0 = keep.tile([P, PACK, S], F32, name="gated0")
+        gated1 = keep.tile([P, PACK, 1536], F32, name="gated1")
         w_codes = {}
         w_blocks = [(e, g) for e in range(E - 2) for g in range(PASSES)] + [(e, g) for g in range(PASSES) for e in (E - 2, E - 1)]
         x_codes = {}
@@ -62,11 +64,11 @@ def tile_moe_pre_lin_relu_kernel(tc, xT, w, b, gate, offs, pos1, pos2, pos3, pos
             )
 
         load_x(0, 0)
-        load_gate(0, 128)
+        load_gate(0, 256)
         nc.sync.dma_start(slot_token[:], offs)
-        load_gate(128, 384)
-        load_gate(384, 896)
-        load_gate(896, S)
+        load_gate(256, 512)
+        load_gate(512, 1024)
+        load_gate(1024, S)
         for j in range(1, PACK):
             load_x(0, j)
             load_w(j - 1)
@@ -98,10 +100,9 @@ def tile_moe_pre_lin_relu_kernel(tc, xT, w, b, gate, offs, pos1, pos2, pos3, pos
             for block in range(b0, b1):
                 w_codes[w_blocks[block]] = codes[:, (block - b0) * N : (block - b0 + 1) * N]
 
-        def gather_x(g, s0, s1, tag, first_cuts=(), round_cuts=()):
-            gated = keep.tile([P, PACK, s1 - s0], F32, name="gated%d_%d" % (g, s0), tag=tag)
+        def gather_x(g, s0, s1, gated, first_cuts=(), round_cuts=()):
             for j in range(PACK):
-                cuts = [s0] + (list(first_cuts) if j == 0 else []) + [s1]
+                cuts = [s0] + (list(first_cuts) if j == 0 else []) + (list(round_cuts) if j == PACK - 1 else []) + [s1]
                 for a, z in zip(cuts, cuts[1:]):
                     nc.vector.tensor_tensor(
                         gated[:, j, a - s0 : z - s0], x_rows[g][j][:].indirect(slot_token[:, a // 16 : z // 16]), gates[:, a:z], MULT
@@ -110,8 +111,7 @@ def tile_moe_pre_lin_relu_kernel(tc, xT, w, b, gate, offs, pos1, pos2, pos3, pos
             for a, z in zip(cuts, cuts[1:]):
                 interleave(x_bf[:, g, a * PACK : z * PACK], gated[:, :, a - s0 : z - s0])
 
-        def gather_last(g, s0, cut, s1, tag):
-            gated = keep.tile([P, PACK, s1 - s0], F32, name="gated%d_%d" % (g, s0), tag=tag)
+        def gather_last(g, s0, cut, s1, gated):
             whole = [(j, s0, s1) for j in range(PACK // 2)]
             halves = [(j, a, z) for a, z in ((s0, cut), (cut, s1)) for j in range(PACK // 2, PACK)]
             for j, a, z in whole + halves:
@@ -147,19 +147,21 @@ def tile_moe_pre_lin_relu_kernel(tc, xT, w, b, gate, offs, pos1, pos2, pos3, pos
         for e in range(E):
             round_w(e)
         y = keep.tile([P, S], F32, name="y", tag="w_raw")
-        gather_x(0, 0, S, "gated_pass0", first_cuts=(128, 384, 896))
-        gather_x(1, 0, 1536, "gated_pass1", round_cuts=(1024,))
+        gather_x(0, 0, S, gated0, first_cuts=(256, 512, 1024))
+        gather_x(1, 0, 1536, gated1, round_cuts=(1024,))
         quantize_w(0, 8, tag="x_rows0_1")
         quantize_w(8, 12, tag="x_rows0_2")
         quantize_w(12, 14, tag="x_rows0_3")
         quantize_x(0, 0, 1024)
         quantize_x(0, 1024, 2048)
-        gather_x(1, 1536, 1792, "gated_pass0")
         quantize_x(1, 0, 1024)
-        quantize_x(1, 1024, 1536)
-        for e in range(6):
+        for e in range(4):
             expert(e * C, (e + 1) * C)
-        gather_last(1, 1792, 1920, 2048, "gated_pass1")
+        gather_x(1, 1536, 1792, gated1[:, :, 0:256])
+        quantize_x(1, 1024, 1536)
+        for e in range(4, 6):
+            expert(e * C, (e + 1) * C)
+        gather_last(1, 1792, 1920, 2048, gated1[:, :, 1024:1280])
         quantize_w(14, 16, tag="x_rows1_1")
         quantize_x(1, 1536, 1792)
         quantize_x(1, 1792, 1920)

@@ -21,8 +21,8 @@ RELU = mybir.ActivationFunctionType.Relu
 P = 128
 PACK = 4
 PASSES = K // (P * PACK)
-WINDOW = (S + 16, 1536 + 16)
-SPLIT = 256
+WINDOW = ((1024 + 16, S + 16, S + 16, S + 16), (1536 + 16,) * PACK)
+LAST = 64
 
 
 def tile_moe_pre_lin_relu_kernel(tc, xT, w, b, gate, offs, pos1, pos2, pos3, pos4, out):
@@ -34,7 +34,7 @@ def tile_moe_pre_lin_relu_kernel(tc, xT, w, b, gate, offs, pos1, pos2, pos3, pos
         slot_token = keep.tile([P, S // 16], U16, name="slot_token")
         token_slot = [keep.tile([P, T // 16], U16, name="token_slot%d" % r) for r in range(TOP)]
         x_rows = [
-            [keep.tile([P, WINDOW[g]], F32, name="x_rows%d_%d" % (g, j), align_bytes=64) for j in range(PACK)] for g in range(PASSES)
+            [keep.tile([P, WINDOW[g][j]], F32, name="x_rows%d_%d" % (g, j), align_bytes=64) for j in range(PACK)] for g in range(PASSES)
         ]
         gates = keep.tile([P, S], F32, name="gates")
         w_raw = keep.tile([P, E, PASSES, PACK, N], F32, name="w_raw")
@@ -64,8 +64,9 @@ def tile_moe_pre_lin_relu_kernel(tc, xT, w, b, gate, offs, pos1, pos2, pos3, pos
             )
 
         load_x(0, 0)
-        load_gate(0, 256)
+        load_gate(0, 64)
         nc.sync.dma_start(slot_token[:], offs)
+        load_gate(64, 256)
         load_gate(256, 512)
         load_gate(512, 1024)
         load_gate(1024, S)
@@ -147,7 +148,7 @@ def tile_moe_pre_lin_relu_kernel(tc, xT, w, b, gate, offs, pos1, pos2, pos3, pos
         for e in range(E):
             round_w(e)
         y = keep.tile([P, S], F32, name="y", tag="w_raw")
-        gather_x(0, 0, S, gated0, first_cuts=(256, 512, 1024))
+        gather_x(0, 0, S, gated0, first_cuts=(64, 256, 512, 1024))
         gather_x(1, 0, 1536, gated1, round_cuts=(1024,))
         quantize_w(0, 8, tag="x_rows0_1")
         quantize_w(8, 12, tag="x_rows0_2")
@@ -170,14 +171,15 @@ def tile_moe_pre_lin_relu_kernel(tc, xT, w, b, gate, offs, pos1, pos2, pos3, pos
         expert(1792, 1920)
         expert(1920, 2048)
 
-        parts = [slice(0, SPLIT), slice(SPLIT, T)]
-        sums = [[keep.tile([P, part.stop - part.start], F32, name="sum%d_%d" % (h, r), tag="x_rows%d_%d" % (h, r), align_bytes=64) for r in range(TOP)] for h, part in enumerate(parts)]
+        halves = [slice(0, T // 2), slice(T // 2, T)]
+        sums = [keep.tile([P, T], F32, name="sum%d" % r) for r in range(TOP)]
         for r in range(TOP):
-            for h, part in enumerate(parts):
+            parts = halves if r < TOP - 1 else [halves[0], slice(T // 2, T - LAST), slice(T - LAST, T)]
+            for part in parts:
                 looked_up = y[:].indirect(token_slot[r][:, part.start // 16 : part.stop // 16])
                 if r == 0:
-                    nc.vector.tensor_copy(sums[h][r][:], looked_up)
+                    nc.vector.tensor_copy(sums[r][:, part], looked_up)
                 else:
-                    nc.vector.tensor_tensor(sums[h][r][:], looked_up, sums[h][r - 1][:], ADD)
-        for h, queue in enumerate((nc.sync, nc.scalar)):
-            queue.dma_start(out=out[:, parts[h]], in_=sums[h][TOP - 1][:])
+                    nc.vector.tensor_tensor(sums[r][:, part], looked_up, sums[r - 1][:, part], ADD)
+                if r == TOP - 1:
+                    nc.sync.dma_start(out=out[:, part], in_=sums[r][:, part])

@@ -16,13 +16,21 @@ U8 = mybir.dt.uint8
 FP8X4 = mybir.dt.float8_e4m3fn_x4
 MULT = mybir.AluOpType.mult
 ADD = mybir.AluOpType.add
+MAX = mybir.AluOpType.max
 RELU = mybir.ActivationFunctionType.Relu
 
 P = 128
 PACK = 4
 PASSES = K // (P * PACK)
-WINDOW = ((1024 + 16, S + 16, S + 16, S + 16), (1536 + 16,) * PACK)
-LAST = 64
+STRIPE = 16
+MX_ALIGN = 64
+WIDEST = 1024
+
+GATE_CUTS = (64, 256, 512, 1024, S)
+LONG = (E - 2) * C
+LAST_EXPERT = (E - 1) * C
+LAST_HALF = LAST_EXPERT + C // 2
+LAST_TOKENS = 64
 
 
 def tile_moe_pre_lin_relu_kernel(tc, xT, w, b, gate, offs, pos1, pos2, pos3, pos4, out):
@@ -31,22 +39,23 @@ def tile_moe_pre_lin_relu_kernel(tc, xT, w, b, gate, offs, pos1, pos2, pos3, pos
         keep = ctx.enter_context(tc.tile_pool(name="keep", bufs=1))
         psum = ctx.enter_context(tc.psum_pool(name="psum", bufs=6))
 
-        slot_token = keep.tile([P, S // 16], U16, name="slot_token")
-        token_slot = [keep.tile([P, T // 16], U16, name="token_slot%d" % r) for r in range(TOP)]
+        most_slots = [[S // 2] + [S] * (PACK - 1), [LONG] * PACK]
+        slot_token = keep.tile([P, S // STRIPE], U16, name="slot_token")
+        token_slot = [keep.tile([P, T // STRIPE], U16, name="token_slot%d" % r) for r in range(TOP)]
         x_rows = [
-            [keep.tile([P, WINDOW[g][j]], F32, name="x_rows%d_%d" % (g, j), align_bytes=64) for j in range(PACK)] for g in range(PASSES)
+            [keep.tile([P, most_slots[g][j] + STRIPE], F32, name="x_rows%d_%d" % (g, j), align_bytes=MX_ALIGN) for j in range(PACK)]
+            for g in range(PASSES)
         ]
         gates = keep.tile([P, S], F32, name="gates")
         w_raw = keep.tile([P, E, PASSES, PACK, N], F32, name="w_raw")
-        w_bf = keep.tile([P, E * PASSES * N * PACK], BF16, name="w_bf", align_bytes=64)
-        w_scales = keep.tile([P, E * PASSES * N], U8, name="w_scales", align_bytes=64)
-        x_bf = keep.tile([P, PASSES, S * PACK], BF16, name="x_bf", align_bytes=64)
-        x_scales = keep.tile([P, PASSES, S], U8, name="x_scales", align_bytes=64)
+        w_bf = keep.tile([P, E * PASSES * N * PACK], BF16, name="w_bf", align_bytes=MX_ALIGN)
+        w_scales = keep.tile([P, E * PASSES * N], U8, name="w_scales", align_bytes=MX_ALIGN)
+        x_bf = keep.tile([P, PASSES, S * PACK], BF16, name="x_bf", align_bytes=MX_ALIGN)
+        x_scales = keep.tile([P, PASSES, S], U8, name="x_scales", align_bytes=MX_ALIGN)
         bias = keep.tile([P, E], F32, name="bias")
         gated0 = keep.tile([P, PACK, S], F32, name="gated0")
-        gated1 = keep.tile([P, PACK, 1536], F32, name="gated1")
+        gated1 = keep.tile([P, PACK, LONG], F32, name="gated1")
         w_codes = {}
-        w_blocks = [(e, g) for e in range(E - 2) for g in range(PASSES)] + [(e, g) for g in range(PASSES) for e in (E - 2, E - 1)]
         x_codes = {}
 
         x_view = xT.rearrange("(g p j) t -> g j p t", g=PASSES, j=PACK)
@@ -64,20 +73,18 @@ def tile_moe_pre_lin_relu_kernel(tc, xT, w, b, gate, offs, pos1, pos2, pos3, pos
             )
 
         load_x(0, 0)
-        load_gate(0, 64)
+        load_gate(0, GATE_CUTS[0])
         nc.sync.dma_start(slot_token[:], offs)
-        load_gate(64, 256)
-        load_gate(256, 512)
-        load_gate(512, 1024)
-        load_gate(1024, S)
+        for s0, s1 in zip(GATE_CUTS, GATE_CUTS[1:]):
+            load_gate(s0, s1)
         for j in range(1, PACK):
             load_x(0, j)
             load_w(j - 1)
-        load_w(3)
+        load_w(PACK - 1)
         for j in range(PACK):
             load_x(1, j)
         nc.sync.dma_start(out=bias[:], in_=b)
-        for e in range(4, E):
+        for e in range(PACK, E):
             load_w(e)
         for r, pos in enumerate((pos1, pos2, pos3, pos4)):
             nc.sync.dma_start(token_slot[r][:], pos)
@@ -87,99 +94,123 @@ def tile_moe_pre_lin_relu_kernel(tc, xT, w, b, gate, offs, pos1, pos2, pos3, pos
                 out=dst.rearrange("p (c i j) -> p c j i", i=PACK, j=PACK), in_=src.rearrange("p j (c i) -> p c j i", i=PACK)
             )
 
-        def round_w(e):
-            for g in range(PASSES):
-                first = w_blocks.index((e, g)) * N * PACK
-                interleave(w_bf[:, first : first + N * PACK], w_raw[:, e, g])
+        def gather_row(g, j, s0, s1, dst):
+            window = x_rows[g][j][:].indirect(slot_token[:, s0 // STRIPE : s1 // STRIPE])
+            nc.vector.tensor_tensor(dst, window, gates[:, s0:s1], MULT)
 
-        def quantize_w(b0, b1, tag=""):
-            cols = slice(b0 * N, b1 * N)
-            codes = keep.tile([P, cols.stop - cols.start], U32, name="w_codes%d" % b0, tag=tag, align_bytes=64)
+        def round_x(g, s0, s1, src):
+            interleave(x_bf[:, g, s0 * PACK : s1 * PACK], src)
+
+        def words_tile(width, name, after):
+            tag = "x_rows%d_%d" % after if after else name
+            return keep.tile([P, width], U32, name=name, tag=tag, align_bytes=MX_ALIGN)
+
+        def quantize_w(m0, m1, after):
+            codes = words_tile((m1 - m0) * N, "w_codes%d" % m0, after)
             nc.vector.quantize_mx(
-                out=codes[:].bitcast(FP8X4), scales=w_scales[:, cols], in_=w_bf[:, cols.start * PACK : cols.stop * PACK]
+                out=codes[:].bitcast(FP8X4), scales=w_scales[:, m0 * N : m1 * N], in_=w_bf[:, m0 * N * PACK : m1 * N * PACK]
             )
-            for block in range(b0, b1):
-                w_codes[w_blocks[block]] = codes[:, (block - b0) * N : (block - b0 + 1) * N]
+            for m in range(m0, m1):
+                w_codes[m] = codes[:, (m - m0) * N : (m - m0 + 1) * N]
 
-        def gather_x(g, s0, s1, gated, first_cuts=(), round_cuts=()):
-            for j in range(PACK):
-                cuts = [s0] + (list(first_cuts) if j == 0 else []) + (list(round_cuts) if j == PACK - 1 else []) + [s1]
-                for a, z in zip(cuts, cuts[1:]):
-                    nc.vector.tensor_tensor(
-                        gated[:, j, a - s0 : z - s0], x_rows[g][j][:].indirect(slot_token[:, a // 16 : z // 16]), gates[:, a:z], MULT
-                    )
-            cuts = [s0] + list(round_cuts) + [s1]
-            for a, z in zip(cuts, cuts[1:]):
-                interleave(x_bf[:, g, a * PACK : z * PACK], gated[:, :, a - s0 : z - s0])
-
-        def gather_last(g, s0, cut, s1, gated):
-            whole = [(j, s0, s1) for j in range(PACK // 2)]
-            halves = [(j, a, z) for a, z in ((s0, cut), (cut, s1)) for j in range(PACK // 2, PACK)]
-            for j, a, z in whole + halves:
-                nc.vector.tensor_tensor(
-                    gated[:, j, a - s0 : z - s0], x_rows[g][j][:].indirect(slot_token[:, a // 16 : z // 16]), gates[:, a:z], MULT
-                )
-            for a, z in ((s0, cut), (cut, s1)):
-                interleave(x_bf[:, g, a * PACK : z * PACK], gated[:, :, a - s0 : z - s0])
-
-        def quantize_x(g, s0, s1, tag=""):
-            codes = keep.tile([P, s1 - s0], U32, name="x_codes%d_%d" % (g, s0), tag=tag, align_bytes=64)
+        def quantize_x(g, s0, s1, after=None):
+            codes = words_tile(s1 - s0, "x_codes%d_%d" % (g, s0), after)
             nc.vector.quantize_mx(out=codes[:].bitcast(FP8X4), scales=x_scales[:, g, s0:s1], in_=x_bf[:, g, s0 * PACK : s1 * PACK])
             for s in range(s0, s1, P):
                 x_codes[g, s] = (codes, s - s0)
 
-        def expert(s0, s1):
-            e = s0 // C
+        def multiply(s0, s1):
             acc = psum.tile([P, s1 - s0], F32, name="acc")
             for g in range(PASSES):
-                cols = slice(w_blocks.index((e, g)) * N, (w_blocks.index((e, g)) + 1) * N)
+                m = s0 // C * PASSES + g
                 codes, first = x_codes[g, s0]
                 nc.tensor.matmul_mx(
                     out=acc[:],
-                    lhsT=w_codes[e, g].bitcast(FP8X4),
-                    lhsT_scale=w_scales[:, cols],
+                    lhsT=w_codes[m].bitcast(FP8X4),
+                    lhsT_scale=w_scales[:, m * N : (m + 1) * N],
                     rhs=codes[:, first : first + s1 - s0].bitcast(FP8X4),
                     rhs_scale=x_scales[:, g, s0:s1],
                     start=(g == 0),
                     stop=(g == PASSES - 1),
                 )
-            nc.scalar.activation(out=y[:, s0:s1], in_=acc[:], func=RELU, bias=bias[:, e : e + 1])
+            return acc
+
+        def finish_on_scalar(s0, s1):
+            e = s0 // C
+            nc.scalar.activation(out=y[:, s0:s1], in_=multiply(s0, s1)[:], func=RELU, bias=bias[:, e : e + 1])
+
+        def finish_on_vector(s0, s1):
+            e = s0 // C
+            nc.vector.tensor_scalar(out=y[:, s0:s1], in0=multiply(s0, s1)[:], scalar1=bias[:, e : e + 1], scalar2=0.0, op0=ADD, op1=MAX)
 
         for e in range(E):
-            round_w(e)
+            for g in range(PASSES):
+                m = e * PASSES + g
+                interleave(w_bf[:, m * N * PACK : (m + 1) * N * PACK], w_raw[:, e, g])
         y = keep.tile([P, S], F32, name="y", tag="w_raw")
-        gather_x(0, 0, S, gated0, first_cuts=(64, 256, 512, 1024))
-        gather_x(1, 0, 1536, gated1, round_cuts=(1024,))
-        quantize_w(0, 8, tag="x_rows0_1")
-        quantize_w(8, 12, tag="x_rows0_2")
-        quantize_w(12, 14, tag="x_rows0_3")
-        quantize_x(0, 0, 1024)
-        quantize_x(0, 1024, 2048)
-        quantize_x(1, 0, 1024)
-        for e in range(4):
-            expert(e * C, (e + 1) * C)
-        gather_x(1, 1536, 1792, gated1[:, :, 0:256])
-        quantize_x(1, 1024, 1536)
-        for e in range(4, 6):
-            expert(e * C, (e + 1) * C)
-        gather_last(1, 1792, 1920, 2048, gated1[:, :, 1024:1280])
-        quantize_w(14, 16, tag="x_rows1_1")
-        quantize_x(1, 1536, 1792)
-        quantize_x(1, 1792, 1920)
-        quantize_x(1, 1920, 2048)
-        expert(1536, 1792)
-        expert(1792, 1920)
-        expert(1920, 2048)
+
+        for s0, s1 in zip((0,) + GATE_CUTS, GATE_CUTS):
+            gather_row(0, 0, s0, s1, gated0[:, 0, s0:s1])
+        for j in range(1, PACK):
+            gather_row(0, j, 0, S, gated0[:, j, :])
+        round_x(0, 0, S, gated0[:])
+
+        for j in range(PACK - 1):
+            gather_row(1, j, 0, LONG, gated1[:, j, :])
+        for s0, s1 in ((0, WIDEST), (WIDEST, LONG)):
+            gather_row(1, PACK - 1, s0, s1, gated1[:, PACK - 1, s0:s1])
+        for s0, s1 in ((0, WIDEST), (WIDEST, LONG)):
+            round_x(1, s0, s1, gated1[:, :, s0:s1])
+
+        quantize_w(0, 8, after=(0, 1))
+        quantize_w(8, 12, after=(0, 2))
+        quantize_w(12, 14, after=(0, 3))
+        quantize_w(14, 15, after=(0, 0))
+        quantize_x(0, 0, WIDEST)
+        quantize_x(0, WIDEST, LONG)
+        quantize_x(0, LONG, LAST_EXPERT)
+        quantize_x(1, 0, WIDEST)
+        for s in range(0, WIDEST, C):
+            finish_on_scalar(s, s + C)
+
+        for j in range(PACK):
+            gather_row(1, j, LONG, LAST_EXPERT, gated1[:, j, 0:C])
+        round_x(1, LONG, LAST_EXPERT, gated1[:, :, 0:C])
+        quantize_x(1, WIDEST, LONG)
+        for s in range(WIDEST, LONG, C):
+            finish_on_scalar(s, s + C)
+
+        gated_last = gated1[:, :, WIDEST : WIDEST + C]
+        last_halves = ((LAST_EXPERT, LAST_HALF), (LAST_HALF, S))
+        for j in range(PACK // 2):
+            gather_row(1, j, LAST_EXPERT, S, gated_last[:, j, :])
+        for s0, s1 in last_halves:
+            for j in range(PACK // 2, PACK):
+                gather_row(1, j, s0, s1, gated_last[:, j, s0 - LAST_EXPERT : s1 - LAST_EXPERT])
+        for s0, s1 in last_halves:
+            round_x(1, s0, s1, gated_last[:, :, s0 - LAST_EXPERT : s1 - LAST_EXPERT])
+
+        quantize_x(0, LAST_EXPERT, S, after=(1, 0))
+        quantize_x(1, LONG, LAST_EXPERT)
+        quantize_w(15, 16, after=(1, 1))
+        for s0, s1 in last_halves:
+            quantize_x(1, s0, s1)
+        finish_on_scalar(LONG, LAST_EXPERT)
+        finish_on_scalar(LAST_EXPERT, LAST_HALF)
+        finish_on_vector(LAST_HALF, S)
 
         halves = [slice(0, T // 2), slice(T // 2, T)]
+        last_parts = [halves[0], slice(T // 2, T - LAST_TOKENS), slice(T - LAST_TOKENS, T)]
         sums = [keep.tile([P, T], F32, name="sum%d" % r) for r in range(TOP)]
-        for r in range(TOP):
-            parts = halves if r < TOP - 1 else [halves[0], slice(T // 2, T - LAST), slice(T - LAST, T)]
-            for part in parts:
-                looked_up = y[:].indirect(token_slot[r][:, part.start // 16 : part.stop // 16])
-                if r == 0:
-                    nc.vector.tensor_copy(sums[r][:, part], looked_up)
-                else:
-                    nc.vector.tensor_tensor(sums[r][:, part], looked_up, sums[r - 1][:, part], ADD)
-                if r == TOP - 1:
-                    nc.sync.dma_start(out=out[:, part], in_=sums[r][:, part])
+
+        def results(r, part):
+            return y[:].indirect(token_slot[r][:, part.start // STRIPE : part.stop // STRIPE])
+
+        for part in halves:
+            nc.vector.tensor_copy(sums[0][:, part], results(0, part))
+        for r in range(1, TOP - 1):
+            for part in halves:
+                nc.vector.tensor_tensor(sums[r][:, part], results(r, part), sums[r - 1][:, part], ADD)
+        for part in last_parts:
+            nc.vector.tensor_tensor(sums[TOP - 1][:, part], results(TOP - 1, part), sums[TOP - 2][:, part], ADD)
+            nc.sync.dma_start(out=out[:, part], in_=sums[TOP - 1][:, part])

@@ -27,6 +27,8 @@ MX_ALIGN = 64
 WIDEST = 1024
 
 GATE_CUTS = (64, 256, 512, 1024, S)
+HALF = S // 2
+FIRST_STEP = 5 * C
 LONG = (E - 2) * C
 LAST_EXPERT = (E - 1) * C
 LAST_HALF = LAST_EXPERT + C // 2
@@ -37,9 +39,9 @@ def tile_moe_pre_lin_relu_kernel(tc, xT, w, b, gate, offs, pos1, pos2, pos3, pos
     nc = tc.nc
     with ExitStack() as ctx:
         keep = ctx.enter_context(tc.tile_pool(name="keep", bufs=1))
-        psum = ctx.enter_context(tc.psum_pool(name="psum", bufs=6))
+        psum = ctx.enter_context(tc.psum_pool(name="psum", bufs=8))
 
-        most_slots = [[S // 2] + [S] * (PACK - 1), [LONG] * PACK]
+        most_slots = [[S // 2] + [S] * (PACK - 1), [FIRST_STEP] * PACK]
         slot_token = keep.tile([P, S // STRIPE], U16, name="slot_token")
         token_slot = [keep.tile([P, T // STRIPE], U16, name="token_slot%d" % r) for r in range(TOP)]
         x_rows = [
@@ -54,7 +56,10 @@ def tile_moe_pre_lin_relu_kernel(tc, xT, w, b, gate, offs, pos1, pos2, pos3, pos
         x_scales = keep.tile([P, PASSES, S], U8, name="x_scales", align_bytes=MX_ALIGN)
         bias = keep.tile([P, E], F32, name="bias")
         gated0 = keep.tile([P, PACK, S], F32, name="gated0")
-        gated1 = keep.tile([P, PACK, LONG], F32, name="gated1")
+        gated1 = [
+            keep.tile([P, PACK, width], F32, name="gated1_%d" % step, align_bytes=MX_ALIGN)
+            for step, width in enumerate((FIRST_STEP, S - FIRST_STEP))
+        ]
         w_codes = {}
         x_codes = {}
 
@@ -102,20 +107,19 @@ def tile_moe_pre_lin_relu_kernel(tc, xT, w, b, gate, offs, pos1, pos2, pos3, pos
             interleave(x_bf[:, g, s0 * PACK : s1 * PACK], src)
 
         def words_tile(width, name, after):
-            tag = "x_rows%d_%d" % after if after else name
-            return keep.tile([P, width], U32, name=name, tag=tag, align_bytes=MX_ALIGN)
+            return keep.tile([P, width], U32, name=name, tag=after or name, align_bytes=MX_ALIGN)
 
-        def quantize_w(m0, m1, after):
-            codes = words_tile((m1 - m0) * N, "w_codes%d" % m0, after)
+        def quantize_w(m0, m1, codes):
             nc.vector.quantize_mx(
-                out=codes[:].bitcast(FP8X4), scales=w_scales[:, m0 * N : m1 * N], in_=w_bf[:, m0 * N * PACK : m1 * N * PACK]
+                out=codes.bitcast(FP8X4), scales=w_scales[:, m0 * N : m1 * N], in_=w_bf[:, m0 * N * PACK : m1 * N * PACK]
             )
             for m in range(m0, m1):
                 w_codes[m] = codes[:, (m - m0) * N : (m - m0 + 1) * N]
 
-        def quantize_x(g, s0, s1, after=None):
-            codes = words_tile(s1 - s0, "x_codes%d_%d" % (g, s0), after)
-            nc.vector.quantize_mx(out=codes[:].bitcast(FP8X4), scales=x_scales[:, g, s0:s1], in_=x_bf[:, g, s0 * PACK : s1 * PACK])
+        def quantize_x(g, s0, s1, codes=None):
+            if codes is None:
+                codes = words_tile(s1 - s0, "x_codes%d_%d" % (g, s0), None)[:]
+            nc.vector.quantize_mx(out=codes.bitcast(FP8X4), scales=x_scales[:, g, s0:s1], in_=x_bf[:, g, s0 * PACK : s1 * PACK])
             for s in range(s0, s1, P):
                 x_codes[g, s] = (codes, s - s0)
 
@@ -155,49 +159,29 @@ def tile_moe_pre_lin_relu_kernel(tc, xT, w, b, gate, offs, pos1, pos2, pos3, pos
             gather_row(0, j, 0, S, gated0[:, j, :])
         round_x(0, 0, S, gated0[:])
 
-        for j in range(PACK - 1):
-            gather_row(1, j, 0, LONG, gated1[:, j, :])
-        for s0, s1 in ((0, WIDEST), (WIDEST, LONG)):
-            gather_row(1, PACK - 1, s0, s1, gated1[:, PACK - 1, s0:s1])
-        for s0, s1 in ((0, WIDEST), (WIDEST, LONG)):
-            round_x(1, s0, s1, gated1[:, :, s0:s1])
+        for step, (s0, s1) in enumerate(((0, FIRST_STEP), (FIRST_STEP, S))):
+            for j in range(PACK):
+                gather_row(1, j, s0, s1, gated1[step][:, j, :])
+            round_x(1, s0, s1, gated1[step][:])
 
-        quantize_w(0, 8, after=(0, 1))
-        quantize_w(8, 12, after=(0, 2))
-        quantize_w(12, 14, after=(0, 3))
-        quantize_w(14, 15, after=(0, 0))
-        quantize_x(0, 0, WIDEST)
-        quantize_x(0, WIDEST, LONG)
-        quantize_x(0, LONG, LAST_EXPERT)
-        quantize_x(1, 0, WIDEST)
-        for s in range(0, WIDEST, C):
+        quantize_w(0, E, words_tile(HALF, "w_codes0", "x_rows1_2")[:])
+        quantize_x(0, 0, HALF, words_tile(HALF, "x_codes0_0", "x_rows1_3")[:])
+        quantize_x(1, 0, HALF)
+        for s in range(0, HALF, C):
             finish_on_scalar(s, s + C)
-
-        for j in range(PACK):
-            gather_row(1, j, LONG, LAST_EXPERT, gated1[:, j, 0:C])
-        round_x(1, LONG, LAST_EXPERT, gated1[:, :, 0:C])
-        quantize_x(1, WIDEST, LONG)
-        for s in range(WIDEST, LONG, C):
+        late = words_tile(LONG, "late_codes", "gated1_0")
+        quantize_w(E, 2 * E, late[:, 0:HALF])
+        quantize_x(0, HALF, LONG, late[:, HALF:LONG])
+        quantize_x(1, HALF, LONG)
+        for s in range(HALF, LONG, C):
             finish_on_scalar(s, s + C)
-
-        gated_last = gated1[:, :, WIDEST : WIDEST + C]
-        last_halves = ((LAST_EXPERT, LAST_HALF), (LAST_HALF, S))
-        for j in range(PACK // 2):
-            gather_row(1, j, LAST_EXPERT, S, gated_last[:, j, :])
-        for s0, s1 in last_halves:
-            for j in range(PACK // 2, PACK):
-                gather_row(1, j, s0, s1, gated_last[:, j, s0 - LAST_EXPERT : s1 - LAST_EXPERT])
-        for s0, s1 in last_halves:
-            round_x(1, s0, s1, gated_last[:, :, s0 - LAST_EXPERT : s1 - LAST_EXPERT])
-
-        quantize_x(0, LAST_EXPERT, S, after=(1, 0))
+        quantize_x(0, LONG, S, words_tile(S - LONG, "last_codes", "gated1_1")[:])
         quantize_x(1, LONG, LAST_EXPERT)
-        quantize_w(15, 16, after=(1, 1))
-        for s0, s1 in last_halves:
+        for s0, s1 in ((LAST_EXPERT, LAST_HALF), (LAST_HALF, S)):
             quantize_x(1, s0, s1)
         finish_on_scalar(LONG, LAST_EXPERT)
-        finish_on_scalar(LAST_EXPERT, LAST_HALF)
-        finish_on_vector(LAST_HALF, S)
+        finish_on_vector(LAST_EXPERT, LAST_HALF)
+        finish_on_scalar(LAST_HALF, S)
 
         halves = [slice(0, T // 2), slice(T // 2, T)]
         last_parts = [halves[0], slice(T // 2, T - LAST_TOKENS), slice(T - LAST_TOKENS, T)]

@@ -55,7 +55,7 @@ def tile_moe_pre_lin_relu_kernel(tc, xT, w, b, gate, offs, pos1, pos2, pos3, pos
         x_bf = keep.tile([P, PASSES, S * PACK], BF16, name="x_bf", align_bytes=MX_ALIGN)
         x_scales = keep.tile([P, PASSES, S], U8, name="x_scales", align_bytes=MX_ALIGN)
         bias = keep.tile([P, E], F32, name="bias")
-        gated0 = keep.tile([P, PACK, S], F32, name="gated0")
+        gated0 = keep.tile([P, PACK, S], F32, name="gated0", align_bytes=MX_ALIGN)
         gated1 = [
             keep.tile([P, PACK, width], F32, name="gated1_%d" % step, align_bytes=MX_ALIGN)
             for step, width in enumerate((FIRST_STEP, S - FIRST_STEP))
@@ -166,12 +166,13 @@ def tile_moe_pre_lin_relu_kernel(tc, xT, w, b, gate, offs, pos1, pos2, pos3, pos
 
         quantize_w(0, E, words_tile(HALF, "w_codes0", "x_rows1_2")[:])
         quantize_x(0, 0, HALF, words_tile(HALF, "x_codes0_0", "x_rows1_3")[:])
+        quantize_w(E, E + 4, words_tile(4 * N, "w_codes8", "gated0")[:])
         quantize_x(1, 0, HALF)
         for s in range(0, HALF, C):
             finish_on_scalar(s, s + C)
-        late = words_tile(LONG, "late_codes", "gated1_0")
-        quantize_w(E, 2 * E, late[:, 0:HALF])
-        quantize_x(0, HALF, LONG, late[:, HALF:LONG])
+        late = words_tile(HALF, "late_codes", "gated1_0")
+        quantize_w(E + 4, 2 * E, late[:, 0 : 4 * N])
+        quantize_x(0, HALF, LONG, late[:, 4 * N : HALF])
         quantize_x(1, HALF, LONG)
         for s in range(HALF, LONG, C):
             finish_on_scalar(s, s + C)

@@ -24,15 +24,14 @@ PACK = 4
 PASSES = K // (P * PACK)
 STRIPE = 16
 MX_ALIGN = 64
-WIDEST = 1024
 
-GATE_CUTS = (64, 256, 512, 1024, S)
-HALF = S // 2
+GATE_CUTS = (128, 256, 512, 1024, S)
 FIRST_STEP = 5 * C
-LONG = (E - 2) * C
+MIDDLE_GROUP = 4 * C
+LAST_GROUP = 6 * C
 LAST_EXPERT = (E - 1) * C
 LAST_HALF = LAST_EXPERT + C // 2
-LAST_TOKENS = 64
+LAST_TOKENS = 128
 
 
 def tile_moe_pre_lin_relu_kernel(tc, xT, w, b, gate, offs, pos1, pos2, pos3, pos4, out):
@@ -106,10 +105,11 @@ def tile_moe_pre_lin_relu_kernel(tc, xT, w, b, gate, offs, pos1, pos2, pos3, pos
         def round_x(g, s0, s1, src):
             interleave(x_bf[:, g, s0 * PACK : s1 * PACK], src)
 
-        def words_tile(width, name, after):
-            return keep.tile([P, width], U32, name=name, tag=after or name, align_bytes=MX_ALIGN)
+        def words_tile(width, name, after=None):
+            return keep.tile([P, width], U32, name=name, tag=after or name, align_bytes=MX_ALIGN)[:]
 
-        def quantize_w(m0, m1, codes):
+        def quantize_w(e0, e1, codes):
+            m0, m1 = e0 * PASSES, e1 * PASSES
             nc.vector.quantize_mx(
                 out=codes.bitcast(FP8X4), scales=w_scales[:, m0 * N : m1 * N], in_=w_bf[:, m0 * N * PACK : m1 * N * PACK]
             )
@@ -118,7 +118,7 @@ def tile_moe_pre_lin_relu_kernel(tc, xT, w, b, gate, offs, pos1, pos2, pos3, pos
 
         def quantize_x(g, s0, s1, codes=None):
             if codes is None:
-                codes = words_tile(s1 - s0, "x_codes%d_%d" % (g, s0), None)[:]
+                codes = words_tile(s1 - s0, "x_codes%d_%d" % (g, s0))
             nc.vector.quantize_mx(out=codes.bitcast(FP8X4), scales=x_scales[:, g, s0:s1], in_=x_bf[:, g, s0 * PACK : s1 * PACK])
             for s in range(s0, s1, P):
                 x_codes[g, s] = (codes, s - s0)
@@ -164,23 +164,26 @@ def tile_moe_pre_lin_relu_kernel(tc, xT, w, b, gate, offs, pos1, pos2, pos3, pos
                 gather_row(1, j, s0, s1, gated1[step][:, j, :])
             round_x(1, s0, s1, gated1[step][:])
 
-        quantize_w(0, E, words_tile(HALF, "w_codes0", "x_rows1_2")[:])
-        quantize_x(0, 0, HALF, words_tile(HALF, "x_codes0_0", "x_rows1_3")[:])
-        quantize_w(E, E + 4, words_tile(4 * N, "w_codes8", "gated0")[:])
-        quantize_x(1, 0, HALF)
-        for s in range(0, HALF, C):
+        pair_words = 2 * PASSES * N
+        quantize_w(0, 4, words_tile(2 * pair_words, "w_codes0", after="x_rows1_2"))
+        quantize_x(0, 0, MIDDLE_GROUP, words_tile(MIDDLE_GROUP, "x_codes0_0", after="x_rows1_3"))
+        quantize_w(4, 6, words_tile(pair_words, "w_codes4", after="gated0"))
+        quantize_x(1, 0, MIDDLE_GROUP)
+        for s in range(0, MIDDLE_GROUP, C):
             finish_on_scalar(s, s + C)
-        late = words_tile(HALF, "late_codes", "gated1_0")
-        quantize_w(E + 4, 2 * E, late[:, 0 : 4 * N])
-        quantize_x(0, HALF, LONG, late[:, 4 * N : HALF])
-        quantize_x(1, HALF, LONG)
-        for s in range(HALF, LONG, C):
+
+        late_codes = words_tile(pair_words + LAST_GROUP - MIDDLE_GROUP, "late_codes", after="gated1_0")
+        quantize_w(6, 8, late_codes[:, 0:pair_words])
+        quantize_x(0, MIDDLE_GROUP, LAST_GROUP, late_codes[:, pair_words:])
+        quantize_x(1, MIDDLE_GROUP, LAST_GROUP)
+        for s in range(MIDDLE_GROUP, LAST_GROUP, C):
             finish_on_scalar(s, s + C)
-        quantize_x(0, LONG, S, words_tile(S - LONG, "last_codes", "gated1_1")[:])
-        quantize_x(1, LONG, LAST_EXPERT)
+
+        quantize_x(0, LAST_GROUP, S, words_tile(S - LAST_GROUP, "last_codes", after="gated1_1"))
+        quantize_x(1, LAST_GROUP, LAST_EXPERT)
         for s0, s1 in ((LAST_EXPERT, LAST_HALF), (LAST_HALF, S)):
             quantize_x(1, s0, s1)
-        finish_on_scalar(LONG, LAST_EXPERT)
+        finish_on_scalar(LAST_GROUP, LAST_EXPERT)
         finish_on_vector(LAST_EXPERT, LAST_HALF)
         finish_on_scalar(LAST_HALF, S)
 

@@ -48,10 +48,9 @@ def tile_moe_pre_lin_relu_kernel(tc, xT, w, b, gate, offs, pos1, pos2, pos3, pos
             for g in range(PASSES)
         ]
         gates = keep.tile([P, S], F32, name="gates")
-        w_raw = keep.tile([P, E, PASSES, PACK, N], F32, name="w_raw")
+        w_raw = keep.tile([P, E, PASSES, PACK, N], F32, name="w_raw", align_bytes=MX_ALIGN)
         w_bf = keep.tile([P, E * PASSES * N * PACK], BF16, name="w_bf", align_bytes=MX_ALIGN)
         w_scales = keep.tile([P, E * PASSES * N], U8, name="w_scales", align_bytes=MX_ALIGN)
-        x_bf = keep.tile([P, PASSES, S * PACK], BF16, name="x_bf", align_bytes=MX_ALIGN)
         x_scales = keep.tile([P, PASSES, S], U8, name="x_scales", align_bytes=MX_ALIGN)
         bias = keep.tile([P, E], F32, name="bias")
         gated0 = keep.tile([P, PACK, S], F32, name="gated0", align_bytes=MX_ALIGN)
@@ -151,7 +150,8 @@ def tile_moe_pre_lin_relu_kernel(tc, xT, w, b, gate, offs, pos1, pos2, pos3, pos
             for g in range(PASSES):
                 m = e * PASSES + g
                 interleave(w_bf[:, m * N * PACK : (m + 1) * N * PACK], w_raw[:, e, g])
-        y = keep.tile([P, S], F32, name="y", tag="w_raw")
+        x_bf = keep.tile([P, PASSES, S * PACK], BF16, name="x_bf", tag="w_raw", align_bytes=MX_ALIGN)
+        y = keep.tile([P, S], F32, name="y")
 
         for s0, s1 in zip((0,) + GATE_CUTS, GATE_CUTS):
             gather_row(0, 0, s0, s1, gated0[:, 0, s0:s1])

@@ -26,8 +26,9 @@ STRIPE = 16
 MX_ALIGN = 64
 
 GATE_CUTS = (128, 256, 512, 1024, S)
-FIRST_STEP = 5 * C
-MIDDLE_GROUP = 4 * C
+HALF = S // 2
+QUARTER = S // 4
+PART = QUARTER * PACK
 LAST_GROUP = 6 * C
 LAST_EXPERT = (E - 1) * C
 LAST_HALF = LAST_EXPERT + C // 2
@@ -40,7 +41,7 @@ def tile_moe_pre_lin_relu_kernel(tc, xT, w, b, gate, offs, pos1, pos2, pos3, pos
         keep = ctx.enter_context(tc.tile_pool(name="keep", bufs=1))
         psum = ctx.enter_context(tc.psum_pool(name="psum", bufs=8))
 
-        most_slots = [[S // 2] + [S] * (PACK - 1), [FIRST_STEP] * PACK]
+        most_slots = [[S // 2] + [S] * (PACK - 1), [S, S, HALF, HALF]]
         slot_token = keep.tile([P, S // STRIPE], U16, name="slot_token")
         token_slot = [keep.tile([P, T // STRIPE], U16, name="token_slot%d" % r) for r in range(TOP)]
         x_rows = [
@@ -48,18 +49,10 @@ def tile_moe_pre_lin_relu_kernel(tc, xT, w, b, gate, offs, pos1, pos2, pos3, pos
             for g in range(PASSES)
         ]
         gates = keep.tile([P, S], F32, name="gates")
-        w_raw = keep.tile([P, E, PASSES, PACK, N], F32, name="w_raw", align_bytes=MX_ALIGN)
-        w_bf = keep.tile([P, E * PASSES * N * PACK], BF16, name="w_bf", align_bytes=MX_ALIGN)
-        w_scales = keep.tile([P, E * PASSES * N], U8, name="w_scales", align_bytes=MX_ALIGN)
-        x_scales = keep.tile([P, PASSES, S], U8, name="x_scales", align_bytes=MX_ALIGN)
+        w_raw = [keep.tile([P, PASSES, PACK, N], F32, name="w_raw%d" % e, align_bytes=MX_ALIGN) for e in range(E)]
         bias = keep.tile([P, E], F32, name="bias")
         gated0 = keep.tile([P, PACK, S], F32, name="gated0", align_bytes=MX_ALIGN)
-        gated1 = [
-            keep.tile([P, PACK, width], F32, name="gated1_%d" % step, align_bytes=MX_ALIGN)
-            for step, width in enumerate((FIRST_STEP, S - FIRST_STEP))
-        ]
-        w_codes = {}
-        x_codes = {}
+        packed = {}
 
         x_view = xT.rearrange("(g p j) t -> g j p t", g=PASSES, j=PACK)
 
@@ -71,7 +64,7 @@ def tile_moe_pre_lin_relu_kernel(tc, xT, w, b, gate, offs, pos1, pos2, pos3, pos
 
         def load_w(e):
             nc.sync.dma_start(
-                out=w_raw[:, e].rearrange("p g j n -> p g (j n)"),
+                out=w_raw[e][:].rearrange("p g j n -> p g (j n)"),
                 in_=w[e].rearrange("(g p j) n -> p g (j n)", g=PASSES, j=PACK),
             )
 
@@ -101,38 +94,31 @@ def tile_moe_pre_lin_relu_kernel(tc, xT, w, b, gate, offs, pos1, pos2, pos3, pos
             window = x_rows[g][j][:].indirect(slot_token[:, s0 // STRIPE : s1 // STRIPE])
             nc.vector.tensor_tensor(dst, window, gates[:, s0:s1], MULT)
 
-        def round_x(g, s0, s1, src):
-            interleave(x_bf[:, g, s0 * PACK : s1 * PACK], src)
+        def quantize(src, runs, name, after=None):
+            width = len(runs) * P
+            words = keep.tile([P, width], U32, name=name, tag=after or name, align_bytes=MX_ALIGN)
+            scales = keep.tile([P, width], U8, name=name + "_scales", align_bytes=MX_ALIGN)
+            nc.vector.quantize_mx(out=words[:].bitcast(FP8X4), scales=scales[:], in_=src)
+            for i, run in enumerate(runs):
+                packed[run] = (words, scales, i * P)
 
-        def words_tile(width, name, after=None):
-            return keep.tile([P, width], U32, name=name, tag=after or name, align_bytes=MX_ALIGN)[:]
+        def w_runs(e0, e1):
+            return [("w", e, g) for e in range(e0, e1) for g in range(PASSES)]
 
-        def quantize_w(e0, e1, codes):
-            m0, m1 = e0 * PASSES, e1 * PASSES
-            nc.vector.quantize_mx(
-                out=codes.bitcast(FP8X4), scales=w_scales[:, m0 * N : m1 * N], in_=w_bf[:, m0 * N * PACK : m1 * N * PACK]
-            )
-            for m in range(m0, m1):
-                w_codes[m] = codes[:, (m - m0) * N : (m - m0 + 1) * N]
-
-        def quantize_x(g, s0, s1, codes=None):
-            if codes is None:
-                codes = words_tile(s1 - s0, "x_codes%d_%d" % (g, s0))
-            nc.vector.quantize_mx(out=codes.bitcast(FP8X4), scales=x_scales[:, g, s0:s1], in_=x_bf[:, g, s0 * PACK : s1 * PACK])
-            for s in range(s0, s1, P):
-                x_codes[g, s] = (codes, s - s0)
+        def x_runs(g, s0, s1):
+            return [("x", g, s) for s in range(s0, s1, P)]
 
         def multiply(s0, s1):
             acc = psum.tile([P, s1 - s0], F32, name="acc")
             for g in range(PASSES):
-                m = s0 // C * PASSES + g
-                codes, first = x_codes[g, s0]
+                w_words, w_scales, w0 = packed["w", s0 // C, g]
+                x_words, x_scales, x0 = packed["x", g, s0]
                 nc.tensor.matmul_mx(
                     out=acc[:],
-                    lhsT=w_codes[m].bitcast(FP8X4),
-                    lhsT_scale=w_scales[:, m * N : (m + 1) * N],
-                    rhs=codes[:, first : first + s1 - s0].bitcast(FP8X4),
-                    rhs_scale=x_scales[:, g, s0:s1],
+                    lhsT=w_words[:, w0 : w0 + N].bitcast(FP8X4),
+                    lhsT_scale=w_scales[:, w0 : w0 + N],
+                    rhs=x_words[:, x0 : x0 + s1 - s0].bitcast(FP8X4),
+                    rhs_scale=x_scales[:, x0 : x0 + s1 - s0],
                     start=(g == 0),
                     stop=(g == PASSES - 1),
                 )
@@ -146,50 +132,62 @@ def tile_moe_pre_lin_relu_kernel(tc, xT, w, b, gate, offs, pos1, pos2, pos3, pos
             e = s0 // C
             nc.vector.tensor_scalar(out=y[:, s0:s1], in0=multiply(s0, s1)[:], scalar1=bias[:, e : e + 1], scalar2=0.0, op0=ADD, op1=MAX)
 
+        with_w = keep.tile([P, 6 * PART], BF16, name="with_w", align_bytes=MX_ALIGN)
+        w_part = (0, 1, 3, 5)
         for e in range(E):
             for g in range(PASSES):
-                m = e * PASSES + g
-                interleave(w_bf[:, m * N * PACK : (m + 1) * N * PACK], w_raw[:, e, g])
-        x_bf = keep.tile([P, PASSES, S * PACK], BF16, name="x_bf", tag="w_raw", align_bytes=MX_ALIGN)
-        y = keep.tile([P, S], F32, name="y")
+                first = w_part[e // 2] * PART + (e % 2 * PASSES + g) * N * PACK
+                interleave(with_w[:, first : first + N * PACK], w_raw[e][:, g])
+        x_only = keep.tile([P, 6 * PART], BF16, name="x_only", tag="w_raw7", align_bytes=MX_ALIGN)
+        gated1 = keep.tile([P, 6 * S], F32, name="gated1", tag="w_raw6", align_bytes=MX_ALIGN)
+        y = keep.tile([P, S], F32, name="y", tag="gated0", align_bytes=MX_ALIGN)
+
+        def part(tile, i, count=1):
+            return tile[:, i * PART : (i + count) * PART]
 
         for s0, s1 in zip((0,) + GATE_CUTS, GATE_CUTS):
             gather_row(0, 0, s0, s1, gated0[:, 0, s0:s1])
         for j in range(1, PACK):
             gather_row(0, j, 0, S, gated0[:, j, :])
-        round_x(0, 0, S, gated0[:])
+        interleave(part(x_only, 0, 2), gated0[:, :, 0:HALF])
+        interleave(part(x_only, 3, 2), gated0[:, :, HALF:S])
 
-        for step, (s0, s1) in enumerate(((0, FIRST_STEP), (FIRST_STEP, S))):
-            for j in range(PACK):
-                gather_row(1, j, s0, s1, gated1[step][:, j, :])
-            round_x(1, s0, s1, gated1[step][:])
+        late = 3 * S + HALF
+        for j in range(2):
+            gather_row(1, j, 0, S, gated1[:, j * S : (j + 1) * S])
+        for j in range(2, PACK):
+            gather_row(1, j, 0, HALF, gated1[:, j * S : j * S + HALF])
+        early_rows = gated1[:, 0 : PACK * S].rearrange("p (j s) -> p j s", j=PACK)
+        interleave(part(with_w, 2), early_rows[:, :, 0:QUARTER])
+        interleave(part(x_only, 2), early_rows[:, :, QUARTER:HALF])
+        for j in range(2, PACK):
+            gather_row(1, j, HALF, S, gated1[:, late + (j - 2) * S : late + (j - 2) * S + HALF])
+        for s0, dst in ((HALF, part(with_w, 4)), (HALF + QUARTER, part(x_only, 5))):
+            src = gated1[:].rearrange("p (u j c i) -> p c u j i", u=2, j=3, i=PACK)[:, s0 // PACK : (s0 + QUARTER) // PACK, :, 0:2, :]
+            nc.scalar.copy(out=dst.rearrange("p (c i u j) -> p c u j i", i=PACK, u=2, j=2), in_=src)
 
-        pair_words = 2 * PASSES * N
-        quantize_w(0, 4, words_tile(2 * pair_words, "w_codes0", after="x_rows1_2"))
-        quantize_x(0, 0, MIDDLE_GROUP, words_tile(MIDDLE_GROUP, "x_codes0_0", after="x_rows1_3"))
-        quantize_w(4, 6, words_tile(pair_words, "w_codes4", after="gated0"))
-        quantize_x(1, 0, MIDDLE_GROUP)
-        for s in range(0, MIDDLE_GROUP, C):
+        quantize(part(with_w, 0, 2), w_runs(0, 4), "packed0", after="x_rows1_2")
+        quantize(part(x_only, 0, 2), x_runs(0, 0, HALF), "packed1", after="x_rows1_3")
+        quantize(part(with_w, 2, 2), x_runs(1, 0, QUARTER) + w_runs(4, 6), "packed2")
+        for s in range(0, QUARTER, C):
             finish_on_scalar(s, s + C)
-
-        late_codes = words_tile(pair_words + LAST_GROUP - MIDDLE_GROUP, "late_codes", after="gated1_0")
-        quantize_w(6, 8, late_codes[:, 0:pair_words])
-        quantize_x(0, MIDDLE_GROUP, LAST_GROUP, late_codes[:, pair_words:])
-        quantize_x(1, MIDDLE_GROUP, LAST_GROUP)
-        for s in range(MIDDLE_GROUP, LAST_GROUP, C):
+        quantize(part(x_only, 2, 2), x_runs(1, QUARTER, HALF) + x_runs(0, HALF, LAST_GROUP), "packed3")
+        for s in range(QUARTER, HALF, C):
             finish_on_scalar(s, s + C)
-
-        quantize_x(0, LAST_GROUP, S, words_tile(S - LAST_GROUP, "last_codes", after="gated1_1"))
-        quantize_x(1, LAST_GROUP, LAST_EXPERT)
-        for s0, s1 in ((LAST_EXPERT, LAST_HALF), (LAST_HALF, S)):
-            quantize_x(1, s0, s1)
+        quantize(part(with_w, 4, 2), x_runs(1, HALF, LAST_GROUP) + w_runs(6, 8), "packed4")
+        for s in range(HALF, LAST_GROUP, C):
+            finish_on_scalar(s, s + C)
+        quantize(part(x_only, 4), x_runs(0, LAST_GROUP, S), "packed5", after="w_raw6")
+        for s0, s1 in ((LAST_GROUP, LAST_EXPERT), (LAST_EXPERT, LAST_HALF), (LAST_HALF, S)):
+            first = 5 * PART + (s0 - LAST_GROUP) * PACK
+            quantize(x_only[:, first : first + (s1 - s0) * PACK], x_runs(1, s0, s1), "packed_last%d" % s0)
         finish_on_scalar(LAST_GROUP, LAST_EXPERT)
         finish_on_vector(LAST_EXPERT, LAST_HALF)
         finish_on_scalar(LAST_HALF, S)
 
         halves = [slice(0, T // 2), slice(T // 2, T)]
         last_parts = [halves[0], slice(T // 2, T - LAST_TOKENS), slice(T - LAST_TOKENS, T)]
-        sums = [keep.tile([P, T], F32, name="sum%d" % r) for r in range(TOP)]
+        sums = [keep.tile([P, T], F32, name="sum%d" % r, tag="x_rows0_%d" % r, align_bytes=MX_ALIGN) for r in range(TOP)]
 
         def results(r, part):
             return y[:].indirect(token_slot[r][:, part.start // STRIPE : part.stop // STRIPE])

@@ -25,7 +25,7 @@ PASSES = K // (P * PACK)
 STRIPE = 16
 MX_ALIGN = 64
 
-GATE_CUTS = (128, 256, 512, 1024, S)
+GATE_CUTS = (128, 256, 512, 1024)
 HALF = S // 2
 QUARTER = S // 4
 PART = QUARTER * PACK
@@ -41,7 +41,7 @@ def tile_moe_pre_lin_relu_kernel(tc, xT, w, b, gate, offs, pos1, pos2, pos3, pos
         keep = ctx.enter_context(tc.tile_pool(name="keep", bufs=1))
         psum = ctx.enter_context(tc.psum_pool(name="psum", bufs=8))
 
-        most_slots = [[S // 2] + [S] * (PACK - 1), [S, S, HALF, HALF]]
+        most_slots = [[S] * PACK, [S, S, HALF, HALF]]
         slot_token = keep.tile([P, S // STRIPE], U16, name="slot_token")
         token_slot = [keep.tile([P, T // STRIPE], U16, name="token_slot%d" % r) for r in range(TOP)]
         x_rows = [
@@ -68,20 +68,19 @@ def tile_moe_pre_lin_relu_kernel(tc, xT, w, b, gate, offs, pos1, pos2, pos3, pos
                 in_=w[e].rearrange("(g p j) n -> p g (j n)", g=PASSES, j=PACK),
             )
 
-        load_x(0, 0)
+        load_x(1, 2)
         load_gate(0, GATE_CUTS[0])
         nc.sync.dma_start(slot_token[:], offs)
         for s0, s1 in zip(GATE_CUTS, GATE_CUTS[1:]):
             load_gate(s0, s1)
-        for j in range(1, PACK):
-            load_x(0, j)
-            load_w(j - 1)
-        load_w(PACK - 1)
-        for j in range(PACK):
-            load_x(1, j)
-        nc.sync.dma_start(out=bias[:], in_=b)
-        for e in range(PACK, E):
+        load_x(1, 3)
+        load_x(0, 0)
+        load_gate(HALF, S)
+        for g, j in ((0, 1), (0, 2), (0, 3), (1, 0), (1, 1)):
+            load_x(g, j)
+        for e in range(E):
             load_w(e)
+        nc.sync.dma_start(out=bias[:], in_=b)
         for r, pos in enumerate((pos1, pos2, pos3, pos4)):
             nc.sync.dma_start(token_slot[r][:], pos)
 
@@ -132,55 +131,55 @@ def tile_moe_pre_lin_relu_kernel(tc, xT, w, b, gate, offs, pos1, pos2, pos3, pos
             e = s0 // C
             nc.vector.tensor_scalar(out=y[:, s0:s1], in0=multiply(s0, s1)[:], scalar1=bias[:, e : e + 1], scalar2=0.0, op0=ADD, op1=MAX)
 
-        with_w = keep.tile([P, 6 * PART], BF16, name="with_w", align_bytes=MX_ALIGN)
-        w_part = (0, 1, 3, 5)
+        w_bf = keep.tile([P, 4 * PART], BF16, name="w_bf", align_bytes=MX_ALIGN)
         for e in range(E):
             for g in range(PASSES):
-                first = w_part[e // 2] * PART + (e % 2 * PASSES + g) * N * PACK
-                interleave(with_w[:, first : first + N * PACK], w_raw[e][:, g])
-        x_only = keep.tile([P, 6 * PART], BF16, name="x_only", tag="w_raw7", align_bytes=MX_ALIGN)
-        gated1 = keep.tile([P, 6 * S], F32, name="gated1", tag="w_raw6", align_bytes=MX_ALIGN)
-        y = keep.tile([P, S], F32, name="y", tag="gated0", align_bytes=MX_ALIGN)
+                first = (e * PASSES + g) * N * PACK
+                interleave(w_bf[:, first : first + N * PACK], w_raw[e][:, g])
+        x_bf = keep.tile([P, 8 * PART], BF16, name="x_bf", tag="w_raw7", align_bytes=MX_ALIGN)
+        gated1 = keep.tile([P, 6 * S], F32, name="gated1", align_bytes=MX_ALIGN)
 
         def part(tile, i, count=1):
             return tile[:, i * PART : (i + count) * PART]
 
         for s0, s1 in zip((0,) + GATE_CUTS, GATE_CUTS):
-            gather_row(0, 0, s0, s1, gated0[:, 0, s0:s1])
-        for j in range(1, PACK):
+            gather_row(1, 2, s0, s1, gated1[:, 2 * S + s0 : 2 * S + s1])
+        gather_row(1, 3, 0, HALF, gated1[:, 3 * S : 3 * S + HALF])
+        for j in range(PACK):
             gather_row(0, j, 0, S, gated0[:, j, :])
-        interleave(part(x_only, 0, 2), gated0[:, :, 0:HALF])
-        interleave(part(x_only, 3, 2), gated0[:, :, HALF:S])
+        interleave(part(x_bf, 0, 2), gated0[:, :, 0:HALF])
+        interleave(part(x_bf, 3), gated0[:, :, HALF : HALF + QUARTER])
+        interleave(part(x_bf, 5), gated0[:, :, HALF + QUARTER : S])
 
         late = 3 * S + HALF
         for j in range(2):
             gather_row(1, j, 0, S, gated1[:, j * S : (j + 1) * S])
-        for j in range(2, PACK):
-            gather_row(1, j, 0, HALF, gated1[:, j * S : j * S + HALF])
         early_rows = gated1[:, 0 : PACK * S].rearrange("p (j s) -> p j s", j=PACK)
-        interleave(part(with_w, 2), early_rows[:, :, 0:QUARTER])
-        interleave(part(x_only, 2), early_rows[:, :, QUARTER:HALF])
+        interleave(part(x_bf, 2), early_rows[:, :, 0:QUARTER])
+        interleave(part(x_bf, 4), early_rows[:, :, QUARTER:HALF])
         for j in range(2, PACK):
             gather_row(1, j, HALF, S, gated1[:, late + (j - 2) * S : late + (j - 2) * S + HALF])
-        for s0, dst in ((HALF, part(with_w, 4)), (HALF + QUARTER, part(x_only, 5))):
+        for s0, dst in ((HALF, part(x_bf, 6)), (HALF + QUARTER, part(x_bf, 7))):
             src = gated1[:].rearrange("p (u j c i) -> p c u j i", u=2, j=3, i=PACK)[:, s0 // PACK : (s0 + QUARTER) // PACK, :, 0:2, :]
             nc.scalar.copy(out=dst.rearrange("p (c i u j) -> p c u j i", i=PACK, u=2, j=2), in_=src)
 
-        quantize(part(with_w, 0, 2), w_runs(0, 4), "packed0", after="x_rows1_2")
-        quantize(part(x_only, 0, 2), x_runs(0, 0, HALF), "packed1", after="x_rows1_3")
-        quantize(part(with_w, 2, 2), x_runs(1, 0, QUARTER) + w_runs(4, 6), "packed2")
+        y = keep.tile([P, S], F32, name="y", tag="gates")
+        quantize(part(w_bf, 0, 2), w_runs(0, 4), "packed0", after="x_rows1_2")
+        quantize(part(x_bf, 0, 2), x_runs(0, 0, HALF), "packed1", after="x_rows1_3")
+        quantize(part(w_bf, 2), w_runs(4, 6), "packed2", after="gated0")
+        quantize(part(x_bf, 2, 2), x_runs(1, 0, QUARTER) + x_runs(0, HALF, LAST_GROUP), "packed3", after="w_raw0")
         for s in range(0, QUARTER, C):
             finish_on_scalar(s, s + C)
-        quantize(part(x_only, 2, 2), x_runs(1, QUARTER, HALF) + x_runs(0, HALF, LAST_GROUP), "packed3")
+        quantize(part(x_bf, 4, 2), x_runs(1, QUARTER, HALF) + x_runs(0, LAST_GROUP, S), "packed4", after="w_raw1")
         for s in range(QUARTER, HALF, C):
             finish_on_scalar(s, s + C)
-        quantize(part(with_w, 4, 2), x_runs(1, HALF, LAST_GROUP) + w_runs(6, 8), "packed4")
+        quantize(part(x_bf, 6), x_runs(1, HALF, LAST_GROUP), "packed5", after="w_raw2")
         for s in range(HALF, LAST_GROUP, C):
             finish_on_scalar(s, s + C)
-        quantize(part(x_only, 4), x_runs(0, LAST_GROUP, S), "packed5", after="w_raw6")
+        quantize(part(w_bf, 3), w_runs(6, 8), "packed6", after="gated1")
         for s0, s1 in ((LAST_GROUP, LAST_EXPERT), (LAST_EXPERT, LAST_HALF), (LAST_HALF, S)):
-            first = 5 * PART + (s0 - LAST_GROUP) * PACK
-            quantize(x_only[:, first : first + (s1 - s0) * PACK], x_runs(1, s0, s1), "packed_last%d" % s0)
+            first = 7 * PART + (s0 - LAST_GROUP) * PACK
+            quantize(x_bf[:, first : first + (s1 - s0) * PACK], x_runs(1, s0, s1), "packed_last%d" % s0)
         finish_on_scalar(LAST_GROUP, LAST_EXPERT)
         finish_on_vector(LAST_EXPERT, LAST_HALF)
         finish_on_scalar(LAST_HALF, S)

@@ -74,15 +74,15 @@ def tile_moe_pre_lin_relu_kernel(tc, xT, w, b, gate, offs, pos1, pos2, pos3, pos
         for s0, s1 in zip(GATE_CUTS, GATE_CUTS[1:]):
             load_gate(s0, s1)
         load_x(1, 3)
+        nc.sync.dma_start(out=bias[:], in_=b)
+        for r, pos in enumerate((pos1, pos2, pos3, pos4)):
+            nc.sync.dma_start(token_slot[r][:], pos)
         load_x(0, 0)
         load_gate(HALF, S)
         for g, j in ((0, 1), (0, 2), (0, 3), (1, 0), (1, 1)):
             load_x(g, j)
         for e in range(E):
             load_w(e)
-        nc.sync.dma_start(out=bias[:], in_=b)
-        for r, pos in enumerate((pos1, pos2, pos3, pos4)):
-            nc.sync.dma_start(token_slot[r][:], pos)
 
         def interleave(dst, src):
             nc.scalar.copy(
@@ -180,8 +180,8 @@ def tile_moe_pre_lin_relu_kernel(tc, xT, w, b, gate, offs, pos1, pos2, pos3, pos
         for s0, s1 in ((LAST_GROUP, LAST_EXPERT), (LAST_EXPERT, LAST_HALF), (LAST_HALF, S)):
             first = 7 * PART + (s0 - LAST_GROUP) * PACK
             quantize(x_bf[:, first : first + (s1 - s0) * PACK], x_runs(1, s0, s1), "packed_last%d" % s0)
-        finish_on_scalar(LAST_GROUP, LAST_EXPERT)
-        finish_on_vector(LAST_EXPERT, LAST_HALF)
+        finish_on_vector(LAST_GROUP, LAST_EXPERT)
+        finish_on_scalar(LAST_EXPERT, LAST_HALF)
         finish_on_scalar(LAST_HALF, S)
 
         halves = [slice(0, T // 2), slice(T // 2, T)]

@@ -27,6 +27,7 @@ MX_ALIGN = 64
 
 GATE_CUTS = (128, 256, 512, 1024)
 HALF = S // 2
+RUN = 2
 QUARTER = S // 4
 PART = QUARTER * PACK
 LAST_GROUP = 6 * C
@@ -86,7 +87,7 @@ def tile_moe_pre_lin_relu_kernel(tc, xT, w, b, gate, offs, pos1, pos2, pos3, pos
 
         def interleave(dst, src):
             nc.scalar.copy(
-                out=dst.rearrange("p (c i j) -> p c j i", i=PACK, j=PACK), in_=src.rearrange("p j (c i) -> p c j i", i=PACK)
+                out=dst.rearrange("p (c i j) -> p c j i", i=RUN, j=PACK), in_=src.rearrange("p j (c i) -> p c j i", i=RUN)
             )
 
         def gather_row(g, j, s0, s1, dst):
@@ -160,8 +161,8 @@ def tile_moe_pre_lin_relu_kernel(tc, xT, w, b, gate, offs, pos1, pos2, pos3, pos
         for j in range(2, PACK):
             gather_row(1, j, HALF, S, gated1[:, late + (j - 2) * S : late + (j - 2) * S + HALF])
         for s0, dst in ((HALF, part(x_bf, 6)), (HALF + QUARTER, part(x_bf, 7))):
-            src = gated1[:].rearrange("p (u j c i) -> p c u j i", u=2, j=3, i=PACK)[:, s0 // PACK : (s0 + QUARTER) // PACK, :, 0:2, :]
-            nc.scalar.copy(out=dst.rearrange("p (c i u j) -> p c u j i", i=PACK, u=2, j=2), in_=src)
+            src = gated1[:].rearrange("p (u j c i) -> p c u j i", u=2, j=3, i=RUN)[:, s0 // RUN : (s0 + QUARTER) // RUN, :, 0:2, :]
+            nc.scalar.copy(out=dst.rearrange("p (c i u j) -> p c u j i", i=RUN, u=2, j=2), in_=src)
 
         y = keep.tile([P, S], F32, name="y", tag="gates")
         quantize(part(w_bf, 0, 2), w_runs(0, 4), "packed0", after="x_rows1_2")

@@ -40,19 +40,25 @@ def tile_moe_pre_lin_relu_kernel(tc, xT, w, b, gate, offs, pos1, pos2, pos3, pos
     nc = tc.nc
     with ExitStack() as ctx:
         keep = ctx.enter_context(tc.tile_pool(name="keep", bufs=1))
+        pass1 = ctx.enter_context(tc.tile_pool(name="pass1", bufs=1))
+        w_pool = ctx.enter_context(tc.tile_pool(name="w_pool", bufs=1))
+        raw = ctx.enter_context(tc.tile_pool(name="raw", bufs=1))
+        last_raw = ctx.enter_context(tc.tile_pool(name="last_raw", bufs=1))
+        pass0 = ctx.enter_context(tc.tile_pool(name="pass0", bufs=1))
+        small = ctx.enter_context(tc.tile_pool(name="small", bufs=1))
         psum = ctx.enter_context(tc.psum_pool(name="psum", bufs=8))
 
         most_slots = [[S] * PACK, [S, S, HALF, HALF]]
         slot_token = keep.tile([P, S // STRIPE], U16, name="slot_token")
         token_slot = [keep.tile([P, T // STRIPE], U16, name="token_slot%d" % r) for r in range(TOP)]
-        x_rows = [
-            [keep.tile([P, most_slots[g][j] + STRIPE], F32, name="x_rows%d_%d" % (g, j), align_bytes=MX_ALIGN) for j in range(PACK)]
-            for g in range(PASSES)
-        ]
         gates = keep.tile([P, S], F32, name="gates")
-        w_raw = [keep.tile([P, PASSES, PACK, N], F32, name="w_raw%d" % e, align_bytes=MX_ALIGN) for e in range(E)]
+        x_rows = [[None] * PACK for g in range(PASSES)]
+        for g in (1, 0):
+            for j in (2, 3, 0, 1):
+                x_rows[g][j] = keep.tile([P, most_slots[g][j] + STRIPE], F32, name="x_rows%d_%d" % (g, j), align_bytes=MX_ALIGN)
+        w_raw = [(raw if e < E - 1 else last_raw).tile([P, PASSES, PACK, N], F32, name="w_raw%d" % e, align_bytes=MX_ALIGN) for e in range(E)]
         bias = keep.tile([P, E], F32, name="bias")
-        gated0 = keep.tile([P, PACK, S], F32, name="gated0", align_bytes=MX_ALIGN)
+        gated0 = pass0.tile([P, PACK, S], F32, name="gated0", align_bytes=MX_ALIGN)
         packed = {}
 
         x_view = xT.rearrange("(g p j) t -> g j p t", g=PASSES, j=PACK)
@@ -94,10 +100,10 @@ def tile_moe_pre_lin_relu_kernel(tc, xT, w, b, gate, offs, pos1, pos2, pos3, pos
             window = x_rows[g][j][:].indirect(slot_token[:, s0 // STRIPE : s1 // STRIPE])
             nc.vector.tensor_tensor(dst, window, gates[:, s0:s1], MULT)
 
-        def quantize(src, runs, name, after=None):
+        def quantize(src, runs, name, pool=small, after=None):
             width = len(runs) * P
-            words = keep.tile([P, width], U32, name=name, tag=after or name, align_bytes=MX_ALIGN)
-            scales = keep.tile([P, width], U8, name=name + "_scales", align_bytes=MX_ALIGN)
+            words = pool.tile([P, width], U32, name=name, tag=after or name, align_bytes=MX_ALIGN)
+            scales = small.tile([P, width], U8, name=name + "_scales", align_bytes=MX_ALIGN)
             nc.vector.quantize_mx(out=words[:].bitcast(FP8X4), scales=scales[:], in_=src)
             for i, run in enumerate(runs):
                 packed[run] = (words, scales, i * P)
@@ -132,13 +138,13 @@ def tile_moe_pre_lin_relu_kernel(tc, xT, w, b, gate, offs, pos1, pos2, pos3, pos
             e = s0 // C
             nc.vector.tensor_scalar(out=y[:, s0:s1], in0=multiply(s0, s1)[:], scalar1=bias[:, e : e + 1], scalar2=0.0, op0=ADD, op1=MAX)
 
-        w_bf = keep.tile([P, 4 * PART], BF16, name="w_bf", align_bytes=MX_ALIGN)
+        w_bf = w_pool.tile([P, 4 * PART], BF16, name="w_bf", align_bytes=MX_ALIGN)
         for e in range(E):
             for g in range(PASSES):
                 first = (e * PASSES + g) * N * PACK
                 interleave(w_bf[:, first : first + N * PACK], w_raw[e][:, g])
-        x_bf = keep.tile([P, 8 * PART], BF16, name="x_bf", tag="w_raw7", align_bytes=MX_ALIGN)
-        gated1 = keep.tile([P, 6 * S], F32, name="gated1", align_bytes=MX_ALIGN)
+        x_bf = last_raw.tile([P, 8 * PART], BF16, name="x_bf", tag="w_raw7", align_bytes=MX_ALIGN)
+        gated1 = pass1.tile([P, 6 * S], F32, name="gated1", align_bytes=MX_ALIGN)
 
         def part(tile, i, count=1):
             return tile[:, i * PART : (i + count) * PART]
@@ -165,19 +171,19 @@ def tile_moe_pre_lin_relu_kernel(tc, xT, w, b, gate, offs, pos1, pos2, pos3, pos
             nc.scalar.copy(out=dst.rearrange("p (c i u j) -> p c u j i", i=RUN, u=2, j=2), in_=src)
 
         y = keep.tile([P, S], F32, name="y", tag="gates")
-        quantize(part(w_bf, 0, 2), w_runs(0, 4), "packed0", after="x_rows1_2")
-        quantize(part(x_bf, 0, 2), x_runs(0, 0, HALF), "packed1", after="x_rows1_3")
-        quantize(part(w_bf, 2), w_runs(4, 6), "packed2", after="gated0")
-        quantize(part(x_bf, 2, 2), x_runs(1, 0, QUARTER) + x_runs(0, HALF, LAST_GROUP), "packed3", after="w_raw0")
+        quantize(part(w_bf, 0, 2), w_runs(0, 4), "packed0", pool=keep, after="x_rows1_2")
+        quantize(part(x_bf, 0, 2), x_runs(0, 0, HALF), "packed1", pool=keep, after="x_rows1_3")
+        quantize(part(w_bf, 2), w_runs(4, 6), "packed2", pool=pass0, after="gated0")
+        quantize(part(x_bf, 2, 2), x_runs(1, 0, QUARTER) + x_runs(0, HALF, LAST_GROUP), "packed3", pool=raw, after="w_raw0")
         for s in range(0, QUARTER, C):
             finish_on_scalar(s, s + C)
-        quantize(part(x_bf, 4, 2), x_runs(1, QUARTER, HALF) + x_runs(0, LAST_GROUP, S), "packed4", after="w_raw1")
+        quantize(part(x_bf, 4, 2), x_runs(1, QUARTER, HALF) + x_runs(0, LAST_GROUP, S), "packed4", pool=raw, after="w_raw1")
         for s in range(QUARTER, HALF, C):
             finish_on_scalar(s, s + C)
-        quantize(part(x_bf, 6), x_runs(1, HALF, LAST_GROUP), "packed5", after="w_raw2")
+        quantize(part(x_bf, 6), x_runs(1, HALF, LAST_GROUP), "packed5", pool=raw, after="w_raw2")
         for s in range(HALF, LAST_GROUP, C):
             finish_on_scalar(s, s + C)
-        quantize(part(w_bf, 3), w_runs(6, 8), "packed6", after="gated1")
+        quantize(part(w_bf, 3), w_runs(6, 8), "packed6", pool=pass1, after="gated1")
         for s0, s1 in ((LAST_GROUP, LAST_EXPERT), (LAST_EXPERT, LAST_HALF), (LAST_HALF, S)):
             first = 7 * PART + (s0 - LAST_GROUP) * PACK
             quantize(x_bf[:, first : first + (s1 - s0) * PACK], x_runs(1, s0, s1), "packed_last%d" % s0)

@@ -16,7 +16,7 @@ U8 = mybir.dt.uint8
 FP8X4 = mybir.dt.float8_e4m3fn_x4
 MULT = mybir.AluOpType.mult
 ADD = mybir.AluOpType.add
-MAX = mybir.AluOpType.max
+COPY = mybir.ActivationFunctionType.Copy
 RELU = mybir.ActivationFunctionType.Relu
 
 P = 128
@@ -24,41 +24,31 @@ PACK = 4
 PASSES = K // (P * PACK)
 STRIPE = 16
 MX_ALIGN = 64
-
-GATE_CUTS = (128, 256, 512, 1024)
-HALF = S // 2
 RUN = 2
+HALF = S // 2
 QUARTER = S // 4
-PART = QUARTER * PACK
-LAST_GROUP = 6 * C
-LAST_EXPERT = (E - 1) * C
-LAST_HALF = LAST_EXPERT + C // 2
-LAST_TOKENS = 128
+WINDOW = HALF + STRIPE
+FIRST_GATE = 128
 
 
 def tile_moe_pre_lin_relu_kernel(tc, xT, w, b, gate, offs, pos1, pos2, pos3, pos4, out):
     nc = tc.nc
     with ExitStack() as ctx:
         keep = ctx.enter_context(tc.tile_pool(name="keep", bufs=1))
-        pass1 = ctx.enter_context(tc.tile_pool(name="pass1", bufs=1))
-        w_pool = ctx.enter_context(tc.tile_pool(name="w_pool", bufs=1))
-        raw = ctx.enter_context(tc.tile_pool(name="raw", bufs=1))
-        last_raw = ctx.enter_context(tc.tile_pool(name="last_raw", bufs=1))
-        pass0 = ctx.enter_context(tc.tile_pool(name="pass0", bufs=1))
-        small = ctx.enter_context(tc.tile_pool(name="small", bufs=1))
         psum = ctx.enter_context(tc.psum_pool(name="psum", bufs=8))
 
-        most_slots = [[S] * PACK, [S, S, HALF, HALF]]
         slot_token = keep.tile([P, S // STRIPE], U16, name="slot_token")
         token_slot = [keep.tile([P, T // STRIPE], U16, name="token_slot%d" % r) for r in range(TOP)]
         gates = keep.tile([P, S], F32, name="gates")
-        x_rows = [[None] * PACK for g in range(PASSES)]
-        for g in (1, 0):
-            for j in (2, 3, 0, 1):
-                x_rows[g][j] = keep.tile([P, most_slots[g][j] + STRIPE], F32, name="x_rows%d_%d" % (g, j), align_bytes=MX_ALIGN)
-        w_raw = [(raw if e < E - 1 else last_raw).tile([P, PASSES, PACK, N], F32, name="w_raw%d" % e, align_bytes=MX_ALIGN) for e in range(E)]
+        x_rows = [
+            [keep.tile([P, WINDOW], F32, name="x_rows%d_%d" % (g, j), align_bytes=MX_ALIGN) for j in range(PACK)]
+            for g in range(PASSES)
+        ]
+        w_raw = keep.tile([P, E * PASSES, PACK, N], F32, name="w_raw", align_bytes=MX_ALIGN)
         bias = keep.tile([P, E], F32, name="bias")
-        gated0 = pass0.tile([P, PACK, S], F32, name="gated0", align_bytes=MX_ALIGN)
+        w_bf = keep.tile([P, E * PASSES * N * PACK], BF16, name="w_bf", align_bytes=MX_ALIGN)
+        x_bf = [keep.tile([P, S * PACK], BF16, name="x_bf%d" % g, align_bytes=MX_ALIGN) for g in range(PASSES)]
+        y = keep.tile([P, S], F32, name="y")
         packed = {}
 
         x_view = xT.rearrange("(g p j) t -> g j p t", g=PASSES, j=PACK)
@@ -71,53 +61,88 @@ def tile_moe_pre_lin_relu_kernel(tc, xT, w, b, gate, offs, pos1, pos2, pos3, pos
 
         def load_w(e):
             nc.sync.dma_start(
-                out=w_raw[e][:].rearrange("p g j n -> p g (j n)"),
+                out=w_raw[:, e * PASSES : (e + 1) * PASSES].rearrange("p g j n -> p g (j n)"),
                 in_=w[e].rearrange("(g p j) n -> p g (j n)", g=PASSES, j=PACK),
             )
 
-        load_x(1, 2)
-        load_gate(0, GATE_CUTS[0])
+        load_x(0, 0)
         nc.sync.dma_start(slot_token[:], offs)
-        for s0, s1 in zip(GATE_CUTS, GATE_CUTS[1:]):
-            load_gate(s0, s1)
-        load_x(1, 3)
+        load_gate(0, FIRST_GATE)
+        load_gate(FIRST_GATE, QUARTER)
+        for j in range(1, PACK):
+            load_x(0, j)
+        load_gate(QUARTER, HALF)
         nc.sync.dma_start(out=bias[:], in_=b)
         for r, pos in enumerate((pos1, pos2, pos3, pos4)):
             nc.sync.dma_start(token_slot[r][:], pos)
-        load_x(0, 0)
-        load_gate(HALF, S)
-        for g, j in ((0, 1), (0, 2), (0, 3), (1, 0), (1, 1)):
-            load_x(g, j)
-        for e in range(E):
+        for e in range(E // 2):
+            load_w(e)
+        load_gate(S - P, S)
+        for j in range(PACK):
+            load_x(1, j)
+        load_gate(HALF, S - P)
+        for e in range(E // 2, E):
             load_w(e)
 
-        def interleave(dst, src):
-            nc.scalar.copy(
-                out=dst.rearrange("p (c i j) -> p c j i", i=RUN, j=PACK), in_=src.rearrange("p j (c i) -> p c j i", i=RUN)
+        def tokens(g, j, s0, s1):
+            return x_rows[g][j][:].indirect(slot_token[:, s0 // STRIPE : s1 // STRIPE])
+
+        def words(dst):
+            return dst.rearrange("p (c i j) -> p c j i", i=RUN, j=PACK)
+
+        def rows(src):
+            return src.rearrange("p j (c i) -> p c j i", i=RUN)
+
+        def gather_on_scalar(g, s0, s1):
+            raw = keep.tile([P, PACK, s1 - s0], F32, name="raw%d_%d" % (g, s0), align_bytes=MX_ALIGN)
+            for j in range(PACK):
+                nc.scalar.activation(raw[:, j, :], tokens(g, j, s0, s1), COPY)
+            return raw
+
+        def gate_and_round(g, s0, s1, raw):
+            n = (s1 - s0) // RUN
+            spread = gates[:, s0:s1].rearrange("p (c i) -> p c i", i=RUN).unsqueeze(2).to_broadcast([P, n, PACK, RUN])
+            nc.vector.tensor_tensor(words(x_bf[g][:, s0 * PACK : s1 * PACK]), rows(raw), spread, MULT)
+
+        def gather_on_vector(g, s0, s1, first_cuts=()):
+            gated = keep.tile([P, PACK, s1 - s0], F32, name="gated%d_%d" % (g, s0), align_bytes=MX_ALIGN)
+            for j in range(PACK):
+                cuts = (s0,) + (first_cuts if j == 0 else ()) + (s1,)
+                for a, z in zip(cuts, cuts[1:]):
+                    nc.vector.tensor_tensor(gated[:, j, a - s0 : z - s0], tokens(g, j, a, z), gates[:, a:z], MULT)
+            return gated
+
+        def round_x(g, s0, s1, gated):
+            nc.vector.tensor_copy(words(x_bf[g][:, s0 * PACK : s1 * PACK]), rows(gated[:]))
+
+        def round_w(e0, e1):
+            dst = w_bf[:, e0 * PASSES * N * PACK : e1 * PASSES * N * PACK]
+            nc.vector.tensor_copy(
+                dst.rearrange("p (m c i j) -> p m c j i", i=RUN, j=PACK, c=N // RUN),
+                w_raw[:, e0 * PASSES : e1 * PASSES].rearrange("p m j (c i) -> p m c j i", i=RUN),
             )
 
-        def gather_row(g, j, s0, s1, dst):
-            window = x_rows[g][j][:].indirect(slot_token[:, s0 // STRIPE : s1 // STRIPE])
-            nc.vector.tensor_tensor(dst, window, gates[:, s0:s1], MULT)
-
-        def quantize(src, runs, name, pool=small, after=None):
+        def quantize(src, runs, name):
             width = len(runs) * P
-            words = pool.tile([P, width], U32, name=name, tag=after or name, align_bytes=MX_ALIGN)
-            scales = small.tile([P, width], U8, name=name + "_scales", align_bytes=MX_ALIGN)
-            nc.vector.quantize_mx(out=words[:].bitcast(FP8X4), scales=scales[:], in_=src)
+            codes = keep.tile([P, width], U32, name=name, align_bytes=MX_ALIGN)
+            scales = keep.tile([P, width], U8, name=name + "_scales", align_bytes=MX_ALIGN)
+            nc.vector.quantize_mx(out=codes[:].bitcast(FP8X4), scales=scales[:], in_=src)
             for i, run in enumerate(runs):
-                packed[run] = (words, scales, i * P)
+                packed[run] = (codes, scales, i * P)
 
-        def w_runs(e0, e1):
-            return [("w", e, g) for e in range(e0, e1) for g in range(PASSES)]
+        def quantize_w(e0, e1):
+            runs = [("w", e, g) for e in range(e0, e1) for g in range(PASSES)]
+            quantize(w_bf[:, e0 * PASSES * N * PACK : e1 * PASSES * N * PACK], runs, "w_packed%d" % e0)
 
-        def x_runs(g, s0, s1):
-            return [("x", g, s) for s in range(s0, s1, P)]
+        def quantize_x(g, s0, s1):
+            runs = [("x", g, s) for s in range(s0, s1, P)]
+            quantize(x_bf[g][:, s0 * PACK : s1 * PACK], runs, "x_packed%d_%d" % (g, s0))
 
-        def multiply(s0, s1):
+        def finish(s0, s1):
+            e = s0 // C
             acc = psum.tile([P, s1 - s0], F32, name="acc")
             for g in range(PASSES):
-                w_words, w_scales, w0 = packed["w", s0 // C, g]
+                w_words, w_scales, w0 = packed["w", e, g]
                 x_words, x_scales, x0 = packed["x", g, s0]
                 nc.tensor.matmul_mx(
                     out=acc[:],
@@ -128,81 +153,57 @@ def tile_moe_pre_lin_relu_kernel(tc, xT, w, b, gate, offs, pos1, pos2, pos3, pos
                     start=(g == 0),
                     stop=(g == PASSES - 1),
                 )
-            return acc
+            nc.scalar.activation(out=y[:, s0:s1], in_=acc[:], func=RELU, bias=bias[:, e : e + 1])
 
-        def finish_on_scalar(s0, s1):
-            e = s0 // C
-            nc.scalar.activation(out=y[:, s0:s1], in_=multiply(s0, s1)[:], func=RELU, bias=bias[:, e : e + 1])
+        own = S - P
+        steps = [(0, QUARTER, HALF), (0, HALF, S), (1, 0, HALF), (1, HALF, 6 * C), (1, 6 * C, own)]
+        raws = [gather_on_scalar(*step) for step in steps]
 
-        def finish_on_vector(s0, s1):
-            e = s0 // C
-            nc.vector.tensor_scalar(out=y[:, s0:s1], in0=multiply(s0, s1)[:], scalar1=bias[:, e : e + 1], scalar2=0.0, op0=ADD, op1=MAX)
-
-        w_bf = w_pool.tile([P, 4 * PART], BF16, name="w_bf", align_bytes=MX_ALIGN)
-        for e in range(E):
-            for g in range(PASSES):
-                first = (e * PASSES + g) * N * PACK
-                interleave(w_bf[:, first : first + N * PACK], w_raw[e][:, g])
-        x_bf = last_raw.tile([P, 8 * PART], BF16, name="x_bf", tag="w_raw7", align_bytes=MX_ALIGN)
-        gated1 = pass1.tile([P, 6 * S], F32, name="gated1", align_bytes=MX_ALIGN)
-
-        def part(tile, i, count=1):
-            return tile[:, i * PART : (i + count) * PART]
-
-        for s0, s1 in zip((0,) + GATE_CUTS, GATE_CUTS):
-            gather_row(1, 2, s0, s1, gated1[:, 2 * S + s0 : 2 * S + s1])
-        gather_row(1, 3, 0, HALF, gated1[:, 3 * S : 3 * S + HALF])
-        for j in range(PACK):
-            gather_row(0, j, 0, S, gated0[:, j, :])
-        interleave(part(x_bf, 0, 2), gated0[:, :, 0:HALF])
-        interleave(part(x_bf, 3), gated0[:, :, HALF : HALF + QUARTER])
-        interleave(part(x_bf, 5), gated0[:, :, HALF + QUARTER : S])
-
-        late = 3 * S + HALF
-        for j in range(2):
-            gather_row(1, j, 0, S, gated1[:, j * S : (j + 1) * S])
-        early_rows = gated1[:, 0 : PACK * S].rearrange("p (j s) -> p j s", j=PACK)
-        interleave(part(x_bf, 2), early_rows[:, :, 0:QUARTER])
-        interleave(part(x_bf, 4), early_rows[:, :, QUARTER:HALF])
-        for j in range(2, PACK):
-            gather_row(1, j, HALF, S, gated1[:, late + (j - 2) * S : late + (j - 2) * S + HALF])
-        for s0, dst in ((HALF, part(x_bf, 6)), (HALF + QUARTER, part(x_bf, 7))):
-            src = gated1[:].rearrange("p (u j c i) -> p c u j i", u=2, j=3, i=RUN)[:, s0 // RUN : (s0 + QUARTER) // RUN, :, 0:2, :]
-            nc.scalar.copy(out=dst.rearrange("p (c i u j) -> p c u j i", i=RUN, u=2, j=2), in_=src)
-
-        y = keep.tile([P, S], F32, name="y", tag="gates")
-        quantize(part(w_bf, 0, 2), w_runs(0, 4), "packed0", pool=keep, after="x_rows1_2")
-        quantize(part(x_bf, 0, 2), x_runs(0, 0, HALF), "packed1", pool=keep, after="x_rows1_3")
-        quantize(part(w_bf, 2), w_runs(4, 6), "packed2", pool=pass0, after="gated0")
-        quantize(part(x_bf, 2, 2), x_runs(1, 0, QUARTER) + x_runs(0, HALF, LAST_GROUP), "packed3", pool=raw, after="w_raw0")
-        for s in range(0, QUARTER, C):
-            finish_on_scalar(s, s + C)
-        quantize(part(x_bf, 4, 2), x_runs(1, QUARTER, HALF) + x_runs(0, LAST_GROUP, S), "packed4", pool=raw, after="w_raw1")
-        for s in range(QUARTER, HALF, C):
-            finish_on_scalar(s, s + C)
-        quantize(part(x_bf, 6), x_runs(1, HALF, LAST_GROUP), "packed5", pool=raw, after="w_raw2")
-        for s in range(HALF, LAST_GROUP, C):
-            finish_on_scalar(s, s + C)
-        quantize(part(w_bf, 3), w_runs(6, 8), "packed6", pool=pass1, after="gated1")
-        for s0, s1 in ((LAST_GROUP, LAST_EXPERT), (LAST_EXPERT, LAST_HALF), (LAST_HALF, S)):
-            first = 7 * PART + (s0 - LAST_GROUP) * PACK
-            quantize(x_bf[:, first : first + (s1 - s0) * PACK], x_runs(1, s0, s1), "packed_last%d" % s0)
-        finish_on_vector(LAST_GROUP, LAST_EXPERT)
-        finish_on_scalar(LAST_EXPERT, LAST_HALF)
-        finish_on_scalar(LAST_HALF, S)
+        gated = gather_on_vector(0, 0, QUARTER, first_cuts=(FIRST_GATE,))
+        gate_and_round(*steps[0], raws[0][:])
+        round_x(0, 0, QUARTER, gated)
+        round_w(0, 2)
+        quantize_x(0, 0, HALF)
+        round_w(2, 4)
+        gated = gather_on_vector(1, own, S)
+        quantize_w(0, 4)
+        round_x(1, own, S, gated)
+        gate_and_round(*steps[1], raws[1][:])
+        round_w(4, 6)
+        quantize_x(0, HALF, S)
+        round_w(6, 8)
+        quantize_x(1, own, S)
+        quantize_w(4, 8)
+        gate_and_round(*steps[2], raws[2][:])
+        gate_and_round(*steps[3], raws[3][:])
+        quantize_x(1, 0, HALF)
+        quantize_x(1, HALF, 6 * C)
+        gate_and_round(1, 6 * C, 7 * C, raws[4][:, :, 0:C])
+        gate_and_round(1, 7 * C, own, raws[4][:, :, C : C + P])
+        quantize_x(1, 6 * C, 7 * C)
+        quantize_x(1, 7 * C, own)
+        for s in range(0, 6 * C, C):
+            finish(s, s + C)
+        finish(own, S)
+        finish(6 * C, 7 * C)
+        finish(7 * C, own)
 
         halves = [slice(0, T // 2), slice(T // 2, T)]
-        last_parts = [halves[0], slice(T // 2, T - LAST_TOKENS), slice(T - LAST_TOKENS, T)]
-        sums = [keep.tile([P, T], F32, name="sum%d" % r, tag="x_rows0_%d" % r, align_bytes=MX_ALIGN) for r in range(TOP)]
 
         def results(r, part):
             return y[:].indirect(token_slot[r][:, part.start // STRIPE : part.stop // STRIPE])
 
+        got = [keep.tile([P, T], F32, name="got%d" % r, align_bytes=MX_ALIGN) for r in range(6)]
+        h0, h1 = halves
         for part in halves:
-            nc.vector.tensor_copy(sums[0][:, part], results(0, part))
-        for r in range(1, TOP - 1):
-            for part in halves:
-                nc.vector.tensor_tensor(sums[r][:, part], results(r, part), sums[r - 1][:, part], ADD)
-        for part in last_parts:
-            nc.vector.tensor_tensor(sums[TOP - 1][:, part], results(TOP - 1, part), sums[TOP - 2][:, part], ADD)
-            nc.sync.dma_start(out=out[:, part], in_=sums[TOP - 1][:, part])
+            for r in range(2):
+                nc.scalar.activation(got[r][:, part], results(r, part), COPY)
+        nc.vector.tensor_copy(got[2][:, h0], results(2, h0))
+        nc.vector.tensor_tensor(got[3][:, h0], results(3, h0), got[0][:, h0], ADD)
+        nc.vector.tensor_tensor(got[4][:, h0], got[2][:, h0], got[1][:, h0], ADD)
+        nc.vector.tensor_tensor(got[2][:, h1], results(2, h1), got[0][:, h1], ADD)
+        nc.vector.tensor_tensor(got[5][:, h0], got[4][:, h0], got[3][:, h0], ADD)
+        nc.sync.dma_start(out=out[:, h0], in_=got[5][:, h0])
+        nc.vector.tensor_tensor(got[3][:, h1], results(3, h1), got[1][:, h1], ADD)
+        nc.vector.tensor_tensor(got[5][:, h1], got[2][:, h1], got[3][:, h1], ADD)
+        nc.sync.dma_start(out=out[:, h1], in_=got[5][:, h1])

@@ -44,10 +44,8 @@ def tile_moe_pre_lin_relu_kernel(tc, xT, w, b, gate, offs, pos1, pos2, pos3, pos
             [keep.tile([P, WINDOW], F32, name="x_rows%d_%d" % (g, j), align_bytes=MX_ALIGN) for j in range(PACK)]
             for g in range(PASSES)
         ]
-        w_raw = keep.tile([P, E * PASSES, PACK, N], F32, name="w_raw", align_bytes=MX_ALIGN)
+        w_raw = [keep.tile([P, 2 * PASSES, PACK, N], F32, name="w_raw%d" % i, align_bytes=MX_ALIGN) for i in range(E // 2)]
         bias = keep.tile([P, E], F32, name="bias")
-        w_bf = keep.tile([P, E * PASSES * N * PACK], BF16, name="w_bf", align_bytes=MX_ALIGN)
-        x_bf = [keep.tile([P, S * PACK], BF16, name="x_bf%d" % g, align_bytes=MX_ALIGN) for g in range(PASSES)]
         y = keep.tile([P, S], F32, name="y")
         packed = {}
 
@@ -61,9 +59,13 @@ def tile_moe_pre_lin_relu_kernel(tc, xT, w, b, gate, offs, pos1, pos2, pos3, pos
 
         def load_w(e):
             nc.sync.dma_start(
-                out=w_raw[:, e * PASSES : (e + 1) * PASSES].rearrange("p g j n -> p g (j n)"),
+                out=w_raw[e // 2][:, e % 2 * PASSES : (e % 2 + 1) * PASSES].rearrange("p g j n -> p g (j n)"),
                 in_=w[e].rearrange("(g p j) n -> p g (j n)", g=PASSES, j=PACK),
             )
+
+        warm = keep.tile([P, 2], F32, name="warm")
+        nc.vector.memset(warm[:, 0:1], 0.0)
+        nc.scalar.activation(warm[:, 1:2], warm[:, 0:1], COPY)
 
         load_x(0, 0)
         nc.sync.dma_start(slot_token[:], offs)
@@ -71,15 +73,15 @@ def tile_moe_pre_lin_relu_kernel(tc, xT, w, b, gate, offs, pos1, pos2, pos3, pos
         load_gate(FIRST_GATE, QUARTER)
         for j in range(1, PACK):
             load_x(0, j)
+        for j in range(PACK):
+            load_x(1, j)
         load_gate(QUARTER, HALF)
+        load_gate(S - P, S)
         nc.sync.dma_start(out=bias[:], in_=b)
         for r, pos in enumerate((pos1, pos2, pos3, pos4)):
             nc.sync.dma_start(token_slot[r][:], pos)
         for e in range(E // 2):
             load_w(e)
-        load_gate(S - P, S)
-        for j in range(PACK):
-            load_x(1, j)
         load_gate(HALF, S - P)
         for e in range(E // 2, E):
             load_w(e)
@@ -93,50 +95,50 @@ def tile_moe_pre_lin_relu_kernel(tc, xT, w, b, gate, offs, pos1, pos2, pos3, pos
         def rows(src):
             return src.rearrange("p j (c i) -> p c j i", i=RUN)
 
-        def gather_on_scalar(g, s0, s1):
-            raw = keep.tile([P, PACK, s1 - s0], F32, name="raw%d_%d" % (g, s0), align_bytes=MX_ALIGN)
+        def gather_on_scalar(g, s0, s1, tag):
+            raw = keep.tile([P, PACK, s1 - s0], F32, name="raw%d_%d" % (g, s0), tag=tag, align_bytes=MX_ALIGN)
             for j in range(PACK):
                 nc.scalar.activation(raw[:, j, :], tokens(g, j, s0, s1), COPY)
             return raw
 
-        def gate_and_round(g, s0, s1, raw):
+        def rounded(name, columns, after=None):
+            return keep.tile([P, columns * PACK], BF16, name=name, tag=after or name, align_bytes=MX_ALIGN)
+
+        def gate_and_round(dst, raw, s0, s1):
             n = (s1 - s0) // RUN
             spread = gates[:, s0:s1].rearrange("p (c i) -> p c i", i=RUN).unsqueeze(2).to_broadcast([P, n, PACK, RUN])
-            nc.vector.tensor_tensor(words(x_bf[g][:, s0 * PACK : s1 * PACK]), rows(raw), spread, MULT)
+            nc.vector.tensor_tensor(words(dst), rows(raw), spread, MULT)
 
         def gather_on_vector(g, s0, s1, first_cuts=()):
-            gated = keep.tile([P, PACK, s1 - s0], F32, name="gated%d_%d" % (g, s0), align_bytes=MX_ALIGN)
+            gated = keep.tile([P, PACK, s1 - s0], F32, name="gated%d" % g, align_bytes=MX_ALIGN)
             for j in range(PACK):
                 cuts = (s0,) + (first_cuts if j == 0 else ()) + (s1,)
                 for a, z in zip(cuts, cuts[1:]):
                     nc.vector.tensor_tensor(gated[:, j, a - s0 : z - s0], tokens(g, j, a, z), gates[:, a:z], MULT)
             return gated
 
-        def round_x(g, s0, s1, gated):
-            nc.vector.tensor_copy(words(x_bf[g][:, s0 * PACK : s1 * PACK]), rows(gated[:]))
+        def round_x(dst, gated):
+            nc.vector.tensor_copy(words(dst), rows(gated))
 
-        def round_w(e0, e1):
-            dst = w_bf[:, e0 * PASSES * N * PACK : e1 * PASSES * N * PACK]
+        def round_w(dst, e0, e1):
             nc.vector.tensor_copy(
                 dst.rearrange("p (m c i j) -> p m c j i", i=RUN, j=PACK, c=N // RUN),
-                w_raw[:, e0 * PASSES : e1 * PASSES].rearrange("p m j (c i) -> p m c j i", i=RUN),
+                w_raw[e0 // 2][:].rearrange("p m j (c i) -> p m c j i", i=RUN),
             )
 
-        def quantize(src, runs, name):
+        def quantize(src, runs, name, after=None):
             width = len(runs) * P
-            codes = keep.tile([P, width], U32, name=name, align_bytes=MX_ALIGN)
+            codes = keep.tile([P, width], U32, name=name, tag=after or name, align_bytes=MX_ALIGN)
             scales = keep.tile([P, width], U8, name=name + "_scales", align_bytes=MX_ALIGN)
             nc.vector.quantize_mx(out=codes[:].bitcast(FP8X4), scales=scales[:], in_=src)
             for i, run in enumerate(runs):
                 packed[run] = (codes, scales, i * P)
 
-        def quantize_w(e0, e1):
-            runs = [("w", e, g) for e in range(e0, e1) for g in range(PASSES)]
-            quantize(w_bf[:, e0 * PASSES * N * PACK : e1 * PASSES * N * PACK], runs, "w_packed%d" % e0)
+        def quantize_w(src, e0, e1, after=None):
+            quantize(src, [("w", e, g) for e in range(e0, e1) for g in range(PASSES)], "w_packed%d" % e0, after)
 
-        def quantize_x(g, s0, s1):
-            runs = [("x", g, s) for s in range(s0, s1, P)]
-            quantize(x_bf[g][:, s0 * PACK : s1 * PACK], runs, "x_packed%d_%d" % (g, s0))
+        def quantize_x(src, g, s0, s1):
+            quantize(src, [("x", g, s) for s in range(s0, s1, P)], "x_packed%d_%d" % (g, s0))
 
         def finish(s0, s1):
             e = s0 // C
@@ -156,32 +158,44 @@ def tile_moe_pre_lin_relu_kernel(tc, xT, w, b, gate, offs, pos1, pos2, pos3, pos
             nc.scalar.activation(out=y[:, s0:s1], in_=acc[:], func=RELU, bias=bias[:, e : e + 1])
 
         own = S - P
-        steps = [(0, QUARTER, HALF), (0, HALF, S), (1, 0, HALF), (1, HALF, 6 * C), (1, 6 * C, own)]
-        raws = [gather_on_scalar(*step) for step in steps]
+        part = QUARTER * PACK
 
+        raw1 = gather_on_scalar(0, QUARTER, HALF, "raw_a")
+        raw2 = gather_on_scalar(1, 0, HALF, "raw_b")
         gated = gather_on_vector(0, 0, QUARTER, first_cuts=(FIRST_GATE,))
-        gate_and_round(*steps[0], raws[0][:])
-        round_x(0, 0, QUARTER, gated)
-        round_w(0, 2)
-        quantize_x(0, 0, HALF)
-        round_w(2, 4)
+        x_bf = rounded("x_first", HALF)
+        gate_and_round(x_bf[:, part:], raw1[:], QUARTER, HALF)
+        raw3 = gather_on_scalar(0, HALF, S, "raw_a")
+        round_x(x_bf[:, 0:part], gated[:])
         gated = gather_on_vector(1, own, S)
-        quantize_w(0, 4)
-        round_x(1, own, S, gated)
-        gate_and_round(*steps[1], raws[1][:])
-        round_w(4, 6)
-        quantize_x(0, HALF, S)
-        round_w(6, 8)
-        quantize_x(1, own, S)
-        quantize_w(4, 8)
-        gate_and_round(*steps[2], raws[2][:])
-        gate_and_round(*steps[3], raws[3][:])
-        quantize_x(1, 0, HALF)
-        quantize_x(1, HALF, 6 * C)
-        gate_and_round(1, 6 * C, 7 * C, raws[4][:, :, 0:C])
-        gate_and_round(1, 7 * C, own, raws[4][:, :, C : C + P])
-        quantize_x(1, 6 * C, 7 * C)
-        quantize_x(1, 7 * C, own)
+        quantize_x(x_bf[:], 0, 0, HALF)
+        w_bf = rounded("w_first", HALF)
+        round_w(w_bf[:, 0:part], 0, 2)
+        x_own = rounded("x_own", P)
+        round_x(x_own[:], gated[:])
+        round_w(w_bf[:, part:], 2, 4)
+        quantize_x(x_own[:], 1, own, S)
+        quantize_w(w_bf[:], 0, 4)
+        x_bf = w_bf
+        gate_and_round(x_bf[:], raw2[:], 0, HALF)
+        raw4 = gather_on_scalar(1, HALF, 6 * C, "raw_b")
+        w_bf = rounded("w_second", HALF)
+        round_w(w_bf[:, 0:part], 4, 6)
+        round_w(w_bf[:, part:], 6, 8)
+        raw5 = gather_on_scalar(1, 6 * C, own, "w_raw3")
+        quantize_x(x_bf[:], 1, 0, HALF)
+        quantize_w(w_bf[:], 4, 8)
+        x_third = w_bf
+        gate_and_round(x_third[:], raw3[:], HALF, S)
+        x_bf = rounded("x_fourth", QUARTER, after="raw_a")
+        gate_and_round(x_bf[:], raw4[:], HALF, 6 * C)
+        quantize_x(x_third[:], 0, HALF, S)
+        quantize_x(x_bf[:], 1, HALF, 6 * C)
+        x_bf = x_third
+        gate_and_round(x_bf[:, 0 : C * PACK], raw5[:, :, 0:C], 6 * C, 7 * C)
+        gate_and_round(x_bf[:, C * PACK : (C + P) * PACK], raw5[:, :, C : C + P], 7 * C, own)
+        quantize_x(x_bf[:, 0 : C * PACK], 1, 6 * C, 7 * C)
+        quantize_x(x_bf[:, C * PACK : (C + P) * PACK], 1, 7 * C, own)
         for s in range(0, 6 * C, C):
             finish(s, s + C)
         finish(own, S)
@@ -195,15 +209,14 @@ def tile_moe_pre_lin_relu_kernel(tc, xT, w, b, gate, offs, pos1, pos2, pos3, pos
 
         got = [keep.tile([P, T], F32, name="got%d" % r, align_bytes=MX_ALIGN) for r in range(6)]
         h0, h1 = halves
-        for part in halves:
-            for r in range(2):
+        for r in range(2):
+            for part in halves:
                 nc.scalar.activation(got[r][:, part], results(r, part), COPY)
         nc.vector.tensor_copy(got[2][:, h0], results(2, h0))
         nc.vector.tensor_tensor(got[3][:, h0], results(3, h0), got[0][:, h0], ADD)
-        nc.vector.tensor_tensor(got[4][:, h0], got[2][:, h0], got[1][:, h0], ADD)
         nc.vector.tensor_tensor(got[2][:, h1], results(2, h1), got[0][:, h1], ADD)
-        nc.vector.tensor_tensor(got[5][:, h0], got[4][:, h0], got[3][:, h0], ADD)
-        nc.sync.dma_start(out=out[:, h0], in_=got[5][:, h0])
-        nc.vector.tensor_tensor(got[3][:, h1], results(3, h1), got[1][:, h1], ADD)
-        nc.vector.tensor_tensor(got[5][:, h1], got[2][:, h1], got[3][:, h1], ADD)
-        nc.sync.dma_start(out=out[:, h1], in_=got[5][:, h1])
+        nc.vector.tensor_tensor(got[4][:, h0], got[2][:, h0], got[3][:, h0], ADD)
+        nc.vector.tensor_tensor(got[4][:, h1], results(3, h1), got[2][:, h1], ADD)
+        for part in halves:
+            nc.vector.tensor_tensor(got[5][:, part], got[4][:, part], got[1][:, part], ADD)
+            nc.sync.dma_start(out=out[:, part], in_=got[5][:, part])

@@ -24,7 +24,7 @@ PACK = 4
 PASSES = K // (P * PACK)
 STRIPE = 16
 MX_ALIGN = 64
-RUN = 2
+RUN = 4
 HALF = S // 2
 QUARTER = S // 4
 WINDOW = HALF + STRIPE
@@ -171,26 +171,26 @@ def tile_moe_pre_lin_relu_kernel(tc, xT, w, b, gate, offs, pos1, pos2, pos3, pos
         quantize_x(x_bf[:], 0, 0, HALF)
         w_bf = rounded("w_first", HALF)
         round_w(w_bf[:, 0:part], 0, 2)
-        x_own = rounded("x_own", P)
-        round_x(x_own[:], gated[:])
         round_w(w_bf[:, part:], 2, 4)
-        quantize_x(x_own[:], 1, own, S)
+        x_own = rounded("x_own", P, after="w_raw0")
+        round_x(x_own[:], gated[:])
         quantize_w(w_bf[:], 0, 4)
+        quantize_x(x_own[:], 1, own, S)
         x_bf = w_bf
         gate_and_round(x_bf[:], raw2[:], 0, HALF)
         raw4 = gather_on_scalar(1, HALF, 6 * C, "raw_b")
         w_bf = rounded("w_second", HALF)
         round_w(w_bf[:, 0:part], 4, 6)
         round_w(w_bf[:, part:], 6, 8)
-        raw5 = gather_on_scalar(1, 6 * C, own, "w_raw3")
+        raw5 = gather_on_scalar(1, 6 * C, own, "w_raw2")
         quantize_x(x_bf[:], 1, 0, HALF)
         quantize_w(w_bf[:], 4, 8)
-        x_third = w_bf
+        x_third = rounded("x_third", HALF, after="w_raw3")
         gate_and_round(x_third[:], raw3[:], HALF, S)
-        x_bf = rounded("x_fourth", QUARTER, after="raw_a")
-        gate_and_round(x_bf[:], raw4[:], HALF, 6 * C)
+        x_bf = w_bf[:, 0:part]
+        gate_and_round(x_bf, raw4[:], HALF, 6 * C)
         quantize_x(x_third[:], 0, HALF, S)
-        quantize_x(x_bf[:], 1, HALF, 6 * C)
+        quantize_x(x_bf, 1, HALF, 6 * C)
         x_bf = x_third
         gate_and_round(x_bf[:, 0 : C * PACK], raw5[:, :, 0:C], 6 * C, 7 * C)
         gate_and_round(x_bf[:, C * PACK : (C + P) * PACK], raw5[:, :, C : C + P], 7 * C, own)

@@ -1,6 +1,7 @@
 from contextlib import ExitStack
 
 import concourse.mybir as mybir
+from concourse.masks import make_identity
 
 K, T, E, C, N = 1024, 512, 8, 256, 128
 TOP = 4
@@ -35,18 +36,22 @@ def tile_moe_pre_lin_relu_kernel(tc, xT, w, b, gate, offs, pos1, pos2, pos3, pos
     nc = tc.nc
     with ExitStack() as ctx:
         keep = ctx.enter_context(tc.tile_pool(name="keep", bufs=1))
-        psum = ctx.enter_context(tc.psum_pool(name="psum", bufs=8))
+        psum = ctx.enter_context(tc.psum_pool(name="psum", bufs=1))
 
         slot_token = keep.tile([P, S // STRIPE], U16, name="slot_token")
         token_slot = [keep.tile([P, T // STRIPE], U16, name="token_slot%d" % r) for r in range(TOP)]
-        gates = keep.tile([P, S], F32, name="gates")
+        gate_first = keep.tile([P, QUARTER], F32, name="gate_first", align_bytes=MX_ALIGN)
+        gate_last = keep.tile([P, QUARTER], F32, name="gate_last", align_bytes=MX_ALIGN)
+        gate_runs = keep.tile([P, P], F32, name="gate_runs")
+        gate_columns = keep.tile([P, S // P], F32, name="gate_columns")
+        identity = keep.tile([P, P], F32, name="identity")
         x_rows = [
             [keep.tile([P, WINDOW], F32, name="x_rows%d_%d" % (g, j), align_bytes=MX_ALIGN) for j in range(PACK)]
             for g in range(PASSES)
         ]
-        w_raw = [keep.tile([P, 2 * PASSES, PACK, N], F32, name="w_raw%d" % i, align_bytes=MX_ALIGN) for i in range(E // 2)]
+        w_raw = [keep.tile([P, PASSES, PACK, N], F32, name="w_raw%d" % e, align_bytes=MX_ALIGN) for e in range(E - 2)]
+        w_raw_last = keep.tile([P, 2 * PASSES, PACK, N], F32, name="w_raw_last", align_bytes=MX_ALIGN)
         bias = keep.tile([P, E], F32, name="bias")
-        y = keep.tile([P, S], F32, name="y")
         packed = {}
 
         x_view = xT.rearrange("(g p j) t -> g j p t", g=PASSES, j=PACK)
@@ -54,12 +59,10 @@ def tile_moe_pre_lin_relu_kernel(tc, xT, w, b, gate, offs, pos1, pos2, pos3, pos
         def load_x(g, j):
             nc.sync.dma_start(out=x_rows[g][j][:, 0:T], in_=x_view[g, j])
 
-        def load_gate(s0, s1):
-            nc.sync.dma_start(out=gates[:, s0:s1], in_=gate[0:P, s0:s1])
-
         def load_w(e):
+            dst = w_raw[e][:] if e < E - 2 else w_raw_last[:, (e - E + 2) * PASSES : (e - E + 3) * PASSES]
             nc.sync.dma_start(
-                out=w_raw[e // 2][:, e % 2 * PASSES : (e % 2 + 1) * PASSES].rearrange("p g j n -> p g (j n)"),
+                out=dst.rearrange("p g j n -> p g (j n)"),
                 in_=w[e].rearrange("(g p j) n -> p g (j n)", g=PASSES, j=PACK),
             )
 
@@ -67,24 +70,37 @@ def tile_moe_pre_lin_relu_kernel(tc, xT, w, b, gate, offs, pos1, pos2, pos3, pos
         nc.vector.memset(warm[:, 0:1], 0.0)
         nc.scalar.activation(warm[:, 1:2], warm[:, 0:1], COPY)
 
+        make_identity(nc, identity[:])
+        own = S - QUARTER
+
         load_x(0, 0)
         nc.sync.dma_start(slot_token[:], offs)
-        load_gate(0, FIRST_GATE)
-        load_gate(FIRST_GATE, QUARTER)
-        for j in range(1, PACK):
-            load_x(0, j)
+        nc.sync.dma_start(out=gate_first[:, 0:FIRST_GATE], in_=gate[0:P, 0:FIRST_GATE])
+        nc.sync.dma_start(out=gate_first[:, FIRST_GATE:], in_=gate[0:P, FIRST_GATE:QUARTER])
+        load_x(0, 1)
+        nc.sync.dma_start(out=gate_runs[:], in_=gate[0 : P * P // S, :].rearrange("r (c s) -> (r c) s", s=P))
+        load_x(0, 2)
+        load_x(0, 3)
+        load_w(0)
         for j in range(PACK):
             load_x(1, j)
-        load_gate(QUARTER, HALF)
-        load_gate(S - P, S)
+        nc.sync.dma_start(out=gate_last[:], in_=gate[0:P, own:S])
         nc.sync.dma_start(out=bias[:], in_=b)
         for r, pos in enumerate((pos1, pos2, pos3, pos4)):
             nc.sync.dma_start(token_slot[r][:], pos)
-        for e in range(E // 2):
+        for e in range(1, E):
             load_w(e)
-        load_gate(HALF, S - P)
-        for e in range(E // 2, E):
-            load_w(e)
+
+        turned = psum.tile([P, P], F32, name="turned", tag="sums0")
+        nc.tensor.transpose(turned[:], gate_runs[:], identity[:])
+        nc.vector.tensor_copy(gate_columns[:], turned[:, 0 : S // P])
+        gate_banks = [psum.tile([P, QUARTER], F32, name="gate_bank%d" % i) for i in range(S // QUARTER)]
+        for i in (1, 0, 2, 3):
+            for c in range(QUARTER // P):
+                column = i * QUARTER // P + c
+                nc.tensor.transpose(
+                    gate_banks[i][:, c * P : (c + 1) * P], gate_columns[:, column : column + 1].to_broadcast([P, P]), identity[:]
+                )
 
         def tokens(g, j, s0, s1):
             return x_rows[g][j][:].indirect(slot_token[:, s0 // STRIPE : s1 // STRIPE])
@@ -106,24 +122,29 @@ def tile_moe_pre_lin_relu_kernel(tc, xT, w, b, gate, offs, pos1, pos2, pos3, pos
 
         def gate_and_round(dst, raw, s0, s1):
             n = (s1 - s0) // RUN
-            spread = gates[:, s0:s1].rearrange("p (c i) -> p c i", i=RUN).unsqueeze(2).to_broadcast([P, n, PACK, RUN])
+            gates = gate_banks[s0 // QUARTER][:, s0 % QUARTER : s0 % QUARTER + s1 - s0]
+            spread = gates.rearrange("p (c i) -> p c i", i=RUN).unsqueeze(2).to_broadcast([P, n, PACK, RUN])
             nc.vector.tensor_tensor(words(dst), rows(raw), spread, MULT)
 
-        def gather_on_vector(g, s0, s1, first_cuts=()):
-            gated = keep.tile([P, PACK, s1 - s0], F32, name="gated%d" % g, align_bytes=MX_ALIGN)
+        def gather_on_vector(name, s0, s1, gates, first_cuts=()):
+            gated = keep.tile([P, PACK, s1 - s0], F32, name=name, align_bytes=MX_ALIGN)
             for j in range(PACK):
                 cuts = (s0,) + (first_cuts if j == 0 else ()) + (s1,)
                 for a, z in zip(cuts, cuts[1:]):
-                    nc.vector.tensor_tensor(gated[:, j, a - s0 : z - s0], tokens(g, j, a, z), gates[:, a:z], MULT)
+                    nc.vector.tensor_tensor(gated[:, j, a - s0 : z - s0], tokens(0, j, a, z), gates[:, a - s0 : z - s0], MULT)
             return gated
 
         def round_x(dst, gated):
             nc.vector.tensor_copy(words(dst), rows(gated))
 
-        def round_w(dst, e0, e1):
-            nc.vector.tensor_copy(
-                dst.rearrange("p (m c i j) -> p m c j i", i=RUN, j=PACK, c=N // RUN),
-                w_raw[e0 // 2][:].rearrange("p m j (c i) -> p m c j i", i=RUN),
+        def round_w_on_gpsimd(dst, e):
+            nc.gpsimd.tensor_scalar(
+                out=dst.rearrange("p (g n j) -> p g n j", g=PASSES, j=PACK),
+                in0=w_raw[e][:].rearrange("p g j n -> p g n j"),
+                scalar1=1.0,
+                scalar2=0.0,
+                op0=MULT,
+                op1=ADD,
             )
 
         def quantize(src, runs, name, after=None):
@@ -140,14 +161,12 @@ def tile_moe_pre_lin_relu_kernel(tc, xT, w, b, gate, offs, pos1, pos2, pos3, pos
         def quantize_x(src, g, s0, s1):
             quantize(src, [("x", g, s) for s in range(s0, s1, P)], "x_packed%d_%d" % (g, s0))
 
-        def finish(s0, s1):
-            e = s0 // C
-            acc = psum.tile([P, s1 - s0], F32, name="acc")
+        def multiply(acc, s0, s1):
             for g in range(PASSES):
-                w_words, w_scales, w0 = packed["w", e, g]
+                w_words, w_scales, w0 = packed["w", s0 // C, g]
                 x_words, x_scales, x0 = packed["x", g, s0]
                 nc.tensor.matmul_mx(
-                    out=acc[:],
+                    out=acc,
                     lhsT=w_words[:, w0 : w0 + N].bitcast(FP8X4),
                     lhsT_scale=w_scales[:, w0 : w0 + N],
                     rhs=x_words[:, x0 : x0 + s1 - s0].bitcast(FP8X4),
@@ -155,52 +174,72 @@ def tile_moe_pre_lin_relu_kernel(tc, xT, w, b, gate, offs, pos1, pos2, pos3, pos
                     start=(g == 0),
                     stop=(g == PASSES - 1),
                 )
-            nc.scalar.activation(out=y[:, s0:s1], in_=acc[:], func=RELU, bias=bias[:, e : e + 1])
 
-        own = S - P
         part = QUARTER * PACK
+        one = C * PACK
 
         raw1 = gather_on_scalar(0, QUARTER, HALF, "raw_a")
         raw2 = gather_on_scalar(1, 0, HALF, "raw_b")
-        gated = gather_on_vector(0, 0, QUARTER, first_cuts=(FIRST_GATE,))
+        gated = gather_on_vector("gated_first", 0, QUARTER, gate_first, first_cuts=(FIRST_GATE,))
         x_bf = rounded("x_first", HALF)
         gate_and_round(x_bf[:, part:], raw1[:], QUARTER, HALF)
-        raw3 = gather_on_scalar(0, HALF, S, "raw_a")
+        w_0 = rounded("w_0", C, after="gate_first")
+        round_w_on_gpsimd(w_0[:], 0)
+        raw3 = gather_on_scalar(0, HALF, own, "raw_a")
         round_x(x_bf[:, 0:part], gated[:])
-        gated = gather_on_vector(1, own, S)
+        gated = gather_on_vector("gated_last", own, S, gate_last)
         quantize_x(x_bf[:], 0, 0, HALF)
-        w_bf = rounded("w_first", HALF)
-        round_w(w_bf[:, 0:part], 0, 2)
-        round_w(w_bf[:, part:], 2, 4)
-        x_own = rounded("x_own", P, after="w_raw0")
+        x_own = rounded("x_own", QUARTER)
         round_x(x_own[:], gated[:])
-        quantize_w(w_bf[:], 0, 4)
-        quantize_x(x_own[:], 1, own, S)
-        x_bf = w_bf
-        gate_and_round(x_bf[:], raw2[:], 0, HALF)
-        raw4 = gather_on_scalar(1, HALF, 6 * C, "raw_b")
-        w_bf = rounded("w_second", HALF)
-        round_w(w_bf[:, 0:part], 4, 6)
-        round_w(w_bf[:, part:], 6, 8)
-        raw5 = gather_on_scalar(1, 6 * C, own, "w_raw2")
-        quantize_x(x_bf[:], 1, 0, HALF)
-        quantize_w(w_bf[:], 4, 8)
-        x_third = rounded("x_third", HALF, after="w_raw3")
-        gate_and_round(x_third[:], raw3[:], HALF, S)
-        x_bf = w_bf[:, 0:part]
-        gate_and_round(x_bf, raw4[:], HALF, 6 * C)
-        quantize_x(x_third[:], 0, HALF, S)
-        quantize_x(x_bf, 1, HALF, 6 * C)
-        x_bf = x_third
-        gate_and_round(x_bf[:, 0 : C * PACK], raw5[:, :, 0:C], 6 * C, 7 * C)
-        gate_and_round(x_bf[:, C * PACK : (C + P) * PACK], raw5[:, :, C : C + P], 7 * C, own)
-        quantize_x(x_bf[:, 0 : C * PACK], 1, 6 * C, 7 * C)
-        quantize_x(x_bf[:, C * PACK : (C + P) * PACK], 1, 7 * C, own)
-        for s in range(0, 6 * C, C):
-            finish(s, s + C)
-        finish(own, S)
-        finish(6 * C, 7 * C)
-        finish(7 * C, own)
+        x_bf = rounded("x_second", HALF + QUARTER, after="gate_last")
+        for i in range(2):
+            gate_and_round(x_bf[:, i * part : (i + 1) * part], raw2[:, :, i * QUARTER : (i + 1) * QUARTER], i * QUARTER, (i + 1) * QUARTER)
+        w_123 = rounded("w_123", 3 * C, after="gated_last")
+        for i in range(3):
+            round_w_on_gpsimd(w_123[:, i * one : (i + 1) * one], 1 + i)
+        raw4 = gather_on_scalar(1, HALF, own, "raw_b")
+        quantize_x(x_own[:], 0, own, S)
+        gate_and_round(x_bf[:, 2 * part :], raw3[:], HALF, own)
+        w_4 = rounded("w_4", C, after="x_own")
+        round_w_on_gpsimd(w_4[:], 4)
+        raw5 = gather_on_scalar(1, own, S, "raw_a")
+        quantize_x(x_bf[:, 0 : 2 * part], 1, 0, HALF)
+        quantize_w(w_0[:], 0, 1)
+        quantize_w(w_123[:, 0:one], 1, 2)
+        quantize_w(w_123[:, one:], 2, 4)
+        gate_and_round(x_bf[:, 0:part], raw4[:], HALF, own)
+        w_5 = rounded("w_5", C, after="gated_last")
+        round_w_on_gpsimd(w_5[:], 5)
+        quantize_x(x_bf[:, 2 * part :], 0, HALF, own)
+        w_67 = rounded("w_67", 2 * C, after="x_first")
+        nc.vector.tensor_copy(
+            w_67[:].rearrange("p (m c i j) -> p m c j i", i=RUN, j=PACK, c=N // RUN),
+            w_raw_last[:].rearrange("p m j (c i) -> p m c j i", i=RUN),
+        )
+        quantize_x(x_bf[:, 0:part], 1, HALF, own)
+        quantize_w(w_4[:], 4, 5)
+        quantize_w(w_5[:], 5, 6)
+        quantize_w(w_67[:], 6, 8)
+        for i in range(2):
+            gate_and_round(x_bf[:, i * one : (i + 1) * one], raw5[:, :, i * C : (i + 1) * C], own + i * C, own + (i + 1) * C)
+        for i in range(2):
+            quantize_x(x_bf[:, i * one : (i + 1) * one], 1, own + i * C, own + (i + 1) * C)
+
+        y = keep.tile([P, S], F32, name="y", tag="x_rows1_2", align_bytes=MX_ALIGN)
+
+        def finish(e, acc):
+            nc.scalar.activation(out=y[:, e * C : (e + 1) * C], in_=acc, func=RELU, bias=bias[:, e : e + 1])
+
+        for pair in range(3):
+            acc = psum.tile([P, 2 * C], F32, name="sums%d" % pair)
+            for i in range(2):
+                multiply(acc[:, i * C : (i + 1) * C], (2 * pair + i) * C, (2 * pair + i + 1) * C)
+            for i in range(2):
+                finish(2 * pair + i, acc[:, i * C : (i + 1) * C])
+        for e, tag in ((6, "sums3"), (7, "gate_bank0")):
+            acc = psum.tile([P, C], F32, name="sum%d" % e, tag=tag)
+            multiply(acc[:], e * C, (e + 1) * C)
+            finish(e, acc[:])
 
         halves = [slice(0, T // 2), slice(T // 2, T)]
 

@@ -41,8 +41,9 @@ def tile_moe_pre_lin_relu_kernel(tc, xT, w, b, gate, offs, pos1, pos2, pos3, pos
         slot_token = keep.tile([P, S // STRIPE], U16, name="slot_token")
         token_slot = [keep.tile([P, T // STRIPE], U16, name="token_slot%d" % r) for r in range(TOP)]
         gate_first = keep.tile([P, QUARTER], F32, name="gate_first", align_bytes=MX_ALIGN)
-        gate_last = keep.tile([P, QUARTER], F32, name="gate_last", align_bytes=MX_ALIGN)
-        gate_runs = keep.tile([P, P], F32, name="gate_runs")
+        gate_last = keep.tile([P, C + P], F32, name="gate_last", align_bytes=MX_ALIGN)
+        gated_first = keep.tile([P, PACK, QUARTER], F32, name="gated_first", align_bytes=MX_ALIGN)
+        gate_runs = gated_first[:, 2, 0:P]
         gate_columns = keep.tile([P, S // P], F32, name="gate_columns")
         identity = keep.tile([P, P], F32, name="identity")
         x_rows = [
@@ -67,18 +68,18 @@ def tile_moe_pre_lin_relu_kernel(tc, xT, w, b, gate, offs, pos1, pos2, pos3, pos
             )
 
         warm = keep.tile([P, 2], F32, name="warm")
-        nc.vector.memset(warm[:, 0:1], 0.0)
+        nc.gpsimd.memset(warm[:, 0:1], 0.0)
         nc.scalar.activation(warm[:, 1:2], warm[:, 0:1], COPY)
 
         make_identity(nc, identity[:])
-        own = S - QUARTER
+        own = S - C - P
 
         load_x(0, 0)
         nc.sync.dma_start(slot_token[:], offs)
         nc.sync.dma_start(out=gate_first[:, 0:FIRST_GATE], in_=gate[0:P, 0:FIRST_GATE])
         nc.sync.dma_start(out=gate_first[:, FIRST_GATE:], in_=gate[0:P, FIRST_GATE:QUARTER])
         load_x(0, 1)
-        nc.sync.dma_start(out=gate_runs[:], in_=gate[0 : P * P // S, :].rearrange("r (c s) -> (r c) s", s=P))
+        nc.sync.dma_start(out=gate_runs, in_=gate[0 : P * P // S, :].rearrange("r (c s) -> (r c) s", s=P))
         load_x(0, 2)
         load_x(0, 3)
         load_w(0)
@@ -92,7 +93,7 @@ def tile_moe_pre_lin_relu_kernel(tc, xT, w, b, gate, offs, pos1, pos2, pos3, pos
             load_w(e)
 
         turned = psum.tile([P, P], F32, name="turned", tag="sums0")
-        nc.tensor.transpose(turned[:], gate_runs[:], identity[:])
+        nc.tensor.transpose(turned[:], gate_runs, identity[:])
         nc.vector.tensor_copy(gate_columns[:], turned[:, 0 : S // P])
         gate_banks = [psum.tile([P, QUARTER], F32, name="gate_bank%d" % i) for i in range(S // QUARTER)]
         for i in (1, 0, 2, 3):
@@ -126,21 +127,19 @@ def tile_moe_pre_lin_relu_kernel(tc, xT, w, b, gate, offs, pos1, pos2, pos3, pos
             spread = gates.rearrange("p (c i) -> p c i", i=RUN).unsqueeze(2).to_broadcast([P, n, PACK, RUN])
             nc.vector.tensor_tensor(words(dst), rows(raw), spread, MULT)
 
-        def gather_on_vector(name, s0, s1, gates, first_cuts=()):
-            gated = keep.tile([P, PACK, s1 - s0], F32, name=name, align_bytes=MX_ALIGN)
+        def gather_on_vector(gated, s0, s1, gates, first_cuts=()):
             for j in range(PACK):
                 cuts = (s0,) + (first_cuts if j == 0 else ()) + (s1,)
                 for a, z in zip(cuts, cuts[1:]):
                     nc.vector.tensor_tensor(gated[:, j, a - s0 : z - s0], tokens(0, j, a, z), gates[:, a - s0 : z - s0], MULT)
-            return gated
 
         def round_x(dst, gated):
             nc.vector.tensor_copy(words(dst), rows(gated))
 
-        def round_w_on_gpsimd(dst, e):
+        def round_w_on_gpsimd(dst, e, g0=0, g1=PASSES):
             nc.gpsimd.tensor_scalar(
-                out=dst.rearrange("p (g n j) -> p g n j", g=PASSES, j=PACK),
-                in0=w_raw[e][:].rearrange("p g j n -> p g n j"),
+                out=dst.rearrange("p (g n j) -> p g n j", n=N, j=PACK),
+                in0=w_raw[e][:, g0:g1].rearrange("p g j n -> p g n j"),
                 scalar1=1.0,
                 scalar2=0.0,
                 op0=MULT,
@@ -161,8 +160,8 @@ def tile_moe_pre_lin_relu_kernel(tc, xT, w, b, gate, offs, pos1, pos2, pos3, pos
         def quantize_x(src, g, s0, s1):
             quantize(src, [("x", g, s) for s in range(s0, s1, P)], "x_packed%d_%d" % (g, s0))
 
-        def multiply(acc, s0, s1):
-            for g in range(PASSES):
+        def multiply(acc, s0, s1, passes=(0, 1), start=True, stop=True):
+            for g in passes:
                 w_words, w_scales, w0 = packed["w", s0 // C, g]
                 x_words, x_scales, x0 = packed["x", g, s0]
                 nc.tensor.matmul_mx(
@@ -171,59 +170,67 @@ def tile_moe_pre_lin_relu_kernel(tc, xT, w, b, gate, offs, pos1, pos2, pos3, pos
                     lhsT_scale=w_scales[:, w0 : w0 + N],
                     rhs=x_words[:, x0 : x0 + s1 - s0].bitcast(FP8X4),
                     rhs_scale=x_scales[:, x0 : x0 + s1 - s0],
-                    start=(g == 0),
-                    stop=(g == PASSES - 1),
+                    start=start and g == passes[0],
+                    stop=stop and g == passes[-1],
                 )
 
         part = QUARTER * PACK
         one = C * PACK
 
+        sixth = 6 * C
+        half = one // PASSES
+        last = (S - own) * PACK
+
         raw1 = gather_on_scalar(0, QUARTER, HALF, "raw_a")
         raw2 = gather_on_scalar(1, 0, HALF, "raw_b")
-        gated = gather_on_vector("gated_first", 0, QUARTER, gate_first, first_cuts=(FIRST_GATE,))
-        x_bf = rounded("x_first", HALF)
-        gate_and_round(x_bf[:, part:], raw1[:], QUARTER, HALF)
+        gather_on_vector(gated_first, 0, QUARTER, gate_first, first_cuts=(FIRST_GATE,))
+        x_first = rounded("x_first", HALF)
+        gate_and_round(x_first[:, part:], raw1[:], QUARTER, HALF)
         w_0 = rounded("w_0", C, after="gate_first")
         round_w_on_gpsimd(w_0[:], 0)
         raw3 = gather_on_scalar(0, HALF, own, "raw_a")
-        round_x(x_bf[:, 0:part], gated[:])
-        gated = gather_on_vector("gated_last", own, S, gate_last)
-        quantize_x(x_bf[:], 0, 0, HALF)
-        x_own = rounded("x_own", QUARTER)
-        round_x(x_own[:], gated[:])
-        x_bf = rounded("x_second", HALF + QUARTER, after="gate_last")
-        for i in range(2):
-            gate_and_round(x_bf[:, i * part : (i + 1) * part], raw2[:, :, i * QUARTER : (i + 1) * QUARTER], i * QUARTER, (i + 1) * QUARTER)
-        w_123 = rounded("w_123", 3 * C, after="gated_last")
-        for i in range(3):
-            round_w_on_gpsimd(w_123[:, i * one : (i + 1) * one], 1 + i)
-        raw4 = gather_on_scalar(1, HALF, own, "raw_b")
-        quantize_x(x_own[:], 0, own, S)
-        gate_and_round(x_bf[:, 2 * part :], raw3[:], HALF, own)
-        w_4 = rounded("w_4", C, after="x_own")
-        round_w_on_gpsimd(w_4[:], 4)
-        raw5 = gather_on_scalar(1, own, S, "raw_a")
-        quantize_x(x_bf[:, 0 : 2 * part], 1, 0, HALF)
+        round_x(x_first[:, 0:part], gated_first[:])
+
+        mid = keep.tile([P, 3 * last], BF16, name="mid", align_bytes=MX_ALIGN)
+        gated_last = mid[:, last:].bitcast(F32).rearrange("p (j s) -> p j s", j=PACK)
+        gather_on_vector(gated_last, own, S, gate_last)
+        quantize_x(x_first[:], 0, 0, HALF)
         quantize_w(w_0[:], 0, 1)
-        quantize_w(w_123[:, 0:one], 1, 2)
-        quantize_w(w_123[:, one:], 2, 4)
-        gate_and_round(x_bf[:, 0:part], raw4[:], HALF, own)
-        w_5 = rounded("w_5", C, after="gated_last")
-        round_w_on_gpsimd(w_5[:], 5)
-        quantize_x(x_bf[:, 2 * part :], 0, HALF, own)
-        w_67 = rounded("w_67", 2 * C, after="x_first")
+        round_x(mid[:, 0:last], gated_last)
+        x_second = rounded("x_second", HALF, after="gate_last")
+        for i in range(2):
+            gate_and_round(x_second[:, i * part : (i + 1) * part], raw2[:, :, i * QUARTER : (i + 1) * QUARTER], i * QUARTER, (i + 1) * QUARTER)
+        for i in range(2):
+            round_w_on_gpsimd(mid[:, last + i * one : last + (i + 1) * one], 1 + i)
+        round_w_on_gpsimd(mid[:, last + part : last + part + half], 3, 0, 1)
+        raw4 = gather_on_scalar(1, HALF, sixth, "raw_b")
+        runs = [("x", 0, s) for s in range(own, S, P)] + [("w", e, g) for e in (1, 2) for g in range(PASSES)] + [("w", 3, 0)]
+        quantize(mid[:, 0 : 2 * part], runs, "packed_mid")
+        quantize_x(x_second[:], 1, 0, HALF)
+        gate_and_round(mid[:, 0:part], raw3[:, :, 0:QUARTER], HALF, sixth)
+        gate_and_round(mid[:, part : part + half], raw3[:, :, QUARTER:], sixth, own)
+        round_w_on_gpsimd(x_second[:, 0:half], 3, 1, 2)
+        round_w_on_gpsimd(x_second[:, half : half + one], 4)
+        raw5 = gather_on_scalar(1, sixth, S, "raw_a")
+        quantize_x(mid[:, 0:part], 0, HALF, sixth)
+        w_67 = mid[:, part + half :]
         nc.vector.tensor_copy(
-            w_67[:].rearrange("p (m c i j) -> p m c j i", i=RUN, j=PACK, c=N // RUN),
+            w_67.rearrange("p (m c i j) -> p m c j i", i=RUN, j=PACK, c=N // RUN),
             w_raw_last[:].rearrange("p m j (c i) -> p m c j i", i=RUN),
         )
-        quantize_x(x_bf[:, 0:part], 1, HALF, own)
-        quantize_w(w_4[:], 4, 5)
+        quantize_x(mid[:, part : part + half], 0, sixth, own)
+        gate_and_round(mid[:, 0:part], raw4[:], HALF, sixth)
+        w_5 = rounded("w_5", C, after="w_raw_last")
+        round_w_on_gpsimd(w_5[:], 5)
+        quantize(x_second[:, 0 : half + one], [("w", 3, 1), ("w", 4, 0), ("w", 4, 1)], "w_packed4")
         quantize_w(w_5[:], 5, 6)
-        quantize_w(w_67[:], 6, 8)
+        quantize_x(mid[:, 0:part], 1, HALF, sixth)
+        quantize_w(w_67, 6, 8)
+        x_fifth = rounded("x_fifth", QUARTER, after="w_raw_last")
         for i in range(2):
-            gate_and_round(x_bf[:, i * one : (i + 1) * one], raw5[:, :, i * C : (i + 1) * C], own + i * C, own + (i + 1) * C)
+            gate_and_round(x_fifth[:, i * one : (i + 1) * one], raw5[:, :, i * C : (i + 1) * C], sixth + i * C, sixth + (i + 1) * C)
         for i in range(2):
-            quantize_x(x_bf[:, i * one : (i + 1) * one], 1, own + i * C, own + (i + 1) * C)
+            quantize_x(x_fifth[:, i * one : (i + 1) * one], 1, sixth + i * C, sixth + (i + 1) * C)
 
         y = keep.tile([P, S], F32, name="y", tag="x_rows1_2", align_bytes=MX_ALIGN)
 
@@ -236,10 +243,14 @@ def tile_moe_pre_lin_relu_kernel(tc, xT, w, b, gate, offs, pos1, pos2, pos3, pos
                 multiply(acc[:, i * C : (i + 1) * C], (2 * pair + i) * C, (2 * pair + i + 1) * C)
             for i in range(2):
                 finish(2 * pair + i, acc[:, i * C : (i + 1) * C])
-        for e, tag in ((6, "sums3"), (7, "gate_bank0")):
-            acc = psum.tile([P, C], F32, name="sum%d" % e, tag=tag)
-            multiply(acc[:], e * C, (e + 1) * C)
-            finish(e, acc[:])
+        acc = psum.tile([P, C], F32, name="sum6")
+        multiply(acc[:, 0:P], sixth, own, passes=(0,), stop=False)
+        multiply(acc[:, P:], own, own + P, passes=(0,), start=False, stop=False)
+        multiply(acc[:], sixth, 7 * C, passes=(1,), start=False)
+        finish(6, acc[:])
+        acc = psum.tile([P, C], F32, name="sum7", tag="gate_bank0")
+        multiply(acc[:], 7 * C, S)
+        finish(7, acc[:])
 
         halves = [slice(0, T // 2), slice(T // 2, T)]
 

@@ -30,6 +30,7 @@ HALF = S // 2
 QUARTER = S // 4
 WINDOW = HALF + STRIPE
 FIRST_GATE = 128
+W_TURNS = (0, 2, 8, 11, 13, 14, 16)
 
 
 def tile_moe_pre_lin_relu_kernel(tc, xT, w, b, gate, offs, pos1, pos2, pos3, pos4, out):
@@ -50,8 +51,10 @@ def tile_moe_pre_lin_relu_kernel(tc, xT, w, b, gate, offs, pos1, pos2, pos3, pos
             [keep.tile([P, WINDOW], F32, name="x_rows%d_%d" % (g, j), align_bytes=MX_ALIGN) for j in range(PACK)]
             for g in range(PASSES)
         ]
-        w_raw = [keep.tile([P, PASSES, PACK, N], F32, name="w_raw%d" % e, align_bytes=MX_ALIGN) for e in range(E - 2)]
-        w_raw_last = keep.tile([P, 2 * PASSES, PACK, N], F32, name="w_raw_last", align_bytes=MX_ALIGN)
+        w_raw = [
+            keep.tile([P, q1 - q0, PACK, N], F32, name="w_raw%d" % i, align_bytes=MX_ALIGN)
+            for i, (q0, q1) in enumerate(zip(W_TURNS, W_TURNS[1:]))
+        ]
         bias = keep.tile([P, E], F32, name="bias")
         packed = {}
 
@@ -60,12 +63,13 @@ def tile_moe_pre_lin_relu_kernel(tc, xT, w, b, gate, offs, pos1, pos2, pos3, pos
         def load_x(g, j):
             nc.sync.dma_start(out=x_rows[g][j][:, 0:T], in_=x_view[g, j])
 
-        def load_w(e):
-            dst = w_raw[e][:] if e < E - 2 else w_raw_last[:, (e - E + 2) * PASSES : (e - E + 3) * PASSES]
-            nc.sync.dma_start(
-                out=dst.rearrange("p g j n -> p g (j n)"),
-                in_=w[e].rearrange("(g p j) n -> p g (j n)", g=PASSES, j=PACK),
-            )
+        w_view = w.rearrange("e (g p j) n -> p (e g) (j n)", g=PASSES, j=PACK)
+
+        def load_w(turn):
+            first, end = W_TURNS[turn], W_TURNS[turn + 1]
+            for q0 in range(first, end, 2):
+                q1 = min(q0 + 2, end)
+                nc.sync.dma_start(out=w_raw[turn][:, q0 - first : q1 - first].rearrange("p q j n -> p q (j n)"), in_=w_view[:, q0:q1])
 
         warm = keep.tile([P, 2], F32, name="warm")
         nc.gpsimd.memset(warm[:, 0:1], 0.0)
@@ -89,8 +93,8 @@ def tile_moe_pre_lin_relu_kernel(tc, xT, w, b, gate, offs, pos1, pos2, pos3, pos
         nc.sync.dma_start(out=bias[:], in_=b)
         for r, pos in enumerate((pos1, pos2, pos3, pos4)):
             nc.sync.dma_start(token_slot[r][:], pos)
-        for e in range(1, E):
-            load_w(e)
+        for turn in range(1, len(w_raw)):
+            load_w(turn)
 
         turned = psum.tile([P, P], F32, name="turned", tag="sums0")
         nc.tensor.transpose(turned[:], gate_runs, identity[:])
@@ -112,10 +116,11 @@ def tile_moe_pre_lin_relu_kernel(tc, xT, w, b, gate, offs, pos1, pos2, pos3, pos
         def rows(src):
             return src.rearrange("p j (c i) -> p c j i", i=RUN)
 
-        def gather_on_scalar(g, s0, s1, tag):
-            raw = keep.tile([P, PACK, s1 - s0], F32, name="raw%d_%d" % (g, s0), tag=tag, align_bytes=MX_ALIGN)
-            for j in range(PACK):
-                nc.scalar.activation(raw[:, j, :], tokens(g, j, s0, s1), COPY)
+        def gather_on_scalar(g, cuts, tag):
+            raw = keep.tile([P, PACK, cuts[-1] - cuts[0]], F32, name="raw%d_%d" % (g, cuts[0]), tag=tag, align_bytes=MX_ALIGN)
+            for s0, s1 in zip(cuts, cuts[1:]):
+                for j in range(PACK):
+                    nc.scalar.activation(raw[:, j, s0 - cuts[0] : s1 - cuts[0]], tokens(g, j, s0, s1), COPY)
             return raw
 
         def rounded(name, columns, after=None):
@@ -136,10 +141,10 @@ def tile_moe_pre_lin_relu_kernel(tc, xT, w, b, gate, offs, pos1, pos2, pos3, pos
         def round_x(dst, gated):
             nc.vector.tensor_copy(words(dst), rows(gated))
 
-        def round_w_on_gpsimd(dst, e, g0=0, g1=PASSES):
+        def round_w_on_gpsimd(dst, turn):
             nc.gpsimd.tensor_scalar(
-                out=dst.rearrange("p (g n j) -> p g n j", n=N, j=PACK),
-                in0=w_raw[e][:, g0:g1].rearrange("p g j n -> p g n j"),
+                out=dst.rearrange("p (q n j) -> p q n j", n=N, j=PACK),
+                in0=w_raw[turn][:].rearrange("p q j n -> p q n j"),
                 scalar1=1.0,
                 scalar2=0.0,
                 op0=MULT,
@@ -154,8 +159,8 @@ def tile_moe_pre_lin_relu_kernel(tc, xT, w, b, gate, offs, pos1, pos2, pos3, pos
             for i, run in enumerate(runs):
                 packed[run] = (codes, scales, i * P)
 
-        def quantize_w(src, e0, e1, after=None):
-            quantize(src, [("w", e, g) for e in range(e0, e1) for g in range(PASSES)], "w_packed%d" % e0, after)
+        def w_runs(q0, q1):
+            return [("w", q // PASSES, q % PASSES) for q in range(q0, q1)]
 
         def quantize_x(src, g, s0, s1):
             quantize(src, [("x", g, s) for s in range(s0, s1, P)], "x_packed%d_%d" % (g, s0))
@@ -181,76 +186,79 @@ def tile_moe_pre_lin_relu_kernel(tc, xT, w, b, gate, offs, pos1, pos2, pos3, pos
         half = one // PASSES
         last = (S - own) * PACK
 
-        raw1 = gather_on_scalar(0, QUARTER, HALF, "raw_a")
-        raw2 = gather_on_scalar(1, 0, HALF, "raw_b")
+        seventh = 7 * C
+        raw1 = gather_on_scalar(0, (QUARTER, HALF), "raw_a")
+        raw2 = gather_on_scalar(1, (0, HALF), "raw_b")
         gather_on_vector(gated_first, 0, QUARTER, gate_first, first_cuts=(FIRST_GATE,))
         x_first = rounded("x_first", HALF)
         gate_and_round(x_first[:, part:], raw1[:], QUARTER, HALF)
         w_0 = rounded("w_0", C, after="gate_first")
         round_w_on_gpsimd(w_0[:], 0)
-        raw3 = gather_on_scalar(0, HALF, own, "raw_a")
+        raw3 = gather_on_scalar(0, (HALF, own), "raw_a")
         round_x(x_first[:, 0:part], gated_first[:])
 
         mid = keep.tile([P, 3 * last], BF16, name="mid", align_bytes=MX_ALIGN)
         gated_last = mid[:, last:].bitcast(F32).rearrange("p (j s) -> p j s", j=PACK)
         gather_on_vector(gated_last, own, S, gate_last)
         quantize_x(x_first[:], 0, 0, HALF)
-        quantize_w(w_0[:], 0, 1)
+        quantize(w_0[:], w_runs(0, 2), "w_packed0")
         round_x(mid[:, 0:last], gated_last)
         x_second = rounded("x_second", HALF, after="gate_last")
         for i in range(2):
             gate_and_round(x_second[:, i * part : (i + 1) * part], raw2[:, :, i * QUARTER : (i + 1) * QUARTER], i * QUARTER, (i + 1) * QUARTER)
-        for i in range(2):
-            round_w_on_gpsimd(mid[:, last + i * one : last + (i + 1) * one], 1 + i)
-        round_w_on_gpsimd(mid[:, last + part : last + part + half], 3, 0, 1)
-        raw4 = gather_on_scalar(1, HALF, sixth, "raw_b")
-        runs = [("x", 0, s) for s in range(own, S, P)] + [("w", e, g) for e in (1, 2) for g in range(PASSES)] + [("w", 3, 0)]
-        quantize(mid[:, 0 : 2 * part], runs, "packed_mid")
+        round_w_on_gpsimd(mid[:, last:], 1)
+        raw4 = gather_on_scalar(1, (HALF, sixth), "raw_b")
+        quantize(mid[:, 0 : 2 * part], [("x", 0, s) for s in range(own, S, P)] + w_runs(2, 7), "packed_mid")
         quantize_x(x_second[:], 1, 0, HALF)
         gate_and_round(mid[:, 0:part], raw3[:, :, 0:QUARTER], HALF, sixth)
         gate_and_round(mid[:, part : part + half], raw3[:, :, QUARTER:], sixth, own)
-        round_w_on_gpsimd(x_second[:, 0:half], 3, 1, 2)
-        round_w_on_gpsimd(x_second[:, half : half + one], 4)
-        raw5 = gather_on_scalar(1, sixth, S, "raw_a")
+        round_w_on_gpsimd(x_second[:, 0 : 3 * half], 2)
+        raw5 = gather_on_scalar(1, (sixth, seventh, S), "raw_a")
         quantize_x(mid[:, 0:part], 0, HALF, sixth)
-        w_67 = mid[:, part + half :]
         nc.vector.tensor_copy(
-            w_67.rearrange("p (m c i j) -> p m c j i", i=RUN, j=PACK, c=N // RUN),
-            w_raw_last[:].rearrange("p m j (c i) -> p m c j i", i=RUN),
+            mid[:, 2 * part - one : 2 * part].rearrange("p (q c i j) -> p q c j i", i=RUN, j=PACK, c=N // RUN),
+            w_raw[5][:].rearrange("p q j (c i) -> p q c j i", i=RUN),
         )
         quantize_x(mid[:, part : part + half], 0, sixth, own)
         gate_and_round(mid[:, 0:part], raw4[:], HALF, sixth)
-        w_5 = rounded("w_5", C, after="w_raw_last")
-        round_w_on_gpsimd(w_5[:], 5)
-        quantize(x_second[:, 0 : half + one], [("w", 3, 1), ("w", 4, 0), ("w", 4, 1)], "w_packed4")
-        quantize_w(w_5[:], 5, 6)
+        w_3 = rounded("w_3", C, after="w_raw5")
+        round_w_on_gpsimd(w_3[:], 3)
+        quantize(x_second[:, 0 : 3 * half], w_runs(8, 11), "w_packed2")
+        quantize(mid[:, 2 * part - one :], w_runs(14, 16) + w_runs(7, 8), "w_packed5")
+        quantize(w_3[:], w_runs(11, 13), "w_packed3")
         quantize_x(mid[:, 0:part], 1, HALF, sixth)
-        quantize_w(w_67, 6, 8)
-        x_fifth = rounded("x_fifth", QUARTER, after="w_raw_last")
+        x_fifth = rounded("x_fifth", C, after="w_raw5")
+        gate_and_round(x_fifth[:], raw5[:, :, 0:C], sixth, seventh)
+        round_w_on_gpsimd(mid[:, 0:half], 4)
+        quantize_x(x_fifth[:], 1, sixth, seventh)
+        quantize(mid[:, 0:half], w_runs(13, 14), "w_packed4")
+        x_last = (mid[:, 0:half], x_fifth[:, 0:half])
         for i in range(2):
-            gate_and_round(x_fifth[:, i * one : (i + 1) * one], raw5[:, :, i * C : (i + 1) * C], sixth + i * C, sixth + (i + 1) * C)
+            gate_and_round(x_last[i], raw5[:, :, C + i * P : C + (i + 1) * P], seventh + i * P, seventh + (i + 1) * P)
         for i in range(2):
-            quantize_x(x_fifth[:, i * one : (i + 1) * one], 1, sixth + i * C, sixth + (i + 1) * C)
+            quantize_x(x_last[i], 1, seventh + i * P, seventh + (i + 1) * P)
 
         y = keep.tile([P, S], F32, name="y", tag="x_rows1_2", align_bytes=MX_ALIGN)
 
-        def finish(e, acc):
-            nc.scalar.activation(out=y[:, e * C : (e + 1) * C], in_=acc, func=RELU, bias=bias[:, e : e + 1])
+        def finish(s0, s1, acc):
+            e = s0 // C
+            nc.scalar.activation(out=y[:, s0:s1], in_=acc, func=RELU, bias=bias[:, e : e + 1])
 
         for pair in range(3):
             acc = psum.tile([P, 2 * C], F32, name="sums%d" % pair)
             for i in range(2):
                 multiply(acc[:, i * C : (i + 1) * C], (2 * pair + i) * C, (2 * pair + i + 1) * C)
             for i in range(2):
-                finish(2 * pair + i, acc[:, i * C : (i + 1) * C])
+                finish((2 * pair + i) * C, (2 * pair + i + 1) * C, acc[:, i * C : (i + 1) * C])
         acc = psum.tile([P, C], F32, name="sum6")
         multiply(acc[:, 0:P], sixth, own, passes=(0,), stop=False)
         multiply(acc[:, P:], own, own + P, passes=(0,), start=False, stop=False)
         multiply(acc[:], sixth, 7 * C, passes=(1,), start=False)
-        finish(6, acc[:])
-        acc = psum.tile([P, C], F32, name="sum7", tag="gate_bank0")
-        multiply(acc[:], 7 * C, S)
-        finish(7, acc[:])
+        finish(sixth, seventh, acc[:])
+        for i in range(2):
+            acc = psum.tile([P, P], F32, name="sum7_%d" % i, tag="gate_bank%d" % i)
+            multiply(acc[:], seventh + i * P, seventh + (i + 1) * P)
+            finish(seventh + i * P, seventh + (i + 1) * P, acc[:])
 
         halves = [slice(0, T // 2), slice(T // 2, T)]
 

@@ -29,8 +29,8 @@ RUN = 4
 HALF = S // 2
 QUARTER = S // 4
 WINDOW = HALF + STRIPE
-FIRST_GATE = 128
-W_TURNS = (0, 2, 8, 11, 13, 14, 16)
+W_TURNS = ((range(8, 11, 2),), (range(0, 2), range(2, 4), range(4, 6), range(6, 8)), (range(13, 16, 2),), (range(9, 12, 2), range(12, 15, 2)))
+OWN = S - C - P
 
 
 def tile_moe_pre_lin_relu_kernel(tc, xT, w, b, gate, offs, pos1, pos2, pos3, pos4, out):
@@ -42,9 +42,9 @@ def tile_moe_pre_lin_relu_kernel(tc, xT, w, b, gate, offs, pos1, pos2, pos3, pos
         slot_token = keep.tile([P, S // STRIPE], U16, name="slot_token")
         token_slot = [keep.tile([P, T // STRIPE], U16, name="token_slot%d" % r) for r in range(TOP)]
         gate_first = keep.tile([P, QUARTER], F32, name="gate_first", align_bytes=MX_ALIGN)
-        gate_last = keep.tile([P, C + P], F32, name="gate_last", align_bytes=MX_ALIGN)
-        gated_first = keep.tile([P, PACK, QUARTER], F32, name="gated_first", align_bytes=MX_ALIGN)
-        gate_runs = gated_first[:, 2, 0:P]
+        raw_first = keep.tile([P, PACK, QUARTER], F32, name="raw_first", align_bytes=MX_ALIGN)
+        raw_last = keep.tile([P, PACK, S - OWN], F32, name="raw_last", align_bytes=MX_ALIGN)
+        gate_runs = raw_last[:, 0, 0:P]
         gate_columns = keep.tile([P, S // P], F32, name="gate_columns")
         identity = keep.tile([P, P], F32, name="identity")
         x_rows = [
@@ -52,8 +52,8 @@ def tile_moe_pre_lin_relu_kernel(tc, xT, w, b, gate, offs, pos1, pos2, pos3, pos
             for g in range(PASSES)
         ]
         w_raw = [
-            keep.tile([P, q1 - q0, PACK, N], F32, name="w_raw%d" % i, align_bytes=MX_ALIGN)
-            for i, (q0, q1) in enumerate(zip(W_TURNS, W_TURNS[1:]))
+            keep.tile([P, sum(len(load) for load in turn), PACK, N], F32, name="w_raw%d" % i, align_bytes=MX_ALIGN)
+            for i, turn in enumerate(W_TURNS)
         ]
         bias = keep.tile([P, E], F32, name="bias")
         packed = {}
@@ -66,30 +66,28 @@ def tile_moe_pre_lin_relu_kernel(tc, xT, w, b, gate, offs, pos1, pos2, pos3, pos
         w_view = w.rearrange("e (g p j) n -> p (e g) (j n)", g=PASSES, j=PACK)
 
         def load_w(turn):
-            first, end = W_TURNS[turn], W_TURNS[turn + 1]
-            for q0 in range(first, end, 2):
-                q1 = min(q0 + 2, end)
-                nc.sync.dma_start(out=w_raw[turn][:, q0 - first : q1 - first].rearrange("p q j n -> p q (j n)"), in_=w_view[:, q0:q1])
+            first = 0
+            for load in W_TURNS[turn]:
+                dst = w_raw[turn][:, first : first + len(load)].rearrange("p q j n -> p q (j n)")
+                nc.sync.dma_start(out=dst, in_=w_view[:, load.start : load.stop : load.step])
+                first = first + len(load)
 
         warm = keep.tile([P, 2], F32, name="warm")
         nc.gpsimd.memset(warm[:, 0:1], 0.0)
         nc.scalar.activation(warm[:, 1:2], warm[:, 0:1], COPY)
 
         make_identity(nc, identity[:])
-        own = S - C - P
 
         load_x(0, 0)
         nc.sync.dma_start(slot_token[:], offs)
-        nc.sync.dma_start(out=gate_first[:, 0:FIRST_GATE], in_=gate[0:P, 0:FIRST_GATE])
-        nc.sync.dma_start(out=gate_first[:, FIRST_GATE:], in_=gate[0:P, FIRST_GATE:QUARTER])
         load_x(0, 1)
         nc.sync.dma_start(out=gate_runs, in_=gate[0 : P * P // S, :].rearrange("r (c s) -> (r c) s", s=P))
         load_x(0, 2)
         load_x(0, 3)
         load_w(0)
+        nc.sync.dma_start(out=gate_first[:], in_=gate[0:P, 0:QUARTER])
         for j in range(PACK):
             load_x(1, j)
-        nc.sync.dma_start(out=gate_last[:], in_=gate[0:P, own:S])
         nc.sync.dma_start(out=bias[:], in_=b)
         for r, pos in enumerate((pos1, pos2, pos3, pos4)):
             nc.sync.dma_start(token_slot[r][:], pos)
@@ -100,7 +98,7 @@ def tile_moe_pre_lin_relu_kernel(tc, xT, w, b, gate, offs, pos1, pos2, pos3, pos
         nc.tensor.transpose(turned[:], gate_runs, identity[:])
         nc.vector.tensor_copy(gate_columns[:], turned[:, 0 : S // P])
         gate_banks = [psum.tile([P, QUARTER], F32, name="gate_bank%d" % i) for i in range(S // QUARTER)]
-        for i in (1, 0, 2, 3):
+        for i in (1, 3, 0, 2):
             for c in range(QUARTER // P):
                 column = i * QUARTER // P + c
                 nc.tensor.transpose(
@@ -117,11 +115,14 @@ def tile_moe_pre_lin_relu_kernel(tc, xT, w, b, gate, offs, pos1, pos2, pos3, pos
             return src.rearrange("p j (c i) -> p c j i", i=RUN)
 
         def gather_on_scalar(g, cuts, tag):
-            raw = keep.tile([P, PACK, cuts[-1] - cuts[0]], F32, name="raw%d_%d" % (g, cuts[0]), tag=tag, align_bytes=MX_ALIGN)
+            raw = keep.tile([P, (cuts[-1] - cuts[0]) * PACK], F32, name="raw%d_%d" % (g, cuts[0]), tag=tag, align_bytes=MX_ALIGN)
+            steps = []
             for s0, s1 in zip(cuts, cuts[1:]):
+                step = raw[:, (s0 - cuts[0]) * PACK : (s1 - cuts[0]) * PACK].rearrange("p (j s) -> p j s", j=PACK)
                 for j in range(PACK):
-                    nc.scalar.activation(raw[:, j, s0 - cuts[0] : s1 - cuts[0]], tokens(g, j, s0, s1), COPY)
-            return raw
+                    nc.scalar.activation(step[:, j, :], tokens(g, j, s0, s1), COPY)
+                steps.append(step)
+            return steps
 
         def rounded(name, columns, after=None):
             return keep.tile([P, columns * PACK], BF16, name=name, tag=after or name, align_bytes=MX_ALIGN)
@@ -132,14 +133,9 @@ def tile_moe_pre_lin_relu_kernel(tc, xT, w, b, gate, offs, pos1, pos2, pos3, pos
             spread = gates.rearrange("p (c i) -> p c i", i=RUN).unsqueeze(2).to_broadcast([P, n, PACK, RUN])
             nc.vector.tensor_tensor(words(dst), rows(raw), spread, MULT)
 
-        def gather_on_vector(gated, s0, s1, gates, first_cuts=()):
+        def gather_on_vector(raw, g, s0, s1):
             for j in range(PACK):
-                cuts = (s0,) + (first_cuts if j == 0 else ()) + (s1,)
-                for a, z in zip(cuts, cuts[1:]):
-                    nc.vector.tensor_tensor(gated[:, j, a - s0 : z - s0], tokens(0, j, a, z), gates[:, a - s0 : z - s0], MULT)
-
-        def round_x(dst, gated):
-            nc.vector.tensor_copy(words(dst), rows(gated))
+                nc.vector.tensor_copy(raw[:, j, :], tokens(g, j, s0, s1))
 
         def round_w_on_gpsimd(dst, turn):
             nc.gpsimd.tensor_scalar(
@@ -159,8 +155,8 @@ def tile_moe_pre_lin_relu_kernel(tc, xT, w, b, gate, offs, pos1, pos2, pos3, pos
             for i, run in enumerate(runs):
                 packed[run] = (codes, scales, i * P)
 
-        def w_runs(q0, q1):
-            return [("w", q // PASSES, q % PASSES) for q in range(q0, q1)]
+        def w_runs(turn):
+            return [("w", q // PASSES, q % PASSES) for load in W_TURNS[turn] for q in load]
 
         def quantize_x(src, g, s0, s1):
             quantize(src, [("x", g, s) for s in range(s0, s1, P)], "x_packed%d_%d" % (g, s0))
@@ -182,82 +178,83 @@ def tile_moe_pre_lin_relu_kernel(tc, xT, w, b, gate, offs, pos1, pos2, pos3, pos
         part = QUARTER * PACK
         one = C * PACK
 
-        sixth = 6 * C
         half = one // PASSES
-        last = (S - own) * PACK
+        sixth, seventh = 6 * C, 7 * C
 
-        seventh = 7 * C
-        raw1 = gather_on_scalar(0, (QUARTER, HALF), "raw_a")
-        raw2 = gather_on_scalar(1, (0, HALF), "raw_b")
-        gather_on_vector(gated_first, 0, QUARTER, gate_first, first_cuts=(FIRST_GATE,))
-        x_first = rounded("x_first", HALF)
-        gate_and_round(x_first[:, part:], raw1[:], QUARTER, HALF)
-        w_0 = rounded("w_0", C, after="gate_first")
-        round_w_on_gpsimd(w_0[:], 0)
-        raw3 = gather_on_scalar(0, (HALF, own), "raw_a")
-        round_x(x_first[:, 0:part], gated_first[:])
+        def x_runs(g, s0, s1):
+            return [("x", g, s) for s in range(s0, s1, P)]
 
-        mid = keep.tile([P, 3 * last], BF16, name="mid", align_bytes=MX_ALIGN)
-        gated_last = mid[:, last:].bitcast(F32).rearrange("p (j s) -> p j s", j=PACK)
-        gather_on_vector(gated_last, own, S, gate_last)
-        quantize_x(x_first[:], 0, 0, HALF)
-        quantize(w_0[:], w_runs(0, 2), "w_packed0")
-        round_x(mid[:, 0:last], gated_last)
-        x_second = rounded("x_second", HALF, after="gate_last")
-        for i in range(2):
-            gate_and_round(x_second[:, i * part : (i + 1) * part], raw2[:, :, i * QUARTER : (i + 1) * QUARTER], i * QUARTER, (i + 1) * QUARTER)
-        round_w_on_gpsimd(mid[:, last:], 1)
-        raw4 = gather_on_scalar(1, (HALF, sixth), "raw_b")
-        quantize(mid[:, 0 : 2 * part], [("x", 0, s) for s in range(own, S, P)] + w_runs(2, 7), "packed_mid")
-        quantize_x(x_second[:], 1, 0, HALF)
-        gate_and_round(mid[:, 0:part], raw3[:, :, 0:QUARTER], HALF, sixth)
-        gate_and_round(mid[:, part : part + half], raw3[:, :, QUARTER:], sixth, own)
-        round_w_on_gpsimd(x_second[:, 0 : 3 * half], 2)
-        raw5 = gather_on_scalar(1, (sixth, seventh, S), "raw_a")
-        quantize_x(mid[:, 0:part], 0, HALF, sixth)
-        nc.vector.tensor_copy(
-            mid[:, 2 * part - one : 2 * part].rearrange("p (q c i j) -> p q c j i", i=RUN, j=PACK, c=N // RUN),
-            w_raw[5][:].rearrange("p q j (c i) -> p q c j i", i=RUN),
+        def runs(tile, first, count):
+            return tile[:, first * half : (first + count) * half]
+
+        (raw1,) = gather_on_scalar(0, (QUARTER, HALF), "raw_a")
+        (raw2,) = gather_on_scalar(1, (0, HALF), "raw_b")
+        gather_on_vector(raw_first, 0, 0, QUARTER)
+        early = rounded("early", 11 * P)
+        round_w_on_gpsimd(runs(early, 1, 2), 0)
+        nc.gpsimd.tensor_tensor(
+            runs(early, 3, 4).rearrange("p (s j) -> p s j", j=PACK),
+            raw_first[:].rearrange("p j s -> p s j"),
+            gate_first[:].unsqueeze(2).to_broadcast([P, QUARTER, PACK]),
+            MULT,
         )
-        quantize_x(mid[:, part : part + half], 0, sixth, own)
-        gate_and_round(mid[:, 0:part], raw4[:], HALF, sixth)
-        w_3 = rounded("w_3", C, after="w_raw5")
-        round_w_on_gpsimd(w_3[:], 3)
-        quantize(x_second[:, 0 : 3 * half], w_runs(8, 11), "w_packed2")
-        quantize(mid[:, 2 * part - one :], w_runs(14, 16) + w_runs(7, 8), "w_packed5")
-        quantize(w_3[:], w_runs(11, 13), "w_packed3")
-        quantize_x(mid[:, 0:part], 1, HALF, sixth)
-        x_fifth = rounded("x_fifth", C, after="w_raw5")
-        gate_and_round(x_fifth[:], raw5[:, :, 0:C], sixth, seventh)
-        round_w_on_gpsimd(mid[:, 0:half], 4)
-        quantize_x(x_fifth[:], 1, sixth, seventh)
-        quantize(mid[:, 0:half], w_runs(13, 14), "w_packed4")
-        x_last = (mid[:, 0:half], x_fifth[:, 0:half])
-        for i in range(2):
-            gate_and_round(x_last[i], raw5[:, :, C + i * P : C + (i + 1) * P], seventh + i * P, seventh + (i + 1) * P)
-        for i in range(2):
-            quantize_x(x_last[i], 1, seventh + i * P, seventh + (i + 1) * P)
+        gather_on_vector(raw_last, 1, OWN, S)
+        gate_and_round(runs(early, 7, 4), raw1, QUARTER, HALF)
+        (raw3,) = gather_on_scalar(0, (HALF, sixth), "raw_first")
+        quantize_x(runs(early, 3, 8), 0, 0, HALF)
 
-        y = keep.tile([P, S], F32, name="y", tag="x_rows1_2", align_bytes=MX_ALIGN)
+        round_w_on_gpsimd(runs(early, 3, 8), 1)
+        late = rounded("late", 11 * P, after="gate_first")
+        gate_and_round(runs(late, 8, 3), raw_last[:], OWN, S)
+        for i in range(2):
+            gate_and_round(runs(late, 4 * i, 4), raw2[:, :, i * QUARTER : (i + 1) * QUARTER], i * QUARTER, (i + 1) * QUARTER)
+        (raw4,) = gather_on_scalar(1, (HALF, OWN), "raw_b")
+        quantize_x(runs(late, 8, 3), 1, OWN, S)
+        quantize(runs(early, 3, 8), w_runs(1), "packed_w1")
+        quantize_x(runs(late, 0, 8), 1, 0, HALF)
+
+        round_w_on_gpsimd(runs(early, 3, 2), 2)
+        gate_and_round(runs(early, 7, 4), raw3, HALF, sixth)
+        raw5, raw6 = gather_on_scalar(0, (sixth, seventh, S), "raw_first")
+        quantize(runs(early, 1, 4), w_runs(0) + w_runs(2), "packed_w2")
+        quantize_x(runs(early, 7, 4), 0, HALF, sixth)
+
+        round_w_on_gpsimd(runs(early, 7, 4), 3)
+        gate_and_round(runs(early, 3, 4), raw4[:, :, 0:QUARTER], HALF, sixth)
+        gate_and_round(runs(early, 2, 1), raw4[:, :, QUARTER:], sixth, OWN)
+        gate_and_round(runs(early, 0, 2), raw5, sixth, seventh)
+        quantize(runs(early, 7, 4), w_runs(3), "packed_w3")
+        quantize_x(runs(early, 3, 4), 1, HALF, sixth)
+        quantize(runs(early, 0, 3), x_runs(0, sixth, seventh) + x_runs(1, sixth, OWN), "packed_sixth")
+        for i in range(2):
+            gate_and_round(runs(early, 7 + i, 1), raw6[:, :, i * P : (i + 1) * P], seventh + i * P, seventh + (i + 1) * P)
+        for i in range(2):
+            quantize_x(runs(early, 7 + i, 1), 0, seventh + i * P, seventh + (i + 1) * P)
+
+        y = keep.tile([P, S], F32, name="y", tag="x_rows0_2", align_bytes=MX_ALIGN)
 
         def finish(s0, s1, acc):
             e = s0 // C
             nc.scalar.activation(out=y[:, s0:s1], in_=acc, func=RELU, bias=bias[:, e : e + 1])
 
-        for pair in range(3):
+        for pair in range(2):
             acc = psum.tile([P, 2 * C], F32, name="sums%d" % pair)
             for i in range(2):
                 multiply(acc[:, i * C : (i + 1) * C], (2 * pair + i) * C, (2 * pair + i + 1) * C)
             for i in range(2):
                 finish((2 * pair + i) * C, (2 * pair + i + 1) * C, acc[:, i * C : (i + 1) * C])
-        acc = psum.tile([P, C], F32, name="sum6")
-        multiply(acc[:, 0:P], sixth, own, passes=(0,), stop=False)
-        multiply(acc[:, P:], own, own + P, passes=(0,), start=False, stop=False)
-        multiply(acc[:], sixth, 7 * C, passes=(1,), start=False)
+        for e in (4, 5):
+            acc = psum.tile([P, C], F32, name="sums%d" % (e - 2))
+            multiply(acc[:], e * C, (e + 1) * C)
+            finish(e * C, (e + 1) * C, acc[:])
+        acc = psum.tile([P, C], F32, name="sum6", tag="gate_bank0")
+        multiply(acc[:, P:], OWN, seventh, passes=(1,), stop=False)
+        multiply(acc[:, 0:P], sixth, OWN, passes=(1,), start=False, stop=False)
+        multiply(acc[:], sixth, seventh, passes=(0,), start=False)
         finish(sixth, seventh, acc[:])
         for i in range(2):
-            acc = psum.tile([P, P], F32, name="sum7_%d" % i, tag="gate_bank%d" % i)
-            multiply(acc[:], seventh + i * P, seventh + (i + 1) * P)
+            acc = psum.tile([P, P], F32, name="sum7_%d" % i, tag="gate_bank%d" % (i + 1))
+            multiply(acc[:], seventh + i * P, seventh + (i + 1) * P, passes=(1, 0))
             finish(seventh + i * P, seventh + (i + 1) * P, acc[:])
 
         halves = [slice(0, T // 2), slice(T // 2, T)]

@@ -27,10 +27,11 @@ STRIPE = 16
 MX_ALIGN = 64
 RUN = 4
 HALF = S // 2
-QUARTER = S // 4
+BANK = 512
+UNIT = P * PACK
 WINDOW = HALF + STRIPE
-W_TURNS = ((range(8, 11, 2),), (range(0, 2), range(2, 4), range(4, 6), range(6, 8)), (range(13, 16, 2),), (range(9, 12, 2), range(12, 15, 2)))
-OWN = S - C - P
+W_PIECES = (range(0, 2), range(2, 4), range(4, 6), range(6, 8), range(8, 10), range(10, 12), range(12, 14), range(14, 15), range(15, 16))
+SHARED = 5
 
 
 def tile_moe_pre_lin_relu_kernel(tc, xT, w, b, gate, offs, pos1, pos2, pos3, pos4, out):
@@ -41,10 +42,8 @@ def tile_moe_pre_lin_relu_kernel(tc, xT, w, b, gate, offs, pos1, pos2, pos3, pos
 
         slot_token = keep.tile([P, S // STRIPE], U16, name="slot_token")
         token_slot = [keep.tile([P, T // STRIPE], U16, name="token_slot%d" % r) for r in range(TOP)]
-        gate_first = keep.tile([P, QUARTER], F32, name="gate_first", align_bytes=MX_ALIGN)
-        raw_first = keep.tile([P, PACK, QUARTER], F32, name="raw_first", align_bytes=MX_ALIGN)
-        raw_last = keep.tile([P, PACK, S - OWN], F32, name="raw_last", align_bytes=MX_ALIGN)
-        gate_runs = raw_last[:, 0, 0:P]
+        gate_rows = {e: keep.tile([P, C], F32, name="gate_rows%d" % e, align_bytes=MX_ALIGN) for e in range(SHARED, E)}
+        gate_runs = keep.tile([P, P], F32, name="gate_runs")
         gate_columns = keep.tile([P, S // P], F32, name="gate_columns")
         identity = keep.tile([P, P], F32, name="identity")
         x_rows = [
@@ -52,8 +51,8 @@ def tile_moe_pre_lin_relu_kernel(tc, xT, w, b, gate, offs, pos1, pos2, pos3, pos
             for g in range(PASSES)
         ]
         w_raw = [
-            keep.tile([P, sum(len(load) for load in turn), PACK, N], F32, name="w_raw%d" % i, align_bytes=MX_ALIGN)
-            for i, turn in enumerate(W_TURNS)
+            keep.tile([P, len(piece), PACK, N], F32, name="w_raw%d" % i, align_bytes=MX_ALIGN)
+            for i, piece in enumerate(W_PIECES)
         ]
         bias = keep.tile([P, E], F32, name="bias")
         packed = {}
@@ -65,12 +64,12 @@ def tile_moe_pre_lin_relu_kernel(tc, xT, w, b, gate, offs, pos1, pos2, pos3, pos
 
         w_view = w.rearrange("e (g p j) n -> p (e g) (j n)", g=PASSES, j=PACK)
 
-        def load_w(turn):
-            first = 0
-            for load in W_TURNS[turn]:
-                dst = w_raw[turn][:, first : first + len(load)].rearrange("p q j n -> p q (j n)")
-                nc.sync.dma_start(out=dst, in_=w_view[:, load.start : load.stop : load.step])
-                first = first + len(load)
+        def load_w(i):
+            piece = W_PIECES[i]
+            nc.sync.dma_start(out=w_raw[i][:].rearrange("p q j n -> p q (j n)"), in_=w_view[:, piece.start : piece.stop])
+
+        def load_gate(e):
+            nc.sync.dma_start(out=gate_rows[e][:], in_=gate[0:P, e * C : (e + 1) * C])
 
         warm = keep.tile([P, 2], F32, name="warm")
         nc.gpsimd.memset(warm[:, 0:1], 0.0)
@@ -80,27 +79,36 @@ def tile_moe_pre_lin_relu_kernel(tc, xT, w, b, gate, offs, pos1, pos2, pos3, pos
 
         load_x(0, 0)
         nc.sync.dma_start(slot_token[:], offs)
-        load_x(0, 1)
-        nc.sync.dma_start(out=gate_runs, in_=gate[0 : P * P // S, :].rearrange("r (c s) -> (r c) s", s=P))
-        load_x(0, 2)
-        load_x(0, 3)
         load_w(0)
-        nc.sync.dma_start(out=gate_first[:], in_=gate[0:P, 0:QUARTER])
-        for j in range(PACK):
+        load_x(0, 1)
+        nc.sync.dma_start(out=gate_runs[:], in_=gate[0 : P * P // S, :].rearrange("r (c s) -> (r c) s", s=P))
+        load_w(1)
+        load_w(2)
+        load_x(0, 2)
+        load_w(3)
+        load_x(0, 3)
+        load_w(4)
+        load_w(5)
+        load_x(1, 0)
+        load_gate(5)
+        for j in range(1, PACK):
             load_x(1, j)
+        load_w(6)
+        load_w(7)
+        load_gate(6)
+        load_w(8)
+        load_gate(7)
         nc.sync.dma_start(out=bias[:], in_=b)
         for r, pos in enumerate((pos1, pos2, pos3, pos4)):
             nc.sync.dma_start(token_slot[r][:], pos)
-        for turn in range(1, len(w_raw)):
-            load_w(turn)
 
         turned = psum.tile([P, P], F32, name="turned", tag="sums0")
-        nc.tensor.transpose(turned[:], gate_runs, identity[:])
+        nc.tensor.transpose(turned[:], gate_runs[:], identity[:])
         nc.vector.tensor_copy(gate_columns[:], turned[:, 0 : S // P])
-        gate_banks = [psum.tile([P, QUARTER], F32, name="gate_bank%d" % i) for i in range(S // QUARTER)]
-        for i in (1, 3, 0, 2):
-            for c in range(QUARTER // P):
-                column = i * QUARTER // P + c
+        gate_banks = [psum.tile([P, BANK], F32, name="gate_bank%d" % i) for i in range(S // BANK)]
+        for i in range(S // BANK):
+            for c in range(BANK // P):
+                column = i * BANK // P + c
                 nc.tensor.transpose(
                     gate_banks[i][:, c * P : (c + 1) * P], gate_columns[:, column : column + 1].to_broadcast([P, P]), identity[:]
                 )
@@ -108,154 +116,141 @@ def tile_moe_pre_lin_relu_kernel(tc, xT, w, b, gate, offs, pos1, pos2, pos3, pos
         def tokens(g, j, s0, s1):
             return x_rows[g][j][:].indirect(slot_token[:, s0 // STRIPE : s1 // STRIPE])
 
-        def words(dst):
-            return dst.rearrange("p (c i j) -> p c j i", i=RUN, j=PACK)
+        def raw_steps(name, cuts, tag=None):
+            raw = keep.tile([P, (cuts[-1] - cuts[0]) * PACK], F32, name=name, tag=tag or name, align_bytes=MX_ALIGN)
+            return [
+                raw[:, (s0 - cuts[0]) * PACK : (s1 - cuts[0]) * PACK].rearrange("p (j s) -> p j s", j=PACK)
+                for s0, s1 in zip(cuts, cuts[1:])
+            ]
 
-        def rows(src):
-            return src.rearrange("p j (c i) -> p c j i", i=RUN)
-
-        def gather_on_scalar(g, cuts, tag):
-            raw = keep.tile([P, (cuts[-1] - cuts[0]) * PACK], F32, name="raw%d_%d" % (g, cuts[0]), tag=tag, align_bytes=MX_ALIGN)
-            steps = []
-            for s0, s1 in zip(cuts, cuts[1:]):
-                step = raw[:, (s0 - cuts[0]) * PACK : (s1 - cuts[0]) * PACK].rearrange("p (j s) -> p j s", j=PACK)
-                for j in range(PACK):
-                    nc.scalar.activation(step[:, j, :], tokens(g, j, s0, s1), COPY)
-                steps.append(step)
-            return steps
-
-        def rounded(name, columns, after=None):
-            return keep.tile([P, columns * PACK], BF16, name=name, tag=after or name, align_bytes=MX_ALIGN)
-
-        def gate_and_round(dst, raw, s0, s1):
-            n = (s1 - s0) // RUN
-            gates = gate_banks[s0 // QUARTER][:, s0 % QUARTER : s0 % QUARTER + s1 - s0]
-            spread = gates.rearrange("p (c i) -> p c i", i=RUN).unsqueeze(2).to_broadcast([P, n, PACK, RUN])
-            nc.vector.tensor_tensor(words(dst), rows(raw), spread, MULT)
-
-        def gather_on_vector(raw, g, s0, s1):
+        def gather_on_scalar(step, g, s0, s1):
             for j in range(PACK):
-                nc.vector.tensor_copy(raw[:, j, :], tokens(g, j, s0, s1))
+                nc.scalar.activation(step[:, j, :], tokens(g, j, s0, s1), COPY)
 
-        def round_w_on_gpsimd(dst, turn):
+        rounded = keep.tile([P, 27 * UNIT], BF16, name="rounded", align_bytes=MX_ALIGN)
+
+        def units(first, count):
+            return rounded[:, first * UNIT : (first + count) * UNIT]
+
+        def gate_on_vector(first, raw, s0, s1):
+            n = (s1 - s0) // RUN
+            gates = gate_banks[s0 // BANK][:, s0 % BANK : s0 % BANK + s1 - s0]
+            nc.vector.tensor_tensor(
+                units(first, (s1 - s0) // P).rearrange("p (c i j) -> p c j i", i=RUN, j=PACK),
+                raw.rearrange("p j (c i) -> p c j i", i=RUN),
+                gates.rearrange("p (c i) -> p c i", i=RUN).unsqueeze(2).to_broadcast([P, n, PACK, RUN]),
+                MULT,
+            )
+
+        def gate_on_gpsimd(first, e):
+            nc.gpsimd.tensor_tensor(
+                units(first, C // P).rearrange("p (s j) -> p s j", j=PACK),
+                raw_high[:, :, e * C - HALF : (e + 1) * C - HALF].rearrange("p j s -> p s j"),
+                gate_rows[e][:].unsqueeze(2).to_broadcast([P, C, PACK]),
+                MULT,
+            )
+
+        def round_w(first, i):
             nc.gpsimd.tensor_scalar(
-                out=dst.rearrange("p (q n j) -> p q n j", n=N, j=PACK),
-                in0=w_raw[turn][:].rearrange("p q j n -> p q n j"),
+                out=units(first, len(W_PIECES[i])).rearrange("p (q n j) -> p q n j", n=N, j=PACK),
+                in0=w_raw[i][:].rearrange("p q j n -> p q n j"),
                 scalar1=1.0,
                 scalar2=0.0,
                 op0=MULT,
                 op1=ADD,
             )
 
-        def quantize(src, runs, name, after=None):
-            width = len(runs) * P
-            codes = keep.tile([P, width], U32, name=name, tag=after or name, align_bytes=MX_ALIGN)
-            scales = keep.tile([P, width], U8, name=name + "_scales", align_bytes=MX_ALIGN)
-            nc.vector.quantize_mx(out=codes[:].bitcast(FP8X4), scales=scales[:], in_=src)
+        def packed_tiles(name, runs, tag):
+            codes = keep.tile([P, len(runs) * P], U32, name=name, tag=tag, align_bytes=MX_ALIGN)
+            scales = keep.tile([P, len(runs) * P], U8, name=name + "_scales", align_bytes=MX_ALIGN)
             for i, run in enumerate(runs):
                 packed[run] = (codes, scales, i * P)
 
-        def w_runs(turn):
-            return [("w", q // PASSES, q % PASSES) for load in W_TURNS[turn] for q in load]
-
-        def quantize_x(src, g, s0, s1):
-            quantize(src, [("x", g, s) for s in range(s0, s1, P)], "x_packed%d_%d" % (g, s0))
-
-        def multiply(acc, s0, s1, passes=(0, 1), start=True, stop=True):
-            for g in passes:
-                w_words, w_scales, w0 = packed["w", s0 // C, g]
-                x_words, x_scales, x0 = packed["x", g, s0]
-                nc.tensor.matmul_mx(
-                    out=acc,
-                    lhsT=w_words[:, w0 : w0 + N].bitcast(FP8X4),
-                    lhsT_scale=w_scales[:, w0 : w0 + N],
-                    rhs=x_words[:, x0 : x0 + s1 - s0].bitcast(FP8X4),
-                    rhs_scale=x_scales[:, x0 : x0 + s1 - s0],
-                    start=start and g == passes[0],
-                    stop=stop and g == passes[-1],
-                )
-
-        part = QUARTER * PACK
-        one = C * PACK
-
-        half = one // PASSES
-        sixth, seventh = 6 * C, 7 * C
+        def quantize(run, first, count):
+            codes, scales, c0 = packed[run]
+            nc.vector.quantize_mx(
+                out=codes[:, c0 : c0 + count * P].bitcast(FP8X4), scales=scales[:, c0 : c0 + count * P], in_=units(first, count)
+            )
 
         def x_runs(g, s0, s1):
             return [("x", g, s) for s in range(s0, s1, P)]
 
-        def runs(tile, first, count):
-            return tile[:, first * half : (first + count) * half]
+        def multiply(acc, e, g, start, stop):
+            w_words, w_scales, w0 = packed["w", PASSES * e + g]
+            x_words, x_scales, x0 = packed["x", g, e * C]
+            nc.tensor.matmul_mx(
+                out=acc,
+                lhsT=w_words[:, w0 : w0 + N].bitcast(FP8X4),
+                lhsT_scale=w_scales[:, w0 : w0 + N],
+                rhs=x_words[:, x0 : x0 + C].bitcast(FP8X4),
+                rhs_scale=x_scales[:, x0 : x0 + C],
+                start=start,
+                stop=stop,
+            )
 
-        (raw1,) = gather_on_scalar(0, (QUARTER, HALF), "raw_a")
-        (raw2,) = gather_on_scalar(1, (0, HALF), "raw_b")
-        gather_on_vector(raw_first, 0, 0, QUARTER)
-        early = rounded("early", 11 * P)
-        round_w_on_gpsimd(runs(early, 1, 2), 0)
-        nc.gpsimd.tensor_tensor(
-            runs(early, 3, 4).rearrange("p (s j) -> p s j", j=PACK),
-            raw_first[:].rearrange("p j s -> p s j"),
-            gate_first[:].unsqueeze(2).to_broadcast([P, QUARTER, PACK]),
-            MULT,
-        )
-        gather_on_vector(raw_last, 1, OWN, S)
-        gate_and_round(runs(early, 7, 4), raw1, QUARTER, HALF)
-        (raw3,) = gather_on_scalar(0, (HALF, sixth), "raw_first")
-        quantize_x(runs(early, 3, 8), 0, 0, HALF)
+        (raw_low,) = raw_steps("raw_low", (0, HALF))
+        (raw_high,) = raw_steps("raw_high", (HALF, S))
+        gather_on_scalar(raw_low, 0, 0, HALF)
+        for j in range(PACK):
+            nc.vector.tensor_copy(raw_high[:, j, :], tokens(0, j, HALF, S))
+        cuts = (HALF, 6 * C, 7 * C, S)
+        (step1,) = raw_steps("step1", (0, HALF))
+        gather_on_scalar(step1, 1, 0, HALF)
 
-        round_w_on_gpsimd(runs(early, 3, 8), 1)
-        late = rounded("late", 11 * P, after="gate_first")
-        gate_and_round(runs(late, 8, 3), raw_last[:], OWN, S)
+        for i in range(6):
+            round_w(2 * i, i)
+        gate_on_gpsimd(25, 5)
+        round_w(12, 6)
+        round_w(14, 7)
+        later = raw_steps("later", cuts, tag="w_raw6")
+        for step, s0, s1 in zip(later, cuts, cuts[1:]):
+            gather_on_scalar(step, 1, s0, s1)
+
         for i in range(2):
-            gate_and_round(runs(late, 4 * i, 4), raw2[:, :, i * QUARTER : (i + 1) * QUARTER], i * QUARTER, (i + 1) * QUARTER)
-        (raw4,) = gather_on_scalar(1, (HALF, OWN), "raw_b")
-        quantize_x(runs(late, 8, 3), 1, OWN, S)
-        quantize(runs(early, 3, 8), w_runs(1), "packed_w1")
-        quantize_x(runs(late, 0, 8), 1, 0, HALF)
+            gate_on_vector(15 + 4 * i, raw_low[:, :, i * BANK : (i + 1) * BANK], i * BANK, (i + 1) * BANK)
+        gate_on_vector(23, raw_high[:, :, 0:C], HALF, SHARED * C)
 
-        round_w_on_gpsimd(runs(early, 3, 2), 2)
-        gate_and_round(runs(early, 7, 4), raw3, HALF, sixth)
-        raw5, raw6 = gather_on_scalar(0, (sixth, seventh, S), "raw_first")
-        quantize(runs(early, 1, 4), w_runs(0) + w_runs(2), "packed_w2")
-        quantize_x(runs(early, 7, 4), 0, HALF, sixth)
+        early = [("w", q) for q in range(15)] + x_runs(0, 0, 6 * C)
+        packed_tiles("packed_early", early, "w_raw7")
+        for first in (0, 16, 8):
+            quantize(early[first], first, 8)
+        quantize(early[24], 24, 3)
 
-        round_w_on_gpsimd(runs(early, 7, 4), 3)
-        gate_and_round(runs(early, 3, 4), raw4[:, :, 0:QUARTER], HALF, sixth)
-        gate_and_round(runs(early, 2, 1), raw4[:, :, QUARTER:], sixth, OWN)
-        gate_and_round(runs(early, 0, 2), raw5, sixth, seventh)
-        quantize(runs(early, 7, 4), w_runs(3), "packed_w3")
-        quantize_x(runs(early, 3, 4), 1, HALF, sixth)
-        quantize(runs(early, 0, 3), x_runs(0, sixth, seventh) + x_runs(1, sixth, OWN), "packed_sixth")
+        gate_on_gpsimd(8, 6)
+        round_w(10, 8)
         for i in range(2):
-            gate_and_round(runs(early, 7 + i, 1), raw6[:, :, i * P : (i + 1) * P], seventh + i * P, seventh + (i + 1) * P)
-        for i in range(2):
-            quantize_x(runs(early, 7 + i, 1), 0, seventh + i * P, seventh + (i + 1) * P)
+            gate_on_vector(4 * i, step1[:, :, i * BANK : (i + 1) * BANK], i * BANK, (i + 1) * BANK)
+        packed_tiles("packed_second", x_runs(0, 6 * C, 7 * C) + [("w", 15)], "packed_second")
+        quantize(("x", 0, 6 * C), 8, 3)
+        packed_tiles("packed_low", x_runs(1, 0, HALF), "gate_rows6")
+        quantize(("x", 1, 0), 0, 8)
 
-        y = keep.tile([P, S], F32, name="y", tag="x_rows0_2", align_bytes=MX_ALIGN)
+        gate_on_gpsimd(8, 7)
+        gate_on_vector(10, later[0], HALF, 6 * C)
+        gate_on_vector(6, later[1], 6 * C, 7 * C)
+        packed_tiles("packed_third", x_runs(1, HALF, 6 * C), "packed_third")
+        quantize(("x", 1, HALF), 10, 4)
+        gate_on_vector(4, later[2], 7 * C, S)
+        packed_tiles("packed_last", x_runs(1, 6 * C, 7 * C) + x_runs(0, 7 * C, S) + x_runs(1, 7 * C, S), "gate_rows7")
+        quantize(("x", 1, 6 * C), 6, 4)
+        quantize(("x", 1, 7 * C), 4, 2)
 
-        def finish(s0, s1, acc):
-            e = s0 // C
-            nc.scalar.activation(out=y[:, s0:s1], in_=acc, func=RELU, bias=bias[:, e : e + 1])
-
-        for pair in range(2):
-            acc = psum.tile([P, 2 * C], F32, name="sums%d" % pair)
-            for i in range(2):
-                multiply(acc[:, i * C : (i + 1) * C], (2 * pair + i) * C, (2 * pair + i + 1) * C)
-            for i in range(2):
-                finish((2 * pair + i) * C, (2 * pair + i + 1) * C, acc[:, i * C : (i + 1) * C])
-        for e in (4, 5):
-            acc = psum.tile([P, C], F32, name="sums%d" % (e - 2))
-            multiply(acc[:], e * C, (e + 1) * C)
-            finish(e * C, (e + 1) * C, acc[:])
-        acc = psum.tile([P, C], F32, name="sum6", tag="gate_bank0")
-        multiply(acc[:, P:], OWN, seventh, passes=(1,), stop=False)
-        multiply(acc[:, 0:P], sixth, OWN, passes=(1,), start=False, stop=False)
-        multiply(acc[:], sixth, seventh, passes=(0,), start=False)
-        finish(sixth, seventh, acc[:])
-        for i in range(2):
-            acc = psum.tile([P, P], F32, name="sum7_%d" % i, tag="gate_bank%d" % (i + 1))
-            multiply(acc[:], seventh + i * P, seventh + (i + 1) * P, passes=(1, 0))
-            finish(seventh + i * P, seventh + (i + 1) * P, acc[:])
+        y = keep.tile([P, S], F32, name="y", tag="x_rows1_2", align_bytes=MX_ALIGN)
+        pairs = [psum.tile([P, 2 * C], F32, name="sums%d" % i) for i in range(3)]
+        acc = [pairs[e // 2][:, e % 2 * C : (e % 2 + 1) * C] for e in range(6)]
+        sixth = psum.tile([P, C], F32, name="sums3")
+        seventh = psum.tile([P, C], F32, name="seventh", tag="gate_bank0")
+        acc = acc + [sixth[:], seventh[:]]
+        for e in range(6):
+            multiply(acc[e], e, 0, e % 2 == 0, False)
+        multiply(acc[6], 6, 0, True, False)
+        for e in range(6):
+            multiply(acc[e], e, 1, False, e % 2 == 1)
+        multiply(acc[6], 6, 1, False, True)
+        for g in range(PASSES):
+            multiply(acc[7], 7, g, g == 0, g == 1)
+        for e in range(E):
+            nc.scalar.activation(out=y[:, e * C : (e + 1) * C], in_=acc[e], func=RELU, bias=bias[:, e : e + 1])
 
         halves = [slice(0, T // 2), slice(T // 2, T)]
 

@@ -30,7 +30,7 @@ HALF = S // 2
 BANK = 512
 UNIT = P * PACK
 WINDOW = HALF + STRIPE
-W_PIECES = (range(0, 2), range(2, 4), range(4, 6), range(6, 8), range(8, 10), range(10, 12), range(12, 14), range(14, 15), range(15, 16))
+W_PIECES = (range(0, 2), range(2, 4), range(4, 6), range(6, 8), range(8, 10), range(10, 12), range(12, 13), range(13, 16))
 SHARED = 5
 
 
@@ -94,9 +94,8 @@ def tile_moe_pre_lin_relu_kernel(tc, xT, w, b, gate, offs, pos1, pos2, pos3, pos
         for j in range(1, PACK):
             load_x(1, j)
         load_w(6)
-        load_w(7)
         load_gate(6)
-        load_w(8)
+        load_w(7)
         load_gate(7)
         nc.sync.dma_start(out=bias[:], in_=b)
         for r, pos in enumerate((pos1, pos2, pos3, pos4)):
@@ -127,7 +126,7 @@ def tile_moe_pre_lin_relu_kernel(tc, xT, w, b, gate, offs, pos1, pos2, pos3, pos
             for j in range(PACK):
                 nc.scalar.activation(step[:, j, :], tokens(g, j, s0, s1), COPY)
 
-        rounded = keep.tile([P, 27 * UNIT], BF16, name="rounded", align_bytes=MX_ALIGN)
+        rounded = keep.tile([P, 31 * UNIT], BF16, name="rounded", align_bytes=MX_ALIGN)
 
         def units(first, count):
             return rounded[:, first * UNIT : (first + count) * UNIT]
@@ -175,15 +174,15 @@ def tile_moe_pre_lin_relu_kernel(tc, xT, w, b, gate, offs, pos1, pos2, pos3, pos
         def x_runs(g, s0, s1):
             return [("x", g, s) for s in range(s0, s1, P)]
 
-        def multiply(acc, e, g, start, stop):
-            w_words, w_scales, w0 = packed["w", PASSES * e + g]
-            x_words, x_scales, x0 = packed["x", g, e * C]
+        def multiply(acc, s0, s1, g, start, stop):
+            w_words, w_scales, w0 = packed["w", PASSES * (s0 // C) + g]
+            x_words, x_scales, x0 = packed["x", g, s0]
             nc.tensor.matmul_mx(
                 out=acc,
                 lhsT=w_words[:, w0 : w0 + N].bitcast(FP8X4),
                 lhsT_scale=w_scales[:, w0 : w0 + N],
-                rhs=x_words[:, x0 : x0 + C].bitcast(FP8X4),
-                rhs_scale=x_scales[:, x0 : x0 + C],
+                rhs=x_words[:, x0 : x0 + s1 - s0].bitcast(FP8X4),
+                rhs_scale=x_scales[:, x0 : x0 + s1 - s0],
                 start=start,
                 stop=stop,
             )
@@ -193,64 +192,59 @@ def tile_moe_pre_lin_relu_kernel(tc, xT, w, b, gate, offs, pos1, pos2, pos3, pos
         gather_on_scalar(raw_low, 0, 0, HALF)
         for j in range(PACK):
             nc.vector.tensor_copy(raw_high[:, j, :], tokens(0, j, HALF, S))
-        cuts = (HALF, 6 * C, 7 * C, S)
-        (step1,) = raw_steps("step1", (0, HALF))
-        gather_on_scalar(step1, 1, 0, HALF)
+        cuts = (2 * C, 4 * C, 6 * C, 7 * C, S - P, S)
+        (step1,) = raw_steps("step1", (0, cuts[0]))
+        gather_on_scalar(step1, 1, 0, cuts[0])
 
         for i in range(6):
             round_w(2 * i, i)
-        gate_on_gpsimd(25, 5)
+        gate_on_gpsimd(23, 5)
         round_w(12, 6)
-        round_w(14, 7)
+        gate_on_gpsimd(25, 6)
         later = raw_steps("later", cuts, tag="w_raw6")
         for step, s0, s1 in zip(later, cuts, cuts[1:]):
             gather_on_scalar(step, 1, s0, s1)
 
+        gate_on_vector(21, raw_high[:, :, 0:C], HALF, SHARED * C)
         for i in range(2):
-            gate_on_vector(15 + 4 * i, raw_low[:, :, i * BANK : (i + 1) * BANK], i * BANK, (i + 1) * BANK)
-        gate_on_vector(23, raw_high[:, :, 0:C], HALF, SHARED * C)
+            gate_on_vector(13 + 4 * i, raw_low[:, :, i * BANK : (i + 1) * BANK], i * BANK, (i + 1) * BANK)
+        gate_on_vector(27, step1, 0, cuts[0])
 
-        early = [("w", q) for q in range(15)] + x_runs(0, 0, 6 * C)
-        packed_tiles("packed_early", early, "w_raw7")
-        for first in (0, 16, 8):
-            quantize(early[first], first, 8)
-        quantize(early[24], 24, 3)
+        early = [("w", q) for q in range(13)] + x_runs(0, 0, 7 * C) + x_runs(1, 0, cuts[0])
+        packed_tiles("packed_early", early, "gate_rows6")
+        for first, count in ((8, 8), (24, 4), (28, 3), (16, 8), (0, 8)):
+            quantize(early[first], first, count)
 
-        gate_on_gpsimd(8, 6)
-        round_w(10, 8)
+        round_w(21, 7)
+        gate_on_vector(27, later[0], cuts[0], cuts[1])
+        packed_tiles("packed_second", [("w", q) for q in W_PIECES[7]], "packed_second")
+        quantize(("w", 13), 21, 3)
+        packed_tiles("packed_third", x_runs(1, cuts[0], cuts[1]), "w_raw7")
+        quantize(("x", 1, cuts[0]), 27, 4)
+
+        gate_on_gpsimd(21, 7)
+        gate_on_vector(23, later[1], cuts[1], cuts[2])
+        gate_on_vector(27, later[2], cuts[2], cuts[3])
+        packed_tiles("packed_last", x_runs(0, 7 * C, S) + x_runs(1, HALF, S), "gate_rows7")
+        quantize(("x", 0, 7 * C), 21, 4)
+        quantize(("x", 1, 5 * C), 25, 4)
         for i in range(2):
-            gate_on_vector(4 * i, step1[:, :, i * BANK : (i + 1) * BANK], i * BANK, (i + 1) * BANK)
-        packed_tiles("packed_second", x_runs(0, 6 * C, 7 * C) + [("w", 15)], "packed_second")
-        quantize(("x", 0, 6 * C), 8, 3)
-        packed_tiles("packed_low", x_runs(1, 0, HALF), "gate_rows6")
-        quantize(("x", 1, 0), 0, 8)
-
-        gate_on_gpsimd(8, 7)
-        gate_on_vector(10, later[0], HALF, 6 * C)
-        gate_on_vector(6, later[1], 6 * C, 7 * C)
-        packed_tiles("packed_third", x_runs(1, HALF, 6 * C), "packed_third")
-        quantize(("x", 1, HALF), 10, 4)
-        gate_on_vector(4, later[2], 7 * C, S)
-        packed_tiles("packed_last", x_runs(1, 6 * C, 7 * C) + x_runs(0, 7 * C, S) + x_runs(1, 7 * C, S), "gate_rows7")
-        quantize(("x", 1, 6 * C), 6, 4)
-        quantize(("x", 1, 7 * C), 4, 2)
+            gate_on_vector(21 + i, later[3 + i], cuts[3 + i], cuts[4 + i])
+        for i in range(2):
+            quantize(("x", 1, cuts[3 + i]), 21 + i, 1)
 
         y = keep.tile([P, S], F32, name="y", tag="x_rows1_2", align_bytes=MX_ALIGN)
         pairs = [psum.tile([P, 2 * C], F32, name="sums%d" % i) for i in range(3)]
-        acc = [pairs[e // 2][:, e % 2 * C : (e % 2 + 1) * C] for e in range(6)]
         sixth = psum.tile([P, C], F32, name="sums3")
-        seventh = psum.tile([P, C], F32, name="seventh", tag="gate_bank0")
-        acc = acc + [sixth[:], seventh[:]]
-        for e in range(6):
-            multiply(acc[e], e, 0, e % 2 == 0, False)
-        multiply(acc[6], 6, 0, True, False)
-        for e in range(6):
-            multiply(acc[e], e, 1, False, e % 2 == 1)
-        multiply(acc[6], 6, 1, False, True)
-        for g in range(PASSES):
-            multiply(acc[7], 7, g, g == 0, g == 1)
-        for e in range(E):
-            nc.scalar.activation(out=y[:, e * C : (e + 1) * C], in_=acc[e], func=RELU, bias=bias[:, e : e + 1])
+        ends = [psum.tile([P, P], F32, name="end%d" % i, tag="gate_bank%d" % i) for i in range(2)]
+        sums = [(e * C, (e + 1) * C, pairs[e // 2][:, e % 2 * C : (e % 2 + 1) * C], e % 2 == 0, e % 2 == 1) for e in range(6)]
+        sums.append((6 * C, 7 * C, sixth[:], True, True))
+        sums.extend((cuts[3 + i], cuts[4 + i], ends[i][:], True, True) for i in range(2))
+        for g, which in ((0, range(7)), (1, range(4)), (0, range(7, 9)), (1, range(4, 9))):
+            for s0, s1, acc, opens, closes in (sums[i] for i in which):
+                multiply(acc, s0, s1, g, g == 0 and opens, g == 1 and closes)
+        for s0, s1, acc, opens, closes in sums:
+            nc.scalar.activation(out=y[:, s0:s1], in_=acc, func=RELU, bias=bias[:, s0 // C : s0 // C + 1])
 
         halves = [slice(0, T // 2), slice(T // 2, T)]
 

@@ -88,11 +88,11 @@ def tile_moe_pre_lin_relu_kernel(tc, xT, w, b, gate, offs, pos1, pos2, pos3, pos
         load_w(3)
         load_x(0, 3)
         load_w(4)
-        load_w(5)
         load_x(1, 0)
         load_gate(5)
         for j in range(1, PACK):
             load_x(1, j)
+        load_w(5)
         load_w(6)
         load_gate(6)
         load_w(7)
@@ -192,22 +192,24 @@ def tile_moe_pre_lin_relu_kernel(tc, xT, w, b, gate, offs, pos1, pos2, pos3, pos
         gather_on_scalar(raw_low, 0, 0, HALF)
         for j in range(PACK):
             nc.vector.tensor_copy(raw_high[:, j, :], tokens(0, j, HALF, S))
-        cuts = (2 * C, 4 * C, 6 * C, 7 * C, S - P, S)
+        cuts = (2 * C, 4 * C, 6 * C, 7 * C, S)
+        halves7 = (7 * C, S - P, S)
         (step1,) = raw_steps("step1", (0, cuts[0]))
         gather_on_scalar(step1, 1, 0, cuts[0])
 
-        for i in range(6):
+        for i in range(5):
             round_w(2 * i, i)
         gate_on_gpsimd(23, 5)
+        round_w(10, 5)
         round_w(12, 6)
         gate_on_gpsimd(25, 6)
-        later = raw_steps("later", cuts, tag="w_raw6")
-        for step, s0, s1 in zip(later, cuts, cuts[1:]):
-            gather_on_scalar(step, 1, s0, s1)
+        later = raw_steps("later", cuts, tag="w_raw5")
 
         gate_on_vector(21, raw_high[:, :, 0:C], HALF, SHARED * C)
         for i in range(2):
             gate_on_vector(13 + 4 * i, raw_low[:, :, i * BANK : (i + 1) * BANK], i * BANK, (i + 1) * BANK)
+        for step, s0, s1 in zip(later, cuts, cuts[1:]):
+            gather_on_scalar(step, 1, s0, s1)
         gate_on_vector(27, step1, 0, cuts[0])
 
         early = [("w", q) for q in range(13)] + x_runs(0, 0, 7 * C) + x_runs(1, 0, cuts[0])
@@ -229,9 +231,9 @@ def tile_moe_pre_lin_relu_kernel(tc, xT, w, b, gate, offs, pos1, pos2, pos3, pos
         quantize(("x", 0, 7 * C), 21, 4)
         quantize(("x", 1, 5 * C), 25, 4)
         for i in range(2):
-            gate_on_vector(21 + i, later[3 + i], cuts[3 + i], cuts[4 + i])
+            gate_on_vector(21 + i, later[3][:, :, i * P : (i + 1) * P], halves7[i], halves7[i + 1])
         for i in range(2):
-            quantize(("x", 1, cuts[3 + i]), 21 + i, 1)
+            quantize(("x", 1, halves7[i]), 21 + i, 1)
 
         y = keep.tile([P, S], F32, name="y", tag="x_rows1_2", align_bytes=MX_ALIGN)
         pairs = [psum.tile([P, 2 * C], F32, name="sums%d" % i) for i in range(3)]
@@ -239,7 +241,7 @@ def tile_moe_pre_lin_relu_kernel(tc, xT, w, b, gate, offs, pos1, pos2, pos3, pos
         ends = [psum.tile([P, P], F32, name="end%d" % i, tag="gate_bank%d" % i) for i in range(2)]
         sums = [(e * C, (e + 1) * C, pairs[e // 2][:, e % 2 * C : (e % 2 + 1) * C], e % 2 == 0, e % 2 == 1) for e in range(6)]
         sums.append((6 * C, 7 * C, sixth[:], True, True))
-        sums.extend((cuts[3 + i], cuts[4 + i], ends[i][:], True, True) for i in range(2))
+        sums.extend((halves7[i], halves7[i + 1], ends[i][:], True, True) for i in range(2))
         for g, which in ((0, range(7)), (1, range(4)), (0, range(7, 9)), (1, range(4, 9))):
             for s0, s1, acc, opens, closes in (sums[i] for i in which):
                 multiply(acc, s0, s1, g, g == 0 and opens, g == 1 and closes)

@@ -30,7 +30,7 @@ HALF = S // 2
 BANK = 512
 UNIT = P * PACK
 WINDOW = HALF + STRIPE
-W_PIECES = (range(0, 2), range(2, 4), range(4, 6), range(6, 8), range(8, 10), range(10, 12), range(12, 13), range(13, 16))
+W_PIECES = (range(0, 2), range(2, 4), range(4, 6), range(6, 8), range(8, 10), range(10, 11), range(11, 13), range(13, 16))
 SHARED = 5
 
 
@@ -88,11 +88,11 @@ def tile_moe_pre_lin_relu_kernel(tc, xT, w, b, gate, offs, pos1, pos2, pos3, pos
         load_w(3)
         load_x(0, 3)
         load_w(4)
+        load_w(5)
         load_x(1, 0)
         load_gate(5)
         for j in range(1, PACK):
             load_x(1, j)
-        load_w(5)
         load_w(6)
         load_gate(6)
         load_w(7)
@@ -197,13 +197,12 @@ def tile_moe_pre_lin_relu_kernel(tc, xT, w, b, gate, offs, pos1, pos2, pos3, pos
         (step1,) = raw_steps("step1", (0, cuts[0]))
         gather_on_scalar(step1, 1, 0, cuts[0])
 
-        for i in range(5):
+        for i in range(6):
             round_w(2 * i, i)
         gate_on_gpsimd(23, 5)
-        round_w(10, 5)
-        round_w(12, 6)
+        round_w(11, 6)
         gate_on_gpsimd(25, 6)
-        later = raw_steps("later", cuts, tag="w_raw5")
+        later = raw_steps("later", cuts, tag="w_raw6")
 
         gate_on_vector(21, raw_high[:, :, 0:C], HALF, SHARED * C)
         for i in range(2):

@@ -31,7 +31,8 @@ BANK = 512
 UNIT = P * PACK
 WINDOW = HALF + STRIPE
 W_PIECES = (range(0, 2), range(2, 4), range(4, 6), range(6, 8), range(8, 10), range(10, 11), range(11, 13), range(13, 16))
-SHARED = 5
+SPLIT = 5 * C - 64
+G_TURNS = ((6 * C, 7 * C), (SPLIT, 6 * C), (7 * C, S))
 
 
 def tile_moe_pre_lin_relu_kernel(tc, xT, w, b, gate, offs, pos1, pos2, pos3, pos4, out):
@@ -42,7 +43,9 @@ def tile_moe_pre_lin_relu_kernel(tc, xT, w, b, gate, offs, pos1, pos2, pos3, pos
 
         slot_token = keep.tile([P, S // STRIPE], U16, name="slot_token")
         token_slot = [keep.tile([P, T // STRIPE], U16, name="token_slot%d" % r) for r in range(TOP)]
-        gate_rows = {e: keep.tile([P, C], F32, name="gate_rows%d" % e, align_bytes=MX_ALIGN) for e in range(SHARED, E)}
+        gate_rows = [
+            keep.tile([P, s1 - s0], F32, name="gate_rows%d" % i, align_bytes=MX_ALIGN) for i, (s0, s1) in enumerate(G_TURNS)
+        ]
         gate_runs = keep.tile([P, P], F32, name="gate_runs")
         gate_columns = keep.tile([P, S // P], F32, name="gate_columns")
         identity = keep.tile([P, P], F32, name="identity")
@@ -68,8 +71,8 @@ def tile_moe_pre_lin_relu_kernel(tc, xT, w, b, gate, offs, pos1, pos2, pos3, pos
             piece = W_PIECES[i]
             nc.sync.dma_start(out=w_raw[i][:].rearrange("p q j n -> p q (j n)"), in_=w_view[:, piece.start : piece.stop])
 
-        def load_gate(e):
-            nc.sync.dma_start(out=gate_rows[e][:], in_=gate[0:P, e * C : (e + 1) * C])
+        def load_gate(i):
+            nc.sync.dma_start(out=gate_rows[i][:], in_=gate[0:P, G_TURNS[i][0] : G_TURNS[i][1]])
 
         warm = keep.tile([P, 2], F32, name="warm")
         nc.gpsimd.memset(warm[:, 0:1], 0.0)
@@ -90,13 +93,13 @@ def tile_moe_pre_lin_relu_kernel(tc, xT, w, b, gate, offs, pos1, pos2, pos3, pos
         load_w(4)
         load_w(5)
         load_x(1, 0)
-        load_gate(5)
+        load_gate(0)
         for j in range(1, PACK):
             load_x(1, j)
         load_w(6)
-        load_gate(6)
+        load_gate(1)
         load_w(7)
-        load_gate(7)
+        load_gate(2)
         nc.sync.dma_start(out=bias[:], in_=b)
         for r, pos in enumerate((pos1, pos2, pos3, pos4)):
             nc.sync.dma_start(token_slot[r][:], pos)
@@ -135,17 +138,19 @@ def tile_moe_pre_lin_relu_kernel(tc, xT, w, b, gate, offs, pos1, pos2, pos3, pos
             n = (s1 - s0) // RUN
             gates = gate_banks[s0 // BANK][:, s0 % BANK : s0 % BANK + s1 - s0]
             nc.vector.tensor_tensor(
-                units(first, (s1 - s0) // P).rearrange("p (c i j) -> p c j i", i=RUN, j=PACK),
+                rounded[:, first * UNIT : first * UNIT + (s1 - s0) * PACK].rearrange("p (c i j) -> p c j i", i=RUN, j=PACK),
                 raw.rearrange("p j (c i) -> p c j i", i=RUN),
                 gates.rearrange("p (c i) -> p c i", i=RUN).unsqueeze(2).to_broadcast([P, n, PACK, RUN]),
                 MULT,
             )
 
-        def gate_on_gpsimd(first, e):
+        def gate_on_gpsimd(first, i):
+            s0, s1 = G_TURNS[i]
+            c0 = first * UNIT + s0 % P * PACK
             nc.gpsimd.tensor_tensor(
-                units(first, C // P).rearrange("p (s j) -> p s j", j=PACK),
-                raw_high[:, :, e * C - HALF : (e + 1) * C - HALF].rearrange("p j s -> p s j"),
-                gate_rows[e][:].unsqueeze(2).to_broadcast([P, C, PACK]),
+                rounded[:, c0 : c0 + (s1 - s0) * PACK].rearrange("p (s j) -> p s j", j=PACK),
+                raw_high[:, :, s0 - HALF : s1 - HALF].rearrange("p j s -> p s j"),
+                gate_rows[i][:].unsqueeze(2).to_broadcast([P, s1 - s0, PACK]),
                 MULT,
             )
 
@@ -199,12 +204,12 @@ def tile_moe_pre_lin_relu_kernel(tc, xT, w, b, gate, offs, pos1, pos2, pos3, pos
 
         for i in range(6):
             round_w(2 * i, i)
-        gate_on_gpsimd(23, 5)
+        gate_on_gpsimd(25, 0)
         round_w(11, 6)
-        gate_on_gpsimd(25, 6)
+        gate_on_gpsimd(22, 1)
         later = raw_steps("later", cuts, tag="w_raw6")
 
-        gate_on_vector(21, raw_high[:, :, 0:C], HALF, SHARED * C)
+        gate_on_vector(21, raw_high[:, :, 0 : SPLIT - HALF], HALF, SPLIT)
         for i in range(2):
             gate_on_vector(13 + 4 * i, raw_low[:, :, i * BANK : (i + 1) * BANK], i * BANK, (i + 1) * BANK)
         for step, s0, s1 in zip(later, cuts, cuts[1:]):
@@ -212,7 +217,7 @@ def tile_moe_pre_lin_relu_kernel(tc, xT, w, b, gate, offs, pos1, pos2, pos3, pos
         gate_on_vector(27, step1, 0, cuts[0])
 
         early = [("w", q) for q in range(13)] + x_runs(0, 0, 7 * C) + x_runs(1, 0, cuts[0])
-        packed_tiles("packed_early", early, "gate_rows6")
+        packed_tiles("packed_early", early, "gate_rows1")
         for first, count in ((8, 8), (24, 4), (28, 3), (16, 8), (0, 8)):
             quantize(early[first], first, count)
 
@@ -223,10 +228,10 @@ def tile_moe_pre_lin_relu_kernel(tc, xT, w, b, gate, offs, pos1, pos2, pos3, pos
         packed_tiles("packed_third", x_runs(1, cuts[0], cuts[1]), "w_raw7")
         quantize(("x", 1, cuts[0]), 27, 4)
 
-        gate_on_gpsimd(21, 7)
+        gate_on_gpsimd(21, 2)
         gate_on_vector(23, later[1], cuts[1], cuts[2])
         gate_on_vector(27, later[2], cuts[2], cuts[3])
-        packed_tiles("packed_last", x_runs(0, 7 * C, S) + x_runs(1, HALF, S), "gate_rows7")
+        packed_tiles("packed_last", x_runs(0, 7 * C, S) + x_runs(1, HALF, S), "gate_rows2")
         quantize(("x", 0, 7 * C), 21, 4)
         quantize(("x", 1, 5 * C), 25, 4)
         for i in range(2):

@@ -148,9 +148,9 @@ def tile_moe_pre_lin_relu_kernel(tc, xT, w, b, gate, offs, pos1, pos2, pos3, pos
             s0, s1 = G_TURNS[i]
             c0 = first * UNIT + s0 % P * PACK
             nc.gpsimd.tensor_tensor(
-                rounded[:, c0 : c0 + (s1 - s0) * PACK].rearrange("p (s j) -> p s j", j=PACK),
-                raw_high[:, :, s0 - HALF : s1 - HALF].rearrange("p j s -> p s j"),
-                gate_rows[i][:].unsqueeze(2).to_broadcast([P, s1 - s0, PACK]),
+                rounded[:, c0 : c0 + (s1 - s0) * PACK].rearrange("p (c i j) -> p c j i", i=RUN, j=PACK),
+                raw_high[:, :, s0 - HALF : s1 - HALF].rearrange("p j (c i) -> p c j i", i=RUN),
+                gate_rows[i][:].rearrange("p (c i) -> p c i", i=RUN).unsqueeze(2).to_broadcast([P, (s1 - s0) // RUN, PACK, RUN]),
                 MULT,
             )
 

@@ -30,7 +30,7 @@ HALF = S // 2
 BANK = 512
 UNIT = P * PACK
 WINDOW = HALF + STRIPE
-W_PIECES = (range(0, 2), range(2, 4), range(4, 6), range(6, 8), range(8, 10), range(10, 11), range(11, 13), range(13, 16))
+W_PIECES = (range(0, 2), range(2, 4), range(4, 6), range(6, 8), range(8, 10), range(10, 12), range(12, 13), range(13, 16))
 SPLIT = 5 * C - 64
 G_TURNS = ((6 * C, 7 * C), (SPLIT, 6 * C), (7 * C, S))
 
@@ -205,7 +205,7 @@ def tile_moe_pre_lin_relu_kernel(tc, xT, w, b, gate, offs, pos1, pos2, pos3, pos
         for i in range(6):
             round_w(2 * i, i)
         gate_on_gpsimd(25, 0)
-        round_w(11, 6)
+        round_w(12, 6)
         gate_on_gpsimd(22, 1)
         later = raw_steps("later", cuts, tag="w_raw6")
 

from contextlib import ExitStack

import concourse.mybir as mybir
from concourse.masks import make_identity

K, T, E, C, N = 1024, 512, 8, 256, 128
TOP = 4
S = E * C
FLOPS = 2 * K * N * S
BYTES = 4 * (K * T + E * K * N + N * E + 128 * S + N * T) + 2 * 128 * (S // 16 + TOP * T // 16)

F32 = mybir.dt.float32
BF16 = mybir.dt.bfloat16
U32 = mybir.dt.uint32
U16 = mybir.dt.uint16
U8 = mybir.dt.uint8
FP8X4 = mybir.dt.float8_e4m3fn_x4
MULT = mybir.AluOpType.mult
ADD = mybir.AluOpType.add
COPY = mybir.ActivationFunctionType.Copy
RELU = mybir.ActivationFunctionType.Relu

P = 128
PACK = 4
PASSES = K // (P * PACK)
STRIPE = 16
MX_ALIGN = 64
RUN = 4
HALF = S // 2
BANK = 512
UNIT = P * PACK
WINDOW = HALF + STRIPE
W_PIECES = (range(0, 2), range(2, 4), range(4, 6), range(6, 8), range(8, 10), range(10, 12), range(12, 13), range(13, 16))
SPLIT = 5 * C - 64
G_TURNS = ((6 * C, 7 * C), (SPLIT, 6 * C), (7 * C, S))


def tile_moe_pre_lin_relu_kernel(tc, xT, w, b, gate, offs, pos1, pos2, pos3, pos4, out):
    nc = tc.nc
    with ExitStack() as ctx:
        keep = ctx.enter_context(tc.tile_pool(name="keep", bufs=1))
        psum = ctx.enter_context(tc.psum_pool(name="psum", bufs=1))

        slot_token = keep.tile([P, S // STRIPE], U16, name="slot_token")
        token_slot = [keep.tile([P, T // STRIPE], U16, name="token_slot%d" % r) for r in range(TOP)]
        gate_rows = [
            keep.tile([P, s1 - s0], F32, name="gate_rows%d" % i, align_bytes=MX_ALIGN) for i, (s0, s1) in enumerate(G_TURNS)
        ]
        gate_runs = keep.tile([P, P], F32, name="gate_runs")
        gate_columns = keep.tile([P, S // P], F32, name="gate_columns")
        identity = keep.tile([P, P], F32, name="identity")
        x_rows = [
            [keep.tile([P, WINDOW], F32, name="x_rows%d_%d" % (g, j), align_bytes=MX_ALIGN) for j in range(PACK)]
            for g in range(PASSES)
        ]
        w_raw = [
            keep.tile([P, len(piece), PACK, N], F32, name="w_raw%d" % i, align_bytes=MX_ALIGN)
            for i, piece in enumerate(W_PIECES)
        ]
        bias = keep.tile([P, E], F32, name="bias")
        packed = {}

        x_view = xT.rearrange("(g p j) t -> g j p t", g=PASSES, j=PACK)

        def load_x(g, j):
            nc.sync.dma_start(out=x_rows[g][j][:, 0:T], in_=x_view[g, j])

        w_view = w.rearrange("e (g p j) n -> p (e g) (j n)", g=PASSES, j=PACK)

        def load_w(i):
            piece = W_PIECES[i]
            nc.sync.dma_start(out=w_raw[i][:].rearrange("p q j n -> p q (j n)"), in_=w_view[:, piece.start : piece.stop])

        def load_gate(i):
            nc.sync.dma_start(out=gate_rows[i][:], in_=gate[0:P, G_TURNS[i][0] : G_TURNS[i][1]])

        warm = keep.tile([P, 2], F32, name="warm")
        nc.gpsimd.memset(warm[:, 0:1], 0.0)
        nc.scalar.activation(warm[:, 1:2], warm[:, 0:1], COPY)

        make_identity(nc, identity[:])

        load_x(0, 0)
        nc.sync.dma_start(slot_token[:], offs)
        load_w(0)
        load_x(0, 1)
        nc.sync.dma_start(out=gate_runs[:], in_=gate[0 : P * P // S, :].rearrange("r (c s) -> (r c) s", s=P))
        load_w(1)
        load_w(2)
        load_x(0, 2)
        load_w(3)
        load_x(0, 3)
        load_w(4)
        load_w(5)
        load_x(1, 0)
        load_gate(0)
        for j in range(1, PACK):
            load_x(1, j)
        load_w(6)
        load_gate(1)
        load_w(7)
        load_gate(2)
        nc.sync.dma_start(out=bias[:], in_=b)
        for r, pos in enumerate((pos1, pos2, pos3, pos4)):
            nc.sync.dma_start(token_slot[r][:], pos)

        turned = psum.tile([P, P], F32, name="turned", tag="sums0")
        nc.tensor.transpose(turned[:], gate_runs[:], identity[:])
        nc.vector.tensor_copy(gate_columns[:], turned[:, 0 : S // P])
        gate_banks = [psum.tile([P, BANK], F32, name="gate_bank%d" % i) for i in range(S // BANK)]
        for i in range(S // BANK):
            for c in range(BANK // P):
                column = i * BANK // P + c
                nc.tensor.transpose(
                    gate_banks[i][:, c * P : (c + 1) * P], gate_columns[:, column : column + 1].to_broadcast([P, P]), identity[:]
                )

        def tokens(g, j, s0, s1):
            return x_rows[g][j][:].indirect(slot_token[:, s0 // STRIPE : s1 // STRIPE])

        def raw_steps(name, cuts, tag=None):
            raw = keep.tile([P, (cuts[-1] - cuts[0]) * PACK], F32, name=name, tag=tag or name, align_bytes=MX_ALIGN)
            return [
                raw[:, (s0 - cuts[0]) * PACK : (s1 - cuts[0]) * PACK].rearrange("p (j s) -> p j s", j=PACK)
                for s0, s1 in zip(cuts, cuts[1:])
            ]

        def gather_on_scalar(step, g, s0, s1):
            for j in range(PACK):
                nc.scalar.activation(step[:, j, :], tokens(g, j, s0, s1), COPY)

        rounded = keep.tile([P, 31 * UNIT], BF16, name="rounded", align_bytes=MX_ALIGN)

        def units(first, count):
            return rounded[:, first * UNIT : (first + count) * UNIT]

        def gate_on_vector(first, raw, s0, s1):
            n = (s1 - s0) // RUN
            gates = gate_banks[s0 // BANK][:, s0 % BANK : s0 % BANK + s1 - s0]
            nc.vector.tensor_tensor(
                rounded[:, first * UNIT : first * UNIT + (s1 - s0) * PACK].rearrange("p (c i j) -> p c j i", i=RUN, j=PACK),
                raw.rearrange("p j (c i) -> p c j i", i=RUN),
                gates.rearrange("p (c i) -> p c i", i=RUN).unsqueeze(2).to_broadcast([P, n, PACK, RUN]),
                MULT,
            )

        def gate_on_gpsimd(first, i):
            s0, s1 = G_TURNS[i]
            c0 = first * UNIT + s0 % P * PACK
            nc.gpsimd.tensor_tensor(
                rounded[:, c0 : c0 + (s1 - s0) * PACK].rearrange("p (c i j) -> p c j i", i=RUN, j=PACK),
                raw_high[:, :, s0 - HALF : s1 - HALF].rearrange("p j (c i) -> p c j i", i=RUN),
                gate_rows[i][:].rearrange("p (c i) -> p c i", i=RUN).unsqueeze(2).to_broadcast([P, (s1 - s0) // RUN, PACK, RUN]),
                MULT,
            )

        def round_w(first, i):
            nc.gpsimd.tensor_scalar(
                out=units(first, len(W_PIECES[i])).rearrange("p (q n j) -> p q n j", n=N, j=PACK),
                in0=w_raw[i][:].rearrange("p q j n -> p q n j"),
                scalar1=1.0,
                scalar2=0.0,
                op0=MULT,
                op1=ADD,
            )

        def packed_tiles(name, runs, tag):
            codes = keep.tile([P, len(runs) * P], U32, name=name, tag=tag, align_bytes=MX_ALIGN)
            scales = keep.tile([P, len(runs) * P], U8, name=name + "_scales", align_bytes=MX_ALIGN)
            for i, run in enumerate(runs):
                packed[run] = (codes, scales, i * P)

        def quantize(run, first, count):
            codes, scales, c0 = packed[run]
            nc.vector.quantize_mx(
                out=codes[:, c0 : c0 + count * P].bitcast(FP8X4), scales=scales[:, c0 : c0 + count * P], in_=units(first, count)
            )

        def x_runs(g, s0, s1):
            return [("x", g, s) for s in range(s0, s1, P)]

        def multiply(acc, s0, s1, g, start, stop):
            w_words, w_scales, w0 = packed["w", PASSES * (s0 // C) + g]
            x_words, x_scales, x0 = packed["x", g, s0]
            nc.tensor.matmul_mx(
                out=acc,
                lhsT=w_words[:, w0 : w0 + N].bitcast(FP8X4),
                lhsT_scale=w_scales[:, w0 : w0 + N],
                rhs=x_words[:, x0 : x0 + s1 - s0].bitcast(FP8X4),
                rhs_scale=x_scales[:, x0 : x0 + s1 - s0],
                start=start,
                stop=stop,
            )

        (raw_low,) = raw_steps("raw_low", (0, HALF))
        (raw_high,) = raw_steps("raw_high", (HALF, S))
        gather_on_scalar(raw_low, 0, 0, HALF)
        for j in range(PACK):
            nc.vector.tensor_copy(raw_high[:, j, :], tokens(0, j, HALF, S))
        cuts = (2 * C, 4 * C, 6 * C, 7 * C, S)
        halves7 = (7 * C, S - P, S)
        (step1,) = raw_steps("step1", (0, cuts[0]))
        gather_on_scalar(step1, 1, 0, cuts[0])

        for i in range(6):
            round_w(2 * i, i)
        gate_on_gpsimd(25, 0)
        round_w(12, 6)
        gate_on_gpsimd(22, 1)
        later = raw_steps("later", cuts, tag="w_raw6")

        gate_on_vector(21, raw_high[:, :, 0 : SPLIT - HALF], HALF, SPLIT)
        for i in range(2):
            gate_on_vector(13 + 4 * i, raw_low[:, :, i * BANK : (i + 1) * BANK], i * BANK, (i + 1) * BANK)
        for step, s0, s1 in zip(later, cuts, cuts[1:]):
            gather_on_scalar(step, 1, s0, s1)
        gate_on_vector(27, step1, 0, cuts[0])

        early = [("w", q) for q in range(13)] + x_runs(0, 0, 7 * C) + x_runs(1, 0, cuts[0])
        packed_tiles("packed_early", early, "gate_rows1")
        for first, count in ((8, 8), (24, 4), (28, 3), (16, 8), (0, 8)):
            quantize(early[first], first, count)

        round_w(21, 7)
        gate_on_vector(27, later[0], cuts[0], cuts[1])
        packed_tiles("packed_second", [("w", q) for q in W_PIECES[7]], "packed_second")
        quantize(("w", 13), 21, 3)
        packed_tiles("packed_third", x_runs(1, cuts[0], cuts[1]), "w_raw7")
        quantize(("x", 1, cuts[0]), 27, 4)

        gate_on_gpsimd(21, 2)
        gate_on_vector(23, later[1], cuts[1], cuts[2])
        gate_on_vector(27, later[2], cuts[2], cuts[3])
        packed_tiles("packed_last", x_runs(0, 7 * C, S) + x_runs(1, HALF, S), "gate_rows2")
        quantize(("x", 0, 7 * C), 21, 4)
        quantize(("x", 1, 5 * C), 25, 4)
        for i in range(2):
            gate_on_vector(21 + i, later[3][:, :, i * P : (i + 1) * P], halves7[i], halves7[i + 1])
        for i in range(2):
            quantize(("x", 1, halves7[i]), 21 + i, 1)

        y = keep.tile([P, S], F32, name="y", tag="x_rows1_2", align_bytes=MX_ALIGN)
        pairs = [psum.tile([P, 2 * C], F32, name="sums%d" % i) for i in range(3)]
        sixth = psum.tile([P, C], F32, name="sums3")
        ends = [psum.tile([P, P], F32, name="end%d" % i, tag="gate_bank%d" % i) for i in range(2)]
        sums = [(e * C, (e + 1) * C, pairs[e // 2][:, e % 2 * C : (e % 2 + 1) * C], e % 2 == 0, e % 2 == 1) for e in range(6)]
        sums.append((6 * C, 7 * C, sixth[:], True, True))
        sums.extend((halves7[i], halves7[i + 1], ends[i][:], True, True) for i in range(2))
        for g, which in ((0, range(7)), (1, range(4)), (0, range(7, 9)), (1, range(4, 9))):
            for s0, s1, acc, opens, closes in (sums[i] for i in which):
                multiply(acc, s0, s1, g, g == 0 and opens, g == 1 and closes)
        for s0, s1, acc, opens, closes in sums:
            nc.scalar.activation(out=y[:, s0:s1], in_=acc, func=RELU, bias=bias[:, s0 // C : s0 // C + 1])

        halves = [slice(0, T // 2), slice(T // 2, T)]

        def results(r, part):
            return y[:].indirect(token_slot[r][:, part.start // STRIPE : part.stop // STRIPE])

        got = [keep.tile([P, T], F32, name="got%d" % r, align_bytes=MX_ALIGN) for r in range(6)]
        h0, h1 = halves
        for r in range(2):
            for part in halves:
                nc.scalar.activation(got[r][:, part], results(r, part), COPY)
        nc.vector.tensor_copy(got[2][:, h0], results(2, h0))
        nc.vector.tensor_tensor(got[3][:, h0], results(3, h0), got[0][:, h0], ADD)
        nc.vector.tensor_tensor(got[2][:, h1], results(2, h1), got[0][:, h1], ADD)
        nc.vector.tensor_tensor(got[4][:, h0], got[2][:, h0], got[3][:, h0], ADD)
        nc.vector.tensor_tensor(got[4][:, h1], results(3, h1), got[2][:, h1], ADD)
        for part in halves:
            nc.vector.tensor_tensor(got[5][:, part], got[4][:, part], got[1][:, part], ADD)
            nc.sync.dma_start(out=out[:, part], in_=got[5][:, part])
